import numpy as np
import ml_dtypes


def mxq(x, axis, fmt="e4m3"):
    dtype, down = {"e4m3": (ml_dtypes.float8_e4m3fn, 7), "e5m2": (ml_dtypes.float8_e5m2, 14)}[fmt]
    v = np.moveaxis(np.asarray(x, np.float32).astype(ml_dtypes.bfloat16).astype(np.float64), axis, -1)
    blocks = v.reshape(v.shape[:-1] + (-1, 32))
    amax = np.abs(blocks).max(-1, keepdims=True)
    byte = np.maximum(np.where(amax > 0, np.frexp(amax)[1] - 1 + 127, 0) - down, 1)
    scale = np.exp2(byte - 127.0)
    codes = (blocks / scale).astype(np.float32).astype(dtype).astype(np.float64)
    return np.moveaxis((codes * scale).reshape(v.shape), -1, axis)


WIDE = False


def mx_kscale(k):
    if not WIDE:
        return np.ones(k)
    levels = np.array([10, -10, 5, -5, 0])
    if k % 512:
        return np.exp2(np.random.permutation(np.resize(levels, k // 32))).repeat(32)
    a = np.empty((k // 512, 16))
    for p in range(k // 512):
        a[p, :8] = np.random.permutation(np.resize(levels, 8))
        for g in range(8):
            far = levels[np.abs(levels - a[p, g]) >= 10]
            a[p, g + 8] = far[np.random.randint(len(far))]
    return np.exp2(a.ravel()).repeat(32)


def f64(x):
    return np.asarray(x).astype(np.float64)


def striped(idx):
    return np.tile(idx.reshape(-1, 16).T, (8, 1)).astype(np.uint16)


def unstriped(offs):
    return offs[:16].T.reshape(-1).astype(np.int64)


E2M1 = np.array([0.0, 0.5, 1.0, 1.5, 2.0, 3.0, 4.0, 6.0, -0.0, -0.5, -1.0, -1.5, -2.0, -3.0, -4.0, -6.0])


def pack_weight(w, fmt):
    k, n = w.shape
    w = f64(np.asarray(w, np.float32).astype(ml_dtypes.bfloat16)).reshape(k // 32, 32, n)
    amax = np.abs(w).max(1)
    if fmt == "e4m3":
        byte = np.frexp(amax)[1] - 1 + 127 - 7
    else:
        mant, ex = np.frexp(amax / 6.0)
        byte = np.where(mant > 0.5, ex, ex - 1) + 127
    byte = np.clip(np.where(amax > 0, byte, 1), 1, 254)
    scaled = (w * np.exp2(127.0 - byte)[:, None, :]).reshape(k, n).astype(np.float32)
    by_word = np.ascontiguousarray(scaled.reshape(k // 512, 128, 4, n).transpose(0, 1, 3, 2))
    if fmt == "e4m3":
        words = by_word.astype(ml_dtypes.float8_e4m3fn).view(np.uint8)
    else:
        c = by_word.astype(ml_dtypes.float4_e2m1fn).view(np.uint8) & 0xF
        words = (c[..., 0::2] | (c[..., 1::2] << 4)).reshape(k // 512, 128, 2 * n)
    return np.ascontiguousarray(words), np.ascontiguousarray(byte.astype(np.uint8).reshape(k // 512, 16, n))


def unpack_weight(words, scales, fmt):
    g, _, n = scales.shape
    words = np.ascontiguousarray(words).reshape(g, 128, n, -1)
    if fmt == "e4m3":
        vals = words.view(ml_dtypes.float8_e4m3fn).astype(np.float64)
    else:
        nib = np.empty((g, 128, n, 4), np.uint8)
        nib[..., 0::2] = words & 0xF
        nib[..., 1::2] = words >> 4
        vals = E2M1[nib]
    vals = vals * np.repeat(np.exp2(scales.astype(np.float64) - 127.0), 8, axis=1)[..., None]
    return vals.transpose(0, 1, 3, 2).reshape(g * 512, n)


def gelu(v):
    return 0.5 * v * (1.0 + np.tanh(np.sqrt(2.0 / np.pi) * (v + 0.044715 * v**3)))


K, T, S, H, T2, T3, S2, P = 512, 4096, 1024, 1024, 2048, 2048, 512, 1024

def setup_inputs():
    n = np.random.standard_normal
    s = mx_kscale(K)[:, None]
    u = mx_kscale(H)[:, None]
    tab_words, tab_scales = pack_weight(n((K, T)) * s, "e4m3")
    tab2_words, tab2_scales = pack_weight(n((H, T3)) / np.sqrt(H) / u, "e4m3")
    w4_words, w4_scales = pack_weight(n((K, H)) / np.sqrt(K) / s, "e2m1")
    return {
        "tab_words": tab_words, "tab_scales": tab_scales,
        "tab2_words": tab2_words, "tab2_scales": tab2_scales,
        "offs": striped(np.random.permutation(T)[:S]),
        "offs2": striped(np.random.permutation(T3)[:S2]),
        "offs3": striped(np.random.permutation(T2)[:S]),
        "offs4": striped(np.random.permutation(T2)[:P]),
        "w1": (2.0 * n((K, H)) / np.sqrt(K) / s * u.T).astype(np.float32),
        "w4_words": w4_words, "w4_scales": w4_scales,
        "page0": (n((H, T2)) * u).astype(np.float32),
        "wgs": np.exp(0.3 * n((128, S))).astype(np.float32),
        "permit": np.random.uniform(0.25, 1.0, (S2, P)).astype(np.float32),
    }

def reference(tab_words, tab_scales, tab2_words, tab2_scales, offs, offs2, offs3, offs4,
              w1, w4_words, w4_scales, page0, wgs, permit):
    v = unpack_weight(tab_words, tab_scales, "e4m3")[:, unstriped(offs)]
    v2 = unpack_weight(tab2_words, tab2_scales, "e4m3")[:, unstriped(offs2)]
    w4 = unpack_weight(w4_words, w4_scales, "e2m1")
    a = mxq(f64(w1), 0, "e4m3").T @ v
    b = w4.T @ v
    h = a / (1.0 + np.abs(b))
    page = f64(page0).copy()
    page[:, unstriped(offs3)] = np.tile(f64(wgs), (H // 128, 1)) * h
    e = v2.T @ mxq(page, 0, "e4m3")
    x = e[:, unstriped(offs4)]
    return f64(permit) / (1.0 + np.exp(-x))

@@ -1,0 +1,369 @@
+from contextlib import ExitStack
+
+import concourse.mybir as mybir
+
+K, T, S, H, T2, T3, S2, PICK = 512, 4096, 1024, 1024, 2048, 2048, 512, 1024
+FLOPS = 2 * (2 * K * H * S + H * S2 * T2)
+
+F32 = mybir.dt.float32
+BF16 = mybir.dt.bfloat16
+I32 = mybir.dt.int32
+U32 = mybir.dt.uint32
+U16 = mybir.dt.uint16
+U8 = mybir.dt.uint8
+FP8X4 = mybir.dt.float8_e4m3fn_x4
+FP4X4 = mybir.dt.float4_e2m1fn_x4
+ACT = mybir.ActivationFunctionType
+MULT = mybir.AluOpType.mult
+
+P = 128
+BANK = 512
+PASSES = H // 512
+PLANES = 4 * PASSES
+CHUNKS = T2 // BANK
+NTILES = S2 // P
+LATER = {0: ("w1_late", "page3"), 1: ("tab2s", "page4"), 2: ("page5", "page6"), 3: ("page7", "w1s_3")}
+
+
+def tile_list_farm_job_board_kernel(
+    tc, tab_words, tab_scales, tab2_words, tab2_scales, offs, offs2, offs3, offs4,
+    w1, w4_words, w4_scales, page0, wgs, permit, out,
+):
+    nc = tc.nc
+    with ExitStack() as ctx:
+        keep = ctx.enter_context(tc.tile_pool(name="keep", bufs=1))
+        work = ctx.enter_context(tc.tile_pool(name="work", bufs=1))
+        psum = ctx.enter_context(tc.psum_pool(name="psum", bufs=1))
+
+        def bank(i, name):
+            return psum.tile([P, BANK], F32, name=name, tag="bank%d" % i)
+
+        def load_scale_rows(queue, plane, rows, width):
+            for q in range(4):
+                queue.dma_start(
+                    out=plane[32 * q : 32 * q + width, :].bitcast(I32),
+                    in_=(rows[0, 4 * q : 4 * q + 4, :] if width == 4 else rows[:, 4 * q : 4 * q + 4, :]).bitcast(I32),
+                )
+
+        list1 = keep.tile([P, S // 16], U16, name="list1")
+        list2 = keep.tile([P, S2 // 16], U16, name="list2")
+        list3 = keep.tile([P, S // 16], U16, name="list3")
+        list4 = keep.tile([P, PICK // 16], U16, name="list4")
+
+        def slot(shape, dtype, name, tag):
+            return work.tile(shape, dtype, name=name, tag=tag, align_bytes=64)
+
+        nc.sync.dma_start(list1[:], offs)
+        nc.sync.dma_start(list3[:], offs3)
+        nc.sync.dma_start(list2[:], offs2)
+        nc.sync.dma_start(list4[:], offs4)
+        w4_raw = slot([P, 2 * H], U8, "w4_raw", "page0")
+        w4s_raw = slot([P, H], U8, "w4s_raw", "v_1")
+        tabs = slot([P, T], U8, "tabs", "wg_first")
+        one = slot([P, 1], F32, "one", "big")
+        warm = keep.tile([P, 2], F32, name="warm")
+        nc.vector.memset(one[:], 1.0)
+        nc.vector.memset(tabs[:].bitcast(I32), 0)
+        nc.vector.memset(w4s_raw[:].bitcast(I32), 0)
+        nc.scalar.activation(out=warm[:, 0:1], in_=one[:], func=ACT.Abs_reciprocal_sqrt)
+
+        nc.sync.dma_start(out=w4_raw[:].bitcast(I32), in_=w4_words[0].bitcast(I32))
+
+        w1_raw = []
+
+        def load_w1(b):
+            raw = slot([P, 4, 512], F32, "w1_raw", "page1" if b == 0 else "w1_late")
+            nc.sync.dma_start(
+                out=raw[:], in_=w1[:, 512 * b : 512 * (b + 1)].rearrange("(p j) c -> p j c", j=4)
+            )
+            w1_raw.append(raw)
+
+        pages = []
+
+        def load_page(k):
+            b, t = divmod(k, 4)
+            page = slot([P, T2], F32, "page", "page%d" % k)
+            rows = page0[512 * b : 512 * (b + 1), :].rearrange("(p t) c -> t p c", t=4)
+            nc.sync.dma_start(out=page[:], in_=rows[t])
+            pages.append(page)
+
+        load_w1(0)
+        load_scale_rows(nc.sync, tabs, tab_scales, 4)
+        tab = slot([P, T], U32, "tab", "big")
+        nc.sync.dma_start(
+            out=tab[:].bitcast(I32),
+            in_=tab_words[0].rearrange("p n i -> p (n i)").bitcast(I32),
+        )
+        load_scale_rows(nc.scalar, w4s_raw, w4_scales, 4)
+        wg_rows = wgs.rearrange("(q t) j -> q (t j)", t=4)
+        wg = []
+
+        def load_weights(t0, t1, tag):
+            rows = slot([P, (t1 - t0) * S], F32, tag, tag)
+            for q in range(4):
+                nc.sync.dma_start(out=rows[32 * q : 32 * (q + 1), :], in_=wg_rows[:, t0 * S : t1 * S])
+            wg.append(rows)
+
+        def weight_rows(t, cols):
+            if t == 0:
+                return wg[0][:, cols]
+            return wg[1][:, (t - 1) * S + cols.start : (t - 1) * S + cols.stop]
+
+        w4 = []
+        w4s = []
+        for b in range(PASSES):
+            words = keep.tile([P, 1024], U8, name="w4_%d" % b, align_bytes=64)
+            nc.vector.tensor_copy(
+                out=words[:].rearrange("p (t m e) -> p m t e", t=4, e=2),
+                in_=w4_raw[:, 1024 * b : 1024 * (b + 1)].rearrange("p (m t e) -> p m t e", t=4, e=2),
+            )
+            w4.append(words)
+        for b, t0, t1 in ((0, 0, 1), (0, 1, 4), (1, 0, 4)):
+            scales = keep.tile([P, P * (t1 - t0)], U8, name="w4s_%d_%d" % (b, t0), align_bytes=64)
+            nc.vector.tensor_copy(
+                out=scales[:].rearrange("p (t m) -> p m t", t=t1 - t0),
+                in_=w4s_raw[:, 512 * b : 512 * (b + 1)].rearrange("p (m t) -> p m t", t=4)[:, :, t0:t1],
+            )
+            for t in range(t0, t1):
+                w4s.append(scales[:, P * (t - t0) : P * (t - t0 + 1)])
+
+        v = []
+        vs = []
+        for half in range(2):
+            picks = list1[:, 32 * half : 32 * (half + 1)]
+            words = slot([P, BANK], U32, "v", "v_%d" % half)
+            scales = keep.tile([P, BANK], U8, name="vs_%d" % half, align_bytes=64)
+            nc.vector.tensor_copy(scales[:], tabs[:].indirect(picks))
+            nc.vector.tensor_copy(words[:], tab[:].indirect(picks))
+            v.append(words)
+            vs.append(scales)
+
+        w1q = {}
+
+        def quantise_w1(b, t0, t1):
+            n = t1 - t0
+            rounded = slot([P, n * 512], BF16, "w1_bf", "wg_rest" if b == 0 else "allowed")
+            nc.scalar.copy(
+                out=rounded[:].rearrange("p (t m j) -> p m j t", t=n, j=4),
+                in_=w1_raw[b][:].rearrange("p j (m t) -> p m j t", t=4)[:, :, :, t0:t1],
+            )
+            for t in range(t0, t1):
+                tags = LATER.get(4 * b + t, ("w1c%d" % t, "w1s%d" % t))
+                codes = slot([P, P], U32, "w1c", tags[0])
+                scales = slot([P, P], U8, "w1s", tags[1])
+                nc.vector.quantize_mx(
+                    out=codes[:].bitcast(FP8X4),
+                    scales=scales[:],
+                    in_=rounded[:, 512 * (t - t0) : 512 * (t - t0 + 1)],
+                )
+                w1q[4 * b + t] = (codes, scales)
+
+        damped = {}
+
+        def first_stage(k):
+            b, t = divmod(k, 4)
+            base = 4 * (k % 2)
+            acc_b = [bank(base + half, "acc_b") for half in range(2)]
+            acc_a = [bank(base + 2 + half, "acc_a") for half in range(2)]
+            for half in range(2):
+                nc.tensor.matmul_mx(
+                    out=acc_b[half][:],
+                    lhsT=w4[b][:, 256 * t : 256 * (t + 1)].bitcast(FP4X4),
+                    lhsT_scale=w4s[k],
+                    rhs=v[half][:].bitcast(FP8X4), rhs_scale=vs[half][:],
+                    start=True, stop=True,
+                )
+            for half in range(2):
+                nc.tensor.matmul_mx(
+                    out=acc_a[half][:],
+                    lhsT=w1q[k][0][:].bitcast(FP8X4), lhsT_scale=w1q[k][1][:],
+                    rhs=v[half][:].bitcast(FP8X4), rhs_scale=vs[half][:],
+                    start=True, stop=True,
+                )
+            damp = [work.tile([P, BANK], F32, name="damp", tag="damp", bufs=4) for half in range(2)]
+            for halves in ([[0], [1]] if k == 0 else [[0, 1]]):
+                root = {}
+                for half in halves:
+                    place = 0 if k == 0 else half
+                    root[half] = work.tile([P, BANK], F32, name="root", tag="root%d" % place)
+                    nc.scalar.activation(out=root[half][:], in_=acc_b[half][:], func=ACT.Abs)
+                for half in halves:
+                    nc.scalar.activation(
+                        out=root[half][:], in_=root[half][:], func=ACT.Abs_reciprocal_sqrt, bias=1.0
+                    )
+                for half in halves:
+                    nc.scalar.activation(out=damp[half][:], in_=root[half][:], func=ACT.Square)
+            damped[k] = (acc_a, damp)
+
+        def edit_page(k):
+            acc_a, damp = damped[k]
+            if k == 0:
+                for half in range(2):
+                    cols = slice(BANK * half, BANK * (half + 1))
+                    h = slot([P, BANK], F32, "h_half", "page2")
+                    nc.vector.tensor_tensor(out=h[:], in0=acc_a[half][:], in1=damp[half][:], op=MULT)
+                    nc.vector.tensor_tensor(
+                        pages[k][:].indirect(list3[:, 32 * half : 32 * (half + 1)]),
+                        h[:], weight_rows(k % 4, cols), MULT,
+                    )
+                return
+            h = work.tile([P, S], F32, name="h", tag="h", bufs=2)
+            for half in range(2):
+                cols = slice(BANK * half, BANK * (half + 1))
+                nc.vector.tensor_tensor(out=h[:, cols], in0=acc_a[half][:], in1=damp[half][:], op=MULT)
+            nc.vector.tensor_tensor(
+                pages[k][:].indirect(list3[:]), h[:], weight_rows(k % 4, slice(0, S)), MULT
+            )
+
+        pairs = {}
+        board = {}
+
+        def copy_on(engine, dst, src):
+            if engine == "vector":
+                nc.vector.tensor_copy(out=dst, in_=src)
+            else:
+                nc.scalar.copy(out=dst, in_=src)
+
+        def round_plane(k, c, engine):
+            b, t = divmod(k, 4)
+            if t == 0:
+                pairs[(b, c)] = work.tile([P, 2 * BANK * 2], BF16, name="pairs", tag="pairs", bufs=CHUNKS, align_bytes=64)
+            dst = pairs[(b, c)][:].rearrange("p (u c e) -> p u c e", u=2, e=2)
+            src = pages[k][:, BANK * c : BANK * (c + 1)]
+            if k == PLANES - 2 and c % 2 == 0:
+                copy_on(engine, dst[:, t // 2, :, :], src.unsqueeze(2).to_broadcast([P, BANK, 2]))
+            else:
+                copy_on(engine, dst[:, t // 2, :, t % 2], src)
+
+        def weave(b, c, engine):
+            woven = work.tile([P, 4 * BANK], BF16, name="woven", tag="woven", bufs=CHUNKS, align_bytes=64)
+            copy_on(
+                engine,
+                woven[:].bitcast(F32).rearrange("p (c u) -> p c u", u=2),
+                pairs[(b, c)][:].bitcast(F32).rearrange("p (u c) -> p c u", u=2),
+            )
+            board[(b, c)] = woven
+
+        boardq = {}
+
+        def quantise_board(b, c):
+            codes = keep.tile([P, BANK], U32, name="bc_%d_%d" % (b, c), align_bytes=64)
+            scales = keep.tile([P, BANK], U8, name="bs_%d_%d" % (b, c), align_bytes=64)
+            nc.vector.quantize_mx(out=codes[:].bitcast(FP8X4), scales=scales[:], in_=board[(b, c)][:])
+            boardq[(b, c)] = (codes, scales)
+
+        v2 = []
+        v2s = keep.tile([P, S2], U8, name="v2s", align_bytes=64)
+
+        def gather_workers():
+            tab2 = slot([P, PASSES * T3], U32, "tab2", "big")
+            tab2s = slot([P, T3], U8, "tab2s", "tab2s")
+            nc.vector.memset(tab2s[:].bitcast(I32), 0)
+            load_scale_rows(nc.sync, tab2s, tab2_scales, 8)
+            for b in range(PASSES):
+                table = tab2[:, T3 * b : T3 * (b + 1)]
+                nc.sync.dma_start(
+                    out=table.bitcast(I32),
+                    in_=tab2_words[b].rearrange("p n i -> p (n i)").bitcast(I32),
+                )
+                words = keep.tile([P, S2], U32, name="v2_%d" % b, align_bytes=64)
+                nc.vector.tensor_copy(words[:], table.indirect(list2[:]))
+                v2.append(words)
+            nc.vector.tensor_copy(v2s[:], tab2s[:].indirect(list2[:]))
+
+        scores = {}
+
+        def score_pass(n, c, b):
+            if b == 0:
+                scores[(n, c)] = bank(4 * (n % 2) + c, "score")
+            cols = slice(P * n, P * (n + 1))
+            nc.tensor.matmul_mx(
+                out=scores[(n, c)][:],
+                lhsT=v2[b][:, cols].bitcast(FP8X4), lhsT_scale=v2s[4 * b : P, cols],
+                rhs=boardq[(b, c)][0][:].bitcast(FP8X4), rhs_scale=boardq[(b, c)][1][:],
+                start=(b == 0), stop=(b == PASSES - 1),
+            )
+
+        quantise_w1(0, 0, 4)
+        load_page(0)
+        load_weights(0, 1, "wg_first")
+        load_page(1)
+        load_weights(1, 4, "wg_rest")
+        first_stage(0)
+        load_w1(1)
+        first_stage(1)
+        allowed = None
+        for k in range(PLANES):
+            edit_page(k)
+            if k == 0:
+                for later in range(2, 5):
+                    load_page(later)
+            if k == 1:
+                quantise_w1(1, 0, 4)
+                load_page(5)
+                load_page(6)
+                gather_workers()
+                allowed = slot([P, NTILES, PICK], F32, "allowed", "allowed")
+                nc.sync.dma_start(out=allowed[:], in_=permit.rearrange("(n p) m -> p n m", p=P))
+            if k == 2:
+                load_page(7)
+            if k + 2 < PLANES:
+                first_stage(k + 2)
+            if k + 2 == PLANES - 1:
+                nc.scalar.activation(out=warm[:, 1:2], in_=damped[k + 2][1][1][:, 0:1], func=ACT.Sigmoid)
+            if k == 4:
+                for c in range(CHUNKS):
+                    weave(0, c, "scalar")
+                    quantise_board(0, c)
+            if k < PLANES - 1:
+                for c in range(CHUNKS):
+                    round_plane(k, c, "scalar")
+        for n in range(2):
+            for c in range(CHUNKS):
+                score_pass(n, c, 0)
+
+        order = [0, 2, 1, 3]
+        for c in order:
+            engine = "vector" if c % 2 == 0 else "scalar"
+            round_plane(PLANES - 1, c, engine)
+        for c in order:
+            engine = "vector" if c % 2 == 0 else "scalar"
+            weave(1, c, engine)
+        for c in order:
+            quantise_board(1, c)
+            for n in range(2):
+                score_pass(n, c, 1)
+
+        def finish(n):
+            e = slot([P, T2], F32, "e", "page%d" % n)
+            for c in order:
+                engine = "vector" if (n == 0 and c == order[-1]) else "scalar"
+                copy_on(engine, e[:, BANK * c : BANK * (c + 1)], scores[(n, c)][:])
+            if n + 2 < NTILES:
+                for c in order:
+                    for b in range(PASSES):
+                        score_pass(n + 2, c, b)
+            x = work.tile([P, PICK], F32, name="x", tag="pairs", bufs=CHUNKS, align_bytes=64)
+            pieces = 2 if n == NTILES - 1 else 1
+            width = PICK // pieces
+            steps = []
+            for piece in range(pieces):
+                cols = slice(width * piece, width * (piece + 1))
+                picks = list4[:, cols.start // 16 : cols.stop // 16]
+                nc.vector.tensor_copy(x[:, cols], e[:].indirect(picks))
+                steps.append(cols)
+            return x, steps
+
+        def weigh(n, x, steps):
+            for cols in steps:
+                nc.scalar.activation(out=x[:, cols], in_=x[:, cols], func=ACT.Sigmoid)
+                nc.vector.tensor_tensor(out=x[:, cols], in0=x[:, cols], in1=allowed[:, n, cols], op=MULT)
+                nc.sync.dma_start(out=out[P * n : P * (n + 1), cols], in_=x[:, cols])
+
+        picked = []
+        for n in range(NTILES):
+            picked.append(finish(n))
+            if n == NTILES - 2:
+                weigh(0, picked[0][0], picked[0][1])
+        for n in range(1, NTILES):
+            weigh(n, picked[n][0], picked[n][1])

@@ -22,7 +22,9 @@ PASSES = H // 512
 PLANES = 4 * PASSES
 CHUNKS = T2 // BANK
 NTILES = S2 // P
-LATER = {0: ("w1_late", "page3"), 1: ("tab2s", "page4"), 2: ("page5", "page6"), 3: ("page7", "w1s_3")}
+FIRST_PARTS = [[slice(0, 256), slice(256, 512)], [slice(0, 512)]]
+LAST_PARTS = [slice(0, 768), slice(768, 1024)]
+LATER = {0: ("tab2s", "w1_late"), 1: ("page3", "page4"), 2: ("page5", "page6"), 3: ("page7", "w1s_3")}
 
 
 def tile_list_farm_job_board_kernel(
@@ -53,26 +55,35 @@ def tile_list_farm_job_board_kernel(
         def slot(shape, dtype, name, tag):
             return work.tile(shape, dtype, name=name, tag=tag, align_bytes=64)
 
+        w4_raw = slot([P, 2 * H], U8, "w4_raw", "page1")
+        w4s_raw = keep.tile([P, H], U8, name="w4s_raw", align_bytes=64)
+        tabs = slot([P, T], U8, "tabs", "page2")
+        seed = slot([P, 1], F32, "seed", "wg_rest")
+        one = slot([P, 1], F32, "one", "wg_first")
+        warm = slot([P, 1], F32, "warm", "page0")
+        warm_last = keep.tile([P, 1], F32, name="warm_last")
+        nc.vector.memset(tabs[:].bitcast(I32), 0)
+        nc.vector.memset(seed[:], 1.0)
+        nc.vector.tensor_copy(out=one[:], in_=seed[:])
+        nc.vector.memset(w4s_raw[:].bitcast(I32), 0)
+        nc.scalar.activation(out=warm[:], in_=one[:], func=ACT.Abs_reciprocal_sqrt)
+
+        nc.sync.dma_start(out=w4_raw[:].bitcast(I32), in_=w4_words[0].bitcast(I32))
         nc.sync.dma_start(list1[:], offs)
         nc.sync.dma_start(list3[:], offs3)
         nc.sync.dma_start(list2[:], offs2)
         nc.sync.dma_start(list4[:], offs4)
-        w4_raw = slot([P, 2 * H], U8, "w4_raw", "page0")
-        w4s_raw = slot([P, H], U8, "w4s_raw", "v_1")
-        tabs = slot([P, T], U8, "tabs", "wg_first")
-        one = slot([P, 1], F32, "one", "big")
-        warm = keep.tile([P, 2], F32, name="warm")
-        nc.vector.memset(one[:], 1.0)
-        nc.vector.memset(tabs[:].bitcast(I32), 0)
-        nc.vector.memset(w4s_raw[:].bitcast(I32), 0)
-        nc.scalar.activation(out=warm[:, 0:1], in_=one[:], func=ACT.Abs_reciprocal_sqrt)
-
-        nc.sync.dma_start(out=w4_raw[:].bitcast(I32), in_=w4_words[0].bitcast(I32))
+        tab = slot([P, T], U32, "tab", "big")
+        nc.sync.dma_start(
+            out=tab[:].bitcast(I32),
+            in_=tab_words[0].rearrange("p n i -> p (n i)").bitcast(I32),
+        )
+        load_scale_rows(nc.sync, tabs, tab_scales, 4)
 
         w1_raw = []
 
         def load_w1(b):
-            raw = slot([P, 4, 512], F32, "w1_raw", "page1" if b == 0 else "w1_late")
+            raw = slot([P, 4, 512], F32, "w1_raw", "wg_rest" if b == 0 else "w1_late")
             nc.sync.dma_start(
                 out=raw[:], in_=w1[:, 512 * b : 512 * (b + 1)].rearrange("(p j) c -> p j c", j=4)
             )
@@ -88,13 +99,8 @@ def tile_list_farm_job_board_kernel(
             pages.append(page)
 
         load_w1(0)
-        load_scale_rows(nc.sync, tabs, tab_scales, 4)
-        tab = slot([P, T], U32, "tab", "big")
-        nc.sync.dma_start(
-            out=tab[:].bitcast(I32),
-            in_=tab_words[0].rearrange("p n i -> p (n i)").bitcast(I32),
-        )
-        load_scale_rows(nc.scalar, w4s_raw, w4_scales, 4)
+        load_scale_rows(nc.sync, w4s_raw, w4_scales, 4)
+        load_page(0)
         wg_rows = wgs.rearrange("(q t) j -> q (t j)", t=4)
         wg = []
 
@@ -109,6 +115,8 @@ def tile_list_farm_job_board_kernel(
                 return wg[0][:, cols]
             return wg[1][:, (t - 1) * S + cols.start : (t - 1) * S + cols.stop]
 
+        load_weights(0, 1, "wg_first")
+
         w4 = []
         w4s = []
         for b in range(PASSES):
@@ -118,7 +126,9 @@ def tile_list_farm_job_board_kernel(
                 in_=w4_raw[:, 1024 * b : 1024 * (b + 1)].rearrange("p (m t e) -> p m t e", t=4, e=2),
             )
             w4.append(words)
-        for b, t0, t1 in ((0, 0, 1), (0, 1, 4), (1, 0, 4)):
+        load_page(1)
+
+        def order_w4_scales(b, t0, t1):
             scales = keep.tile([P, P * (t1 - t0)], U8, name="w4s_%d_%d" % (b, t0), align_bytes=64)
             nc.vector.tensor_copy(
                 out=scales[:].rearrange("p (t m) -> p m t", t=t1 - t0),
@@ -129,34 +139,42 @@ def tile_list_farm_job_board_kernel(
 
         v = []
         vs = []
-        for half in range(2):
+
+        def gather_vacancies(half):
             picks = list1[:, 32 * half : 32 * (half + 1)]
-            words = slot([P, BANK], U32, "v", "v_%d" % half)
+            words = keep.tile([P, BANK], U32, name="v_%d" % half, align_bytes=64)
             scales = keep.tile([P, BANK], U8, name="vs_%d" % half, align_bytes=64)
-            nc.vector.tensor_copy(scales[:], tabs[:].indirect(picks))
             nc.vector.tensor_copy(words[:], tab[:].indirect(picks))
+            nc.vector.tensor_copy(scales[:], tabs[:].indirect(picks))
             v.append(words)
             vs.append(scales)
 
+        gather_vacancies(0)
+        order_w4_scales(0, 0, 1)
+
         w1q = {}
 
-        def quantise_w1(b, t0, t1):
-            n = t1 - t0
-            rounded = slot([P, n * 512], BF16, "w1_bf", "wg_rest" if b == 0 else "allowed")
+        def quantise_w1(b):
+            rounded = slot([P, 2048], BF16, "w1_bf", "w1_bf")
             nc.scalar.copy(
-                out=rounded[:].rearrange("p (t m j) -> p m j t", t=n, j=4),
-                in_=w1_raw[b][:].rearrange("p j (m t) -> p m j t", t=4)[:, :, :, t0:t1],
+                out=rounded[:].rearrange("p (t m j) -> p m j t", t=4, j=4),
+                in_=w1_raw[b][:].rearrange("p j (m t) -> p m j t", t=4),
             )
-            for t in range(t0, t1):
-                tags = LATER.get(4 * b + t, ("w1c%d" % t, "w1s%d" % t))
-                codes = slot([P, P], U32, "w1c", tags[0])
-                scales = slot([P, P], U8, "w1s", tags[1])
-                nc.vector.quantize_mx(
-                    out=codes[:].bitcast(FP8X4),
-                    scales=scales[:],
-                    in_=rounded[:, 512 * (t - t0) : 512 * (t - t0 + 1)],
-                )
-                w1q[4 * b + t] = (codes, scales)
+            if b == 0:
+                for t in range(4):
+                    codes = slot([P, P], U32, "w1c", LATER[t][0])
+                    scales = slot([P, P], U8, "w1s", LATER[t][1])
+                    nc.vector.quantize_mx(
+                        out=codes[:].bitcast(FP8X4), scales=scales[:],
+                        in_=rounded[:, 512 * t : 512 * (t + 1)],
+                    )
+                    w1q[t] = (codes[:], scales[:])
+                return
+            codes = slot([P, 512], U32, "w1c", "w1c_late")
+            scales = keep.tile([P, 512], U8, name="w1s_late", align_bytes=64)
+            nc.vector.quantize_mx(out=codes[:].bitcast(FP8X4), scales=scales[:], in_=rounded[:])
+            for t in range(4):
+                w1q[4 + t] = (codes[:, P * t : P * (t + 1)], scales[:, P * t : P * (t + 1)])
 
         damped = {}
 
@@ -173,46 +191,69 @@ def tile_list_farm_job_board_kernel(
                     rhs=v[half][:].bitcast(FP8X4), rhs_scale=vs[half][:],
                     start=True, stop=True,
                 )
-            for half in range(2):
                 nc.tensor.matmul_mx(
                     out=acc_a[half][:],
-                    lhsT=w1q[k][0][:].bitcast(FP8X4), lhsT_scale=w1q[k][1][:],
+                    lhsT=w1q[k][0].bitcast(FP8X4), lhsT_scale=w1q[k][1],
                     rhs=v[half][:].bitcast(FP8X4), rhs_scale=vs[half][:],
                     start=True, stop=True,
                 )
-            damp = [work.tile([P, BANK], F32, name="damp", tag="damp", bufs=4) for half in range(2)]
-            for halves in ([[0], [1]] if k == 0 else [[0, 1]]):
-                root = {}
-                for half in halves:
-                    place = 0 if k == 0 else half
-                    root[half] = work.tile([P, BANK], F32, name="root", tag="root%d" % place)
-                    nc.scalar.activation(out=root[half][:], in_=acc_b[half][:], func=ACT.Abs)
-                for half in halves:
+            damp = []
+            for half in range(2):
+                tag = {(3, 1): "w1c_late", (7, 1): "board_codes"}.get((k, half), "damp%d" % (2 * (k % 2) + half))
+                damp.append(slot([P, BANK], F32, "damp", tag))
+            if k == 0:
+                for half in range(2):
+                    size = slot([P, BANK], F32, "size", "root0")
+                    root = slot([P, BANK], F32, "root", "root1")
+                    parts = FIRST_PARTS[half]
+                    for cols in parts:
+                        nc.scalar.activation(out=size[:, cols], in_=acc_b[half][:, cols], func=ACT.Abs)
+                    for cols in parts:
+                        nc.scalar.activation(
+                            out=root[:, cols], in_=size[:, cols], func=ACT.Abs_reciprocal_sqrt, bias=1.0
+                        )
+                    for cols in parts:
+                        nc.scalar.activation(out=damp[half][:, cols], in_=root[:, cols], func=ACT.Square)
+            else:
+                roots = [slot([P, BANK], F32, "root", "root%d" % half) for half in range(2)]
+                for half in range(2):
+                    nc.scalar.activation(out=roots[half][:], in_=acc_b[half][:], func=ACT.Abs)
+                for half in range(2):
                     nc.scalar.activation(
-                        out=root[half][:], in_=root[half][:], func=ACT.Abs_reciprocal_sqrt, bias=1.0
+                        out=roots[half][:], in_=roots[half][:], func=ACT.Abs_reciprocal_sqrt, bias=1.0
                     )
-                for half in halves:
-                    nc.scalar.activation(out=damp[half][:], in_=root[half][:], func=ACT.Square)
+                for half in range(2):
+                    nc.scalar.activation(out=damp[half][:], in_=roots[half][:], func=ACT.Square)
             damped[k] = (acc_a, damp)
 
         def edit_page(k):
             acc_a, damp = damped[k]
             if k == 0:
                 for half in range(2):
-                    cols = slice(BANK * half, BANK * (half + 1))
-                    h = slot([P, BANK], F32, "h_half", "page2")
-                    nc.vector.tensor_tensor(out=h[:], in0=acc_a[half][:], in1=damp[half][:], op=MULT)
-                    nc.vector.tensor_tensor(
-                        pages[k][:].indirect(list3[:, 32 * half : 32 * (half + 1)]),
-                        h[:], weight_rows(k % 4, cols), MULT,
-                    )
-                return
-            h = work.tile([P, S], F32, name="h", tag="h", bufs=2)
+                    h = slot([P, BANK], F32, "h_half", "h1")
+                    for cols in FIRST_PARTS[half]:
+                        entries = slice(BANK * half + cols.start, BANK * half + cols.stop)
+                        nc.vector.tensor_tensor(
+                            out=h[:, cols], in0=acc_a[half][:, cols], in1=damp[half][:, cols], op=MULT
+                        )
+                        nc.vector.tensor_tensor(
+                            pages[k][:].indirect(list3[:, entries.start // 16 : entries.stop // 16]),
+                            h[:, cols], weight_rows(0, entries), MULT,
+                        )
+
+        features = {}
+
+        def damp_next(k):
+            acc_a, damp = damped[k]
+            h = slot([P, S], F32, "h", "h%d" % (k % 2))
             for half in range(2):
                 cols = slice(BANK * half, BANK * (half + 1))
                 nc.vector.tensor_tensor(out=h[:, cols], in0=acc_a[half][:], in1=damp[half][:], op=MULT)
+            features[k] = h
+
+        def scatter(k):
             nc.vector.tensor_tensor(
-                pages[k][:].indirect(list3[:]), h[:], weight_rows(k % 4, slice(0, S)), MULT
+                pages[k][:].indirect(list3[:]), features[k][:], weight_rows(k % 4, slice(0, S)), MULT
             )
 
         pairs = {}
@@ -245,11 +286,14 @@ def tile_list_farm_job_board_kernel(
             board[(b, c)] = woven
 
         boardq = {}
+        board_codes = {}
 
         def quantise_board(b, c):
-            codes = keep.tile([P, BANK], U32, name="bc_%d_%d" % (b, c), align_bytes=64)
+            if c == 0:
+                board_codes[b] = slot([P, T2], U32, "board_codes", "board_codes" if b == 0 else "board_codes_last")
+            codes = board_codes[b][:, BANK * c : BANK * (c + 1)]
             scales = keep.tile([P, BANK], U8, name="bs_%d_%d" % (b, c), align_bytes=64)
-            nc.vector.quantize_mx(out=codes[:].bitcast(FP8X4), scales=scales[:], in_=board[(b, c)][:])
+            nc.vector.quantize_mx(out=codes.bitcast(FP8X4), scales=scales[:], in_=board[(b, c)][:])
             boardq[(b, c)] = (codes, scales)
 
         v2 = []
@@ -280,40 +324,47 @@ def tile_list_farm_job_board_kernel(
             nc.tensor.matmul_mx(
                 out=scores[(n, c)][:],
                 lhsT=v2[b][:, cols].bitcast(FP8X4), lhsT_scale=v2s[4 * b : P, cols],
-                rhs=boardq[(b, c)][0][:].bitcast(FP8X4), rhs_scale=boardq[(b, c)][1][:],
+                rhs=boardq[(b, c)][0].bitcast(FP8X4), rhs_scale=boardq[(b, c)][1][:],
                 start=(b == 0), stop=(b == PASSES - 1),
             )
 
-        quantise_w1(0, 0, 4)
-        load_page(0)
-        load_weights(0, 1, "wg_first")
-        load_page(1)
+        gather_vacancies(1)
+        quantise_w1(0)
         load_weights(1, 4, "wg_rest")
+        order_w4_scales(0, 1, 4)
+        order_w4_scales(1, 0, 4)
+        load_page(2)
         first_stage(0)
         load_w1(1)
+        edit_page(0)
         first_stage(1)
-        allowed = None
-        for k in range(PLANES):
-            edit_page(k)
-            if k == 0:
-                for later in range(2, 5):
-                    load_page(later)
-            if k == 1:
-                quantise_w1(1, 0, 4)
-                load_page(5)
-                load_page(6)
-                gather_workers()
-                allowed = slot([P, NTILES, PICK], F32, "allowed", "allowed")
-                nc.sync.dma_start(out=allowed[:], in_=permit.rearrange("(n p) m -> p n m", p=P))
+        load_page(3)
+        load_page(4)
+        first_stage(2)
+        load_page(5)
+        load_page(6)
+        for c in range(CHUNKS):
+            round_plane(0, c, "scalar")
+        damp_next(1)
+        gather_workers()
+        allowed = slot([P, NTILES, PICK], F32, "allowed", "big")
+        nc.sync.dma_start(out=allowed[:], in_=permit.rearrange("(n p) m -> p n m", p=P))
+        for k in range(1, PLANES):
+            if k + 1 < PLANES:
+                damp_next(k + 1)
+            scatter(k)
             if k == 2:
                 load_page(7)
+                quantise_w1(1)
             if k + 2 < PLANES:
                 first_stage(k + 2)
             if k + 2 == PLANES - 1:
-                nc.scalar.activation(out=warm[:, 1:2], in_=damped[k + 2][1][1][:, 0:1], func=ACT.Sigmoid)
+                nc.scalar.activation(out=warm_last[:], in_=damped[k + 2][1][1][:, 0:1], func=ACT.Sigmoid)
             if k == 4:
                 for c in range(CHUNKS):
                     weave(0, c, "scalar")
+            if k == 6:
+                for c in range(CHUNKS):
                     quantise_board(0, c)
             if k < PLANES - 1:
                 for c in range(CHUNKS):
@@ -344,11 +395,8 @@ def tile_list_farm_job_board_kernel(
                     for b in range(PASSES):
                         score_pass(n + 2, c, b)
             x = work.tile([P, PICK], F32, name="x", tag="pairs", bufs=CHUNKS, align_bytes=64)
-            pieces = 2 if n == NTILES - 1 else 1
-            width = PICK // pieces
             steps = []
-            for piece in range(pieces):
-                cols = slice(width * piece, width * (piece + 1))
+            for cols in (LAST_PARTS if n == NTILES - 1 else [slice(0, PICK)]):
                 picks = list4[:, cols.start // 16 : cols.stop // 16]
                 nc.vector.tensor_copy(x[:, cols], e[:].indirect(picks))
                 steps.append(cols)

@@ -18,13 +18,36 @@ MULT = mybir.AluOpType.mult
 
 P = 128
 BANK = 512
-PASSES = H // 512
-PLANES = 4 * PASSES
+PACK = 4
+PASS = P * PACK
+PASSES = H // PASS
+PLANES = PACK * PASSES
+HALVES = S // BANK
 CHUNKS = T2 // BANK
-NTILES = S2 // P
+ROW_TILES = S2 // P
+LAST = PLANES - 1
+
 FIRST_PARTS = [[slice(0, 256), slice(256, 512)], [slice(0, 512)]]
 LAST_PARTS = [slice(0, 768), slice(768, 1024)]
-LATER = {0: ("tab2s", "w1_late"), 1: ("page3", "page4"), 2: ("page5", "page6"), 3: ("page7", "w1s_3")}
+QUADRANTS = (0, 2, 1, 3)
+CHUNK_ORDER = (0, 2, 1, 3)
+GPSIMD_ROW_TILES = 2
+
+W1_SLOTS = [("page2", "wg2"), ("tab2s", "wg3"), ("page3", "page4"), ("page5", "tab2")]
+DAMP_SLOTS = {
+    (2, 1): "page6",
+    (3, 1): "w1_codes_late",
+    (4, 1): "page7",
+    (5, 0): "v2_0",
+    (5, 1): "v2_1",
+    (6, 0): "v2s",
+    (7, 1): "page_codes0",
+}
+ROUND_W1_AFTER = 2
+LATE_LOADS_STEP = 2
+PAGE7_STEP = 3
+GATHER_WORKERS_STEP = 5
+QUANTISE_PASS0_STEP = 6
 
 
 def tile_list_farm_job_board_kernel(
@@ -40,154 +63,160 @@ def tile_list_farm_job_board_kernel(
         def bank(i, name):
             return psum.tile([P, BANK], F32, name=name, tag="bank%d" % i)
 
-        def load_scale_rows(queue, plane, rows, width):
-            for q in range(4):
+        def slot(shape, dtype, name, tag):
+            return work.tile(shape, dtype, name=name, tag=tag, align_bytes=64)
+
+        def entries(offsets, cols):
+            return offsets[:, cols.start // 16 : cols.stop // 16]
+
+        def load_scale_rows(queue, scales, quadrant_rows, count):
+            for q in QUADRANTS:
                 queue.dma_start(
-                    out=plane[32 * q : 32 * q + width, :].bitcast(I32),
-                    in_=(rows[0, 4 * q : 4 * q + 4, :] if width == 4 else rows[:, 4 * q : 4 * q + 4, :]).bitcast(I32),
+                    out=scales[32 * q : 32 * q + count, :].bitcast(I32),
+                    in_=quadrant_rows(slice(4 * q, 4 * q + 4)).bitcast(I32),
                 )
+
+        def copy_on(engine, dst, src):
+            if engine == "vector":
+                nc.vector.tensor_copy(out=dst, in_=src)
+            else:
+                nc.scalar.copy(out=dst, in_=src)
 
         list1 = keep.tile([P, S // 16], U16, name="list1")
         list2 = keep.tile([P, S2 // 16], U16, name="list2")
         list3 = keep.tile([P, S // 16], U16, name="list3")
         list4 = keep.tile([P, PICK // 16], U16, name="list4")
-
-        def slot(shape, dtype, name, tag):
-            return work.tile(shape, dtype, name=name, tag=tag, align_bytes=64)
-
-        w4_raw = slot([P, 2 * H], U8, "w4_raw", "page1")
-        w4s_raw = keep.tile([P, H], U8, name="w4s_raw", align_bytes=64)
-        tabs = slot([P, T], U8, "tabs", "page2")
-        seed = slot([P, 1], F32, "seed", "wg_rest")
-        one = slot([P, 1], F32, "one", "wg_first")
-        warm = slot([P, 1], F32, "warm", "page0")
-        warm_last = keep.tile([P, 1], F32, name="warm_last")
-        nc.vector.memset(tabs[:].bitcast(I32), 0)
-        nc.vector.memset(seed[:], 1.0)
-        nc.vector.tensor_copy(out=one[:], in_=seed[:])
-        nc.vector.memset(w4s_raw[:].bitcast(I32), 0)
-        nc.scalar.activation(out=warm[:], in_=one[:], func=ACT.Abs_reciprocal_sqrt)
-
-        nc.sync.dma_start(out=w4_raw[:].bitcast(I32), in_=w4_words[0].bitcast(I32))
         nc.sync.dma_start(list1[:], offs)
         nc.sync.dma_start(list3[:], offs3)
         nc.sync.dma_start(list2[:], offs2)
         nc.sync.dma_start(list4[:], offs4)
-        tab = slot([P, T], U32, "tab", "big")
-        nc.sync.dma_start(
-            out=tab[:].bitcast(I32),
-            in_=tab_words[0].rearrange("p n i -> p (n i)").bitcast(I32),
-        )
-        load_scale_rows(nc.sync, tabs, tab_scales, 4)
+
+        w4_raw = slot([P, 2 * H], U8, "w4_raw", "page0")
+        w4s_raw = slot([P, H], U8, "w4s_raw", "v_second")
+        tabs = slot([P, T], U8, "tabs", "wg0")
+        seed = slot([P, 1], F32, "seed", "big")
+        one = keep.tile([P, 1], F32, name="one")
+        warm = keep.tile([P, 2], F32, name="warm")
+        nc.vector.memset(tabs[:].bitcast(I32), 0)
+        nc.vector.memset(seed[:], 1.0)
+        nc.vector.tensor_copy(out=one[:], in_=seed[:])
+        nc.vector.memset(w4s_raw[:].bitcast(I32), 0)
+        nc.scalar.activation(out=warm[:, 0:1], in_=one[:], func=ACT.Abs_reciprocal_sqrt)
+        nc.sync.dma_start(out=w4_raw[:].bitcast(I32), in_=w4_words[0].bitcast(I32))
 
         w1_raw = []
 
         def load_w1(b):
-            raw = slot([P, 4, 512], F32, "w1_raw", "wg_rest" if b == 0 else "w1_late")
+            raw = slot([P, PACK, PASS], F32, "w1_raw", "page1" if b == 0 else "big")
             nc.sync.dma_start(
-                out=raw[:], in_=w1[:, 512 * b : 512 * (b + 1)].rearrange("(p j) c -> p j c", j=4)
+                out=raw[:],
+                in_=w1[:, PASS * b : PASS * (b + 1)].rearrange("(p j) c -> p j c", j=PACK),
             )
             w1_raw.append(raw)
 
         pages = []
 
         def load_page(k):
-            b, t = divmod(k, 4)
+            b, t = divmod(k, PACK)
             page = slot([P, T2], F32, "page", "page%d" % k)
-            rows = page0[512 * b : 512 * (b + 1), :].rearrange("(p t) c -> t p c", t=4)
+            rows = page0[PASS * b : PASS * (b + 1), :].rearrange("(p t) c -> t p c", t=PACK)
             nc.sync.dma_start(out=page[:], in_=rows[t])
             pages.append(page)
 
-        load_w1(0)
-        load_scale_rows(nc.sync, w4s_raw, w4_scales, 4)
-        load_page(0)
-        wg_rows = wgs.rearrange("(q t) j -> q (t j)", t=4)
+        wg_rows = wgs.rearrange("(q t) j -> t q j", t=PACK)
         wg = []
 
-        def load_weights(t0, t1, tag):
-            rows = slot([P, (t1 - t0) * S], F32, tag, tag)
-            for q in range(4):
-                nc.sync.dma_start(out=rows[32 * q : 32 * (q + 1), :], in_=wg_rows[:, t0 * S : t1 * S])
+        def load_weights(t):
+            rows = slot([P, S], F32, "wg", "wg%d" % t)
+            for q in QUADRANTS:
+                nc.sync.dma_start(out=rows[32 * q : 32 * (q + 1), :], in_=wg_rows[t])
             wg.append(rows)
 
-        def weight_rows(t, cols):
-            if t == 0:
-                return wg[0][:, cols]
-            return wg[1][:, (t - 1) * S + cols.start : (t - 1) * S + cols.stop]
-
-        load_weights(0, 1, "wg_first")
+        load_w1(0)
+        load_scale_rows(nc.sync, tabs, lambda rows: tab_scales[0, rows, :], 4)
+        tab = slot([P, T], U32, "tab", "big")
+        nc.sync.dma_start(
+            out=tab[:].bitcast(I32),
+            in_=tab_words[0].rearrange("p n i -> p (n i)").bitcast(I32),
+        )
+        load_scale_rows(nc.scalar, w4s_raw, lambda rows: w4_scales[0, rows, :], 4)
 
         w4 = []
-        w4s = []
         for b in range(PASSES):
-            words = keep.tile([P, 1024], U8, name="w4_%d" % b, align_bytes=64)
+            words = keep.tile([P, 2 * PASS], U8, name="w4_%d" % b, align_bytes=64)
             nc.vector.tensor_copy(
-                out=words[:].rearrange("p (t m e) -> p m t e", t=4, e=2),
-                in_=w4_raw[:, 1024 * b : 1024 * (b + 1)].rearrange("p (m t e) -> p m t e", t=4, e=2),
+                out=words[:].rearrange("p (t m e) -> p m t e", t=PACK, e=2),
+                in_=w4_raw[:, 2 * PASS * b : 2 * PASS * (b + 1)].rearrange(
+                    "p (m t e) -> p m t e", t=PACK, e=2
+                ),
             )
             w4.append(words)
-        load_page(1)
+        load_page(0)
+
+        w4s = []
 
         def order_w4_scales(b, t0, t1):
             scales = keep.tile([P, P * (t1 - t0)], U8, name="w4s_%d_%d" % (b, t0), align_bytes=64)
             nc.vector.tensor_copy(
                 out=scales[:].rearrange("p (t m) -> p m t", t=t1 - t0),
-                in_=w4s_raw[:, 512 * b : 512 * (b + 1)].rearrange("p (m t) -> p m t", t=4)[:, :, t0:t1],
+                in_=w4s_raw[:, PASS * b : PASS * (b + 1)].rearrange("p (m t) -> p m t", t=PACK)[:, :, t0:t1],
             )
             for t in range(t0, t1):
                 w4s.append(scales[:, P * (t - t0) : P * (t - t0 + 1)])
 
+        halves = [slice(BANK * half, BANK * (half + 1)) for half in range(HALVES)]
         v = []
         vs = []
+        for half in range(HALVES):
+            scales = keep.tile([P, BANK], U8, name="vs_%d" % half, align_bytes=64)
+            nc.vector.tensor_copy(scales[:], tabs[:].indirect(entries(list1, halves[half])))
+            vs.append(scales)
+        load_weights(0)
 
         def gather_vacancies(half):
-            picks = list1[:, 32 * half : 32 * (half + 1)]
-            words = keep.tile([P, BANK], U32, name="v_%d" % half, align_bytes=64)
-            scales = keep.tile([P, BANK], U8, name="vs_%d" % half, align_bytes=64)
-            nc.vector.tensor_copy(words[:], tab[:].indirect(picks))
-            nc.vector.tensor_copy(scales[:], tabs[:].indirect(picks))
+            words = slot([P, BANK], U32, "v", "v_second" if half else "v_first")
+            nc.vector.tensor_copy(words[:], tab[:].indirect(entries(list1, halves[half])))
             v.append(words)
-            vs.append(scales)
 
-        gather_vacancies(0)
-        order_w4_scales(0, 0, 1)
+        w1_rounded = []
+        w1q = []
 
-        w1q = {}
-
-        def quantise_w1(b):
-            rounded = slot([P, 2048], BF16, "w1_bf", "w1_bf")
+        def round_w1(b):
+            rounded = slot([P, PACK * PASS], BF16, "w1_rounded", "wg1" if b == 0 else "w1_rounded_late")
             nc.scalar.copy(
-                out=rounded[:].rearrange("p (t m j) -> p m j t", t=4, j=4),
-                in_=w1_raw[b][:].rearrange("p j (m t) -> p m j t", t=4),
+                out=rounded[:].rearrange("p (t m j) -> p m j t", t=PACK, j=PACK),
+                in_=w1_raw[b][:].rearrange("p j (m t) -> p m j t", t=PACK),
             )
-            if b == 0:
-                for t in range(4):
-                    codes = slot([P, P], U32, "w1c", LATER[t][0])
-                    scales = slot([P, P], U8, "w1s", LATER[t][1])
-                    nc.vector.quantize_mx(
-                        out=codes[:].bitcast(FP8X4), scales=scales[:],
-                        in_=rounded[:, 512 * t : 512 * (t + 1)],
-                    )
-                    w1q[t] = (codes[:], scales[:])
-                return
-            codes = slot([P, 512], U32, "w1c", "w1c_late")
-            scales = keep.tile([P, 512], U8, name="w1s_late", align_bytes=64)
-            nc.vector.quantize_mx(out=codes[:].bitcast(FP8X4), scales=scales[:], in_=rounded[:])
-            for t in range(4):
-                w1q[4 + t] = (codes[:, P * t : P * (t + 1)], scales[:, P * t : P * (t + 1)])
+            w1_rounded.append(rounded)
 
-        damped = {}
+        def quantise_w1_first():
+            for t in range(PACK):
+                codes = slot([P, P], U32, "w1_codes", W1_SLOTS[t][0])
+                scales = slot([P, P], U8, "w1_scales", W1_SLOTS[t][1])
+                nc.vector.quantize_mx(
+                    out=codes[:].bitcast(FP8X4), scales=scales[:],
+                    in_=w1_rounded[0][:, PASS * t : PASS * (t + 1)],
+                )
+                w1q.append((codes[:], scales[:]))
+
+        def quantise_w1_second():
+            codes = slot([P, PASS], U32, "w1_codes", "w1_codes_late")
+            scales = keep.tile([P, PASS], U8, name="w1_scales_late", align_bytes=64)
+            nc.vector.quantize_mx(out=codes[:].bitcast(FP8X4), scales=scales[:], in_=w1_rounded[1][:])
+            for t in range(PACK):
+                w1q.append((codes[:, P * t : P * (t + 1)], scales[:, P * t : P * (t + 1)]))
+
+        first_results = {}
 
         def first_stage(k):
-            b, t = divmod(k, 4)
+            b, t = divmod(k, PACK)
             base = 4 * (k % 2)
-            acc_b = [bank(base + half, "acc_b") for half in range(2)]
-            acc_a = [bank(base + 2 + half, "acc_a") for half in range(2)]
-            for half in range(2):
+            acc_b = [bank(base + half, "acc_b") for half in range(HALVES)]
+            acc_a = [bank(base + HALVES + half, "acc_a") for half in range(HALVES)]
+            for half in range(HALVES):
                 nc.tensor.matmul_mx(
                     out=acc_b[half][:],
-                    lhsT=w4[b][:, 256 * t : 256 * (t + 1)].bitcast(FP4X4),
-                    lhsT_scale=w4s[k],
+                    lhsT=w4[b][:, 2 * P * t : 2 * P * (t + 1)].bitcast(FP4X4), lhsT_scale=w4s[k],
                     rhs=v[half][:].bitcast(FP8X4), rhs_scale=vs[half][:],
                     start=True, stop=True,
                 )
@@ -198,220 +227,234 @@ def tile_list_farm_job_board_kernel(
                     start=True, stop=True,
                 )
             damp = []
-            for half in range(2):
-                tag = {(3, 1): "w1c_late", (7, 1): "board_codes"}.get((k, half), "damp%d" % (2 * (k % 2) + half))
+            for half in range(HALVES):
+                tag = DAMP_SLOTS.get((k, half), "damp%d" % (HALVES * (k % 2) + half))
                 damp.append(slot([P, BANK], F32, "damp", tag))
             if k == 0:
-                for half in range(2):
+                for half in range(HALVES):
                     size = slot([P, BANK], F32, "size", "root0")
                     root = slot([P, BANK], F32, "root", "root1")
-                    parts = FIRST_PARTS[half]
-                    for cols in parts:
+                    for cols in FIRST_PARTS[half]:
                         nc.scalar.activation(out=size[:, cols], in_=acc_b[half][:, cols], func=ACT.Abs)
-                    for cols in parts:
+                    for cols in FIRST_PARTS[half]:
                         nc.scalar.activation(
-                            out=root[:, cols], in_=size[:, cols], func=ACT.Abs_reciprocal_sqrt, bias=1.0
+                            out=root[:, cols], in_=size[:, cols], func=ACT.Abs_reciprocal_sqrt, bias=one[:]
                         )
-                    for cols in parts:
+                    for cols in FIRST_PARTS[half]:
                         nc.scalar.activation(out=damp[half][:, cols], in_=root[:, cols], func=ACT.Square)
             else:
-                roots = [slot([P, BANK], F32, "root", "root%d" % half) for half in range(2)]
-                for half in range(2):
-                    nc.scalar.activation(out=roots[half][:], in_=acc_b[half][:], func=ACT.Abs)
-                for half in range(2):
+                roots = [slot([P, BANK], F32, "root", "root%d" % half) for half in range(HALVES)]
+                sizes = list(roots)
+                if k == ROUND_W1_AFTER:
+                    sizes[1] = slot([P, BANK], F32, "size", "w1_rounded_late")
+                for half in range(HALVES):
+                    nc.scalar.activation(out=sizes[half][:], in_=acc_b[half][:], func=ACT.Abs)
+                for half in range(HALVES):
                     nc.scalar.activation(
-                        out=roots[half][:], in_=roots[half][:], func=ACT.Abs_reciprocal_sqrt, bias=1.0
+                        out=roots[half][:], in_=sizes[half][:], func=ACT.Abs_reciprocal_sqrt, bias=one[:]
                     )
-                for half in range(2):
+                for half in range(HALVES):
                     nc.scalar.activation(out=damp[half][:], in_=roots[half][:], func=ACT.Square)
-            damped[k] = (acc_a, damp)
+            first_results[k] = (acc_a, damp)
 
-        def edit_page(k):
-            acc_a, damp = damped[k]
-            if k == 0:
-                for half in range(2):
-                    h = slot([P, BANK], F32, "h_half", "h1")
-                    for cols in FIRST_PARTS[half]:
-                        entries = slice(BANK * half + cols.start, BANK * half + cols.stop)
-                        nc.vector.tensor_tensor(
-                            out=h[:, cols], in0=acc_a[half][:, cols], in1=damp[half][:, cols], op=MULT
-                        )
-                        nc.vector.tensor_tensor(
-                            pages[k][:].indirect(list3[:, entries.start // 16 : entries.stop // 16]),
-                            h[:, cols], weight_rows(0, entries), MULT,
-                        )
+        def edit_first_plane():
+            acc_a, damp = first_results[0]
+            for half in range(HALVES):
+                h = slot([P, BANK], F32, "h_half", "h1")
+                for cols in FIRST_PARTS[half]:
+                    listed = slice(BANK * half + cols.start, BANK * half + cols.stop)
+                    nc.vector.tensor_tensor(
+                        out=h[:, cols], in0=acc_a[half][:, cols], in1=damp[half][:, cols], op=MULT
+                    )
+                    nc.vector.tensor_tensor(
+                        pages[0][:].indirect(entries(list3, listed)), h[:, cols], wg[0][:, listed], MULT
+                    )
 
         features = {}
 
-        def damp_next(k):
-            acc_a, damp = damped[k]
+        def make_h(k):
+            acc_a, damp = first_results[k]
             h = slot([P, S], F32, "h", "h%d" % (k % 2))
-            for half in range(2):
-                cols = slice(BANK * half, BANK * (half + 1))
-                nc.vector.tensor_tensor(out=h[:, cols], in0=acc_a[half][:], in1=damp[half][:], op=MULT)
+            for half in range(HALVES):
+                nc.vector.tensor_tensor(
+                    out=h[:, halves[half]], in0=acc_a[half][:], in1=damp[half][:], op=MULT
+                )
             features[k] = h
 
         def scatter(k):
-            nc.vector.tensor_tensor(
-                pages[k][:].indirect(list3[:]), features[k][:], weight_rows(k % 4, slice(0, S)), MULT
-            )
+            nc.vector.tensor_tensor(pages[k][:].indirect(list3[:]), features[k][:], wg[k % PACK][:], MULT)
 
         pairs = {}
-        board = {}
+        woven = {}
+        page_codes = {}
+        page_q = {}
 
-        def copy_on(engine, dst, src):
-            if engine == "vector":
-                nc.vector.tensor_copy(out=dst, in_=src)
-            else:
-                nc.scalar.copy(out=dst, in_=src)
+        def tail_engine(c):
+            return "vector" if c % 2 == 0 else "scalar"
 
         def round_plane(k, c, engine):
-            b, t = divmod(k, 4)
+            b, t = divmod(k, PACK)
             if t == 0:
-                pairs[(b, c)] = work.tile([P, 2 * BANK * 2], BF16, name="pairs", tag="pairs", bufs=CHUNKS, align_bytes=64)
+                pairs[(b, c)] = work.tile(
+                    [P, PACK * BANK], BF16, name="pairs", tag="pairs", bufs=CHUNKS, align_bytes=64
+                )
             dst = pairs[(b, c)][:].rearrange("p (u c e) -> p u c e", u=2, e=2)
             src = pages[k][:, BANK * c : BANK * (c + 1)]
-            if k == PLANES - 2 and c % 2 == 0:
+            if k == LAST - 1 and tail_engine(c) == "vector":
                 copy_on(engine, dst[:, t // 2, :, :], src.unsqueeze(2).to_broadcast([P, BANK, 2]))
             else:
                 copy_on(engine, dst[:, t // 2, :, t % 2], src)
 
         def weave(b, c, engine):
-            woven = work.tile([P, 4 * BANK], BF16, name="woven", tag="woven", bufs=CHUNKS, align_bytes=64)
+            dense = work.tile([P, PACK * BANK], BF16, name="woven", tag="woven", bufs=CHUNKS, align_bytes=64)
             copy_on(
                 engine,
-                woven[:].bitcast(F32).rearrange("p (c u) -> p c u", u=2),
+                dense[:].bitcast(F32).rearrange("p (c u) -> p c u", u=2),
                 pairs[(b, c)][:].bitcast(F32).rearrange("p (u c) -> p c u", u=2),
             )
-            board[(b, c)] = woven
+            woven[(b, c)] = dense
 
-        boardq = {}
-        board_codes = {}
-
-        def quantise_board(b, c):
+        def quantise_page(b, c):
             if c == 0:
-                board_codes[b] = slot([P, T2], U32, "board_codes", "board_codes" if b == 0 else "board_codes_last")
-            codes = board_codes[b][:, BANK * c : BANK * (c + 1)]
-            scales = keep.tile([P, BANK], U8, name="bs_%d_%d" % (b, c), align_bytes=64)
-            nc.vector.quantize_mx(out=codes.bitcast(FP8X4), scales=scales[:], in_=board[(b, c)][:])
-            boardq[(b, c)] = (codes, scales)
+                page_codes[b] = slot([P, T2], U32, "page_codes", "page_codes%d" % b)
+            codes = page_codes[b][:, BANK * c : BANK * (c + 1)]
+            scales = keep.tile([P, BANK], U8, name="page_scales_%d_%d" % (b, c), align_bytes=64)
+            nc.vector.quantize_mx(out=codes.bitcast(FP8X4), scales=scales[:], in_=woven[(b, c)][:])
+            page_q[(b, c)] = (codes, scales)
 
+        tab2_scale_tile = []
+        tab2_passes = []
         v2 = []
-        v2s = keep.tile([P, S2], U8, name="v2s", align_bytes=64)
+        v2s = []
 
-        def gather_workers():
-            tab2 = slot([P, PASSES * T3], U32, "tab2", "big")
+        def load_worker_scales():
             tab2s = slot([P, T3], U8, "tab2s", "tab2s")
             nc.vector.memset(tab2s[:].bitcast(I32), 0)
-            load_scale_rows(nc.sync, tab2s, tab2_scales, 8)
+            load_scale_rows(nc.sync, tab2s, lambda rows: tab2_scales[:, rows, :], 4 * PASSES)
+            tab2_scale_tile.append(tab2s)
+
+        def load_worker_words():
+            tab2 = slot([P, PASSES * T3], U32, "tab2", "tab2")
             for b in range(PASSES):
                 table = tab2[:, T3 * b : T3 * (b + 1)]
                 nc.sync.dma_start(
                     out=table.bitcast(I32),
                     in_=tab2_words[b].rearrange("p n i -> p (n i)").bitcast(I32),
                 )
-                words = keep.tile([P, S2], U32, name="v2_%d" % b, align_bytes=64)
-                nc.vector.tensor_copy(words[:], table.indirect(list2[:]))
+                tab2_passes.append(table)
+
+        def gather_workers():
+            for b in range(PASSES):
+                words = slot([P, S2], U32, "v2", "v2_%d" % b)
+                nc.vector.tensor_copy(words[:], tab2_passes[b].indirect(list2[:]))
                 v2.append(words)
-            nc.vector.tensor_copy(v2s[:], tab2s[:].indirect(list2[:]))
+            scales = slot([P, S2], U8, "v2s", "v2s")
+            nc.vector.tensor_copy(scales[:], tab2_scale_tile[0][:].indirect(list2[:]))
+            v2s.append(scales)
 
         scores = {}
 
         def score_pass(n, c, b):
             if b == 0:
-                scores[(n, c)] = bank(4 * (n % 2) + c, "score")
+                scores[(n, c)] = bank(CHUNKS * (n % 2) + c, "score")
             cols = slice(P * n, P * (n + 1))
             nc.tensor.matmul_mx(
                 out=scores[(n, c)][:],
-                lhsT=v2[b][:, cols].bitcast(FP8X4), lhsT_scale=v2s[4 * b : P, cols],
-                rhs=boardq[(b, c)][0].bitcast(FP8X4), rhs_scale=boardq[(b, c)][1][:],
+                lhsT=v2[b][:, cols].bitcast(FP8X4), lhsT_scale=v2s[0][4 * b : P, cols],
+                rhs=page_q[(b, c)][0].bitcast(FP8X4), rhs_scale=page_q[(b, c)][1][:],
                 start=(b == 0), stop=(b == PASSES - 1),
             )
 
+        round_w1(0)
+        quantise_w1_first()
+        load_page(1)
+        load_weights(1)
+        order_w4_scales(0, 0, 1)
+        gather_vacancies(0)
+        order_w4_scales(0, 1, PACK)
+        order_w4_scales(1, 0, PACK)
         gather_vacancies(1)
-        quantise_w1(0)
-        load_weights(1, 4, "wg_rest")
-        order_w4_scales(0, 1, 4)
-        order_w4_scales(1, 0, 4)
-        load_page(2)
-        first_stage(0)
         load_w1(1)
-        edit_page(0)
+        first_stage(0)
+        load_page(2)
+        load_weights(2)
+        edit_first_plane()
         first_stage(1)
+        load_weights(3)
+        load_worker_scales()
+        first_stage(2)
         load_page(3)
         load_page(4)
-        first_stage(2)
-        load_page(5)
-        load_page(6)
-        for c in range(CHUNKS):
-            round_plane(0, c, "scalar")
-        damp_next(1)
-        gather_workers()
-        allowed = slot([P, NTILES, PICK], F32, "allowed", "big")
-        nc.sync.dma_start(out=allowed[:], in_=permit.rearrange("(n p) m -> p n m", p=P))
+        round_w1(1)
+        allowed = slot([P, ROW_TILES, PICK], F32, "allowed", "big")
+        make_h(1)
+
         for k in range(1, PLANES):
-            if k + 1 < PLANES:
-                damp_next(k + 1)
+            if k < LAST:
+                make_h(k + 1)
+            if k == LATE_LOADS_STEP:
+                quantise_w1_second()
             scatter(k)
-            if k == 2:
+            if k == GATHER_WORKERS_STEP:
+                gather_workers()
+            if k == LATE_LOADS_STEP:
+                load_page(5)
+                load_page(6)
+                load_worker_words()
+                nc.sync.dma_start(out=allowed[:], in_=permit.rearrange("(n p) m -> p n m", p=P))
+            if k == PAGE7_STEP:
                 load_page(7)
-                quantise_w1(1)
-            if k + 2 < PLANES:
+            if k + 2 <= LAST:
                 first_stage(k + 2)
-            if k + 2 == PLANES - 1:
-                nc.scalar.activation(out=warm_last[:], in_=damped[k + 2][1][1][:, 0:1], func=ACT.Sigmoid)
-            if k == 4:
+            if k + 2 == LAST:
+                nc.scalar.activation(out=warm[:, 1:2], in_=first_results[LAST][1][1][:, 0:1], func=ACT.Sigmoid)
+            for c in range(CHUNKS):
+                round_plane(k - 1, c, "scalar")
+            if k == PACK:
                 for c in range(CHUNKS):
                     weave(0, c, "scalar")
-            if k == 6:
+            if k == QUANTISE_PASS0_STEP:
                 for c in range(CHUNKS):
-                    quantise_board(0, c)
-            if k < PLANES - 1:
-                for c in range(CHUNKS):
-                    round_plane(k, c, "scalar")
+                    quantise_page(0, c)
+
         for n in range(2):
             for c in range(CHUNKS):
                 score_pass(n, c, 0)
-
-        order = [0, 2, 1, 3]
-        for c in order:
-            engine = "vector" if c % 2 == 0 else "scalar"
-            round_plane(PLANES - 1, c, engine)
-        for c in order:
-            engine = "vector" if c % 2 == 0 else "scalar"
-            weave(1, c, engine)
-        for c in order:
-            quantise_board(1, c)
+        for c in CHUNK_ORDER:
+            round_plane(LAST, c, tail_engine(c))
+        for c in CHUNK_ORDER:
+            weave(1, c, tail_engine(c))
+        for c in CHUNK_ORDER:
+            quantise_page(1, c)
             for n in range(2):
                 score_pass(n, c, 1)
 
-        def finish(n):
+        def pick_scores(n):
             e = slot([P, T2], F32, "e", "page%d" % n)
-            for c in order:
-                engine = "vector" if (n == 0 and c == order[-1]) else "scalar"
+            for c in CHUNK_ORDER:
+                engine = "vector" if (n == 0 and c == CHUNK_ORDER[-1]) else "scalar"
                 copy_on(engine, e[:, BANK * c : BANK * (c + 1)], scores[(n, c)][:])
-            if n + 2 < NTILES:
-                for c in order:
+            if n + 2 < ROW_TILES:
+                for c in CHUNK_ORDER:
                     for b in range(PASSES):
                         score_pass(n + 2, c, b)
             x = work.tile([P, PICK], F32, name="x", tag="pairs", bufs=CHUNKS, align_bytes=64)
-            steps = []
-            for cols in (LAST_PARTS if n == NTILES - 1 else [slice(0, PICK)]):
-                picks = list4[:, cols.start // 16 : cols.stop // 16]
-                nc.vector.tensor_copy(x[:, cols], e[:].indirect(picks))
-                steps.append(cols)
-            return x, steps
+            parts = LAST_PARTS if n == ROW_TILES - 1 else [slice(0, PICK)]
+            for cols in parts:
+                nc.vector.tensor_copy(x[:, cols], e[:].indirect(entries(list4, cols)))
+            return x, parts
 
-        def weigh(n, x, steps):
-            for cols in steps:
+        def weigh_and_store(n, x, parts):
+            engine = nc.gpsimd if n < GPSIMD_ROW_TILES else nc.vector
+            for cols in parts:
                 nc.scalar.activation(out=x[:, cols], in_=x[:, cols], func=ACT.Sigmoid)
-                nc.vector.tensor_tensor(out=x[:, cols], in0=x[:, cols], in1=allowed[:, n, cols], op=MULT)
+                engine.tensor_tensor(out=x[:, cols], in0=x[:, cols], in1=allowed[:, n, cols], op=MULT)
                 nc.sync.dma_start(out=out[P * n : P * (n + 1), cols], in_=x[:, cols])
 
         picked = []
-        for n in range(NTILES):
-            picked.append(finish(n))
-            if n == NTILES - 2:
-                weigh(0, picked[0][0], picked[0][1])
-        for n in range(1, NTILES):
-            weigh(n, picked[n][0], picked[n][1])
+        for n in range(ROW_TILES):
+            picked.append(pick_scores(n))
+            if n == ROW_TILES - 2:
+                weigh_and_store(0, picked[0][0], picked[0][1])
+        for n in range(1, ROW_TILES):
+            weigh_and_store(n, picked[n][0], picked[n][1])

@@ -9,12 +9,13 @@ F32 = mybir.dt.float32
 BF16 = mybir.dt.bfloat16
 I32 = mybir.dt.int32
 U32 = mybir.dt.uint32
-U16 = mybir.dt.uint16
 U8 = mybir.dt.uint8
+U16 = mybir.dt.uint16
 FP8X4 = mybir.dt.float8_e4m3fn_x4
 FP4X4 = mybir.dt.float4_e2m1fn_x4
 ACT = mybir.ActivationFunctionType
 MULT = mybir.AluOpType.mult
+ADD = mybir.AluOpType.add
 
 P = 128
 BANK = 512
@@ -26,28 +27,16 @@ HALVES = S // BANK
 CHUNKS = T2 // BANK
 ROW_TILES = S2 // P
 LAST = PLANES - 1
-
-FIRST_PARTS = [[slice(0, 256), slice(256, 512)], [slice(0, 512)]]
-LAST_PARTS = [slice(0, 768), slice(768, 1024)]
+WIDE = T2 // 2
+LINE = 4
 QUADRANTS = (0, 2, 1, 3)
-CHUNK_ORDER = (0, 2, 1, 3)
+LAST_PARTS = [slice(0, 768), slice(768, 1024)]
 GPSIMD_ROW_TILES = 2
-
-W1_SLOTS = [("page2", "wg2"), ("tab2s", "wg3"), ("page3", "page4"), ("page5", "tab2")]
-DAMP_SLOTS = {
-    (2, 1): "page6",
-    (3, 1): "w1_codes_late",
-    (4, 1): "page7",
-    (5, 0): "v2_0",
-    (5, 1): "v2_1",
-    (6, 0): "v2s",
-    (7, 1): "page_codes0",
-}
-ROUND_W1_AFTER = 2
-LATE_LOADS_STEP = 2
-PAGE7_STEP = 3
-GATHER_WORKERS_STEP = 5
-QUANTISE_PASS0_STEP = 6
+GAIN_SLOTS = ["page2", "page3", "page4", "page5", "gain", "page7", "gain", "gain"]
+PLAIN_SLOTS = [None, "plain", "tab2s", "plain", "tab2_0", "tab2_1", "side1", "plain"]
+EDIT_SLOTS = ["edit_a", "edit_b", "edit_a", "page6", "v2s", "codes0_0", "codes0_1", "edit_b"]
+SPLIT_SCATTERS = 2
+FIRST_PARTS = [slice(0, 256), slice(256, 512), slice(512, 1024)]
 
 
 def tile_list_farm_job_board_kernel(
@@ -76,25 +65,26 @@ def tile_list_farm_job_board_kernel(
                     in_=quadrant_rows(slice(4 * q, 4 * q + 4)).bitcast(I32),
                 )
 
-        def copy_on(engine, dst, src):
+        def round_on(engine, dst, src):
             if engine == "vector":
                 nc.vector.tensor_copy(out=dst, in_=src)
-            else:
+            elif engine == "scalar":
                 nc.scalar.copy(out=dst, in_=src)
+            else:
+                nc.gpsimd.tensor_scalar(out=dst, in0=src, scalar1=1.0, scalar2=0.0, op0=MULT, op1=ADD)
+
+        halves = [slice(BANK * half, BANK * (half + 1)) for half in range(HALVES)]
+        chunks = [slice(BANK * c, BANK * (c + 1)) for c in range(CHUNKS)]
 
         list1 = keep.tile([P, S // 16], U16, name="list1")
         list2 = keep.tile([P, S2 // 16], U16, name="list2")
         list3 = keep.tile([P, S // 16], U16, name="list3")
         list4 = keep.tile([P, PICK // 16], U16, name="list4")
-        nc.sync.dma_start(list1[:], offs)
-        nc.sync.dma_start(list3[:], offs3)
-        nc.sync.dma_start(list2[:], offs2)
-        nc.sync.dma_start(list4[:], offs4)
 
-        w4_raw = slot([P, 2 * H], U8, "w4_raw", "page0")
-        w4s_raw = slot([P, H], U8, "w4s_raw", "v_second")
-        tabs = slot([P, T], U8, "tabs", "wg0")
-        seed = slot([P, 1], F32, "seed", "big")
+        tabs = slot([P, T], U8, "tabs", "w4s")
+        w4s_raw = slot([P, H], U8, "w4s_raw", "w1_late")
+        w4_raw = slot([P, 2 * H], U8, "w4_raw", "wg0")
+        seed = slot([P, 1], F32, "seed", "page1")
         one = keep.tile([P, 1], F32, name="one")
         warm = keep.tile([P, 2], F32, name="warm")
         nc.vector.memset(tabs[:].bitcast(I32), 0)
@@ -102,12 +92,11 @@ def tile_list_farm_job_board_kernel(
         nc.vector.tensor_copy(out=one[:], in_=seed[:])
         nc.vector.memset(w4s_raw[:].bitcast(I32), 0)
         nc.scalar.activation(out=warm[:, 0:1], in_=one[:], func=ACT.Abs_reciprocal_sqrt)
-        nc.sync.dma_start(out=w4_raw[:].bitcast(I32), in_=w4_words[0].bitcast(I32))
 
         w1_raw = []
 
         def load_w1(b):
-            raw = slot([P, PACK, PASS], F32, "w1_raw", "page1" if b == 0 else "big")
+            raw = slot([P, PACK, PASS], F32, "w1_raw", "page0" if b == 0 else "w1_late")
             nc.sync.dma_start(
                 out=raw[:],
                 in_=w1[:, PASS * b : PASS * (b + 1)].rearrange("(p j) c -> p j c", j=PACK),
@@ -132,313 +121,308 @@ def tile_list_farm_job_board_kernel(
                 nc.sync.dma_start(out=rows[32 * q : 32 * (q + 1), :], in_=wg_rows[t])
             wg.append(rows)
 
+        nc.sync.dma_start(list1[:], offs)
+        nc.sync.dma_start(list3[:], offs3)
+        nc.sync.dma_start(list2[:], offs2)
+        nc.sync.dma_start(list4[:], offs4)
+        nc.sync.dma_start(out=w4_raw[:].bitcast(I32), in_=w4_words[0].bitcast(I32))
         load_w1(0)
         load_scale_rows(nc.sync, tabs, lambda rows: tab_scales[0, rows, :], 4)
-        tab = slot([P, T], U32, "tab", "big")
+        tab = slot([P, T], U32, "tab", "page1")
         nc.sync.dma_start(
             out=tab[:].bitcast(I32),
             in_=tab_words[0].rearrange("p n i -> p (n i)").bitcast(I32),
         )
         load_scale_rows(nc.scalar, w4s_raw, lambda rows: w4_scales[0, rows, :], 4)
 
-        w4 = []
+        w4 = keep.tile([P, 2 * H], U8, name="w4", align_bytes=64)
         for b in range(PASSES):
-            words = keep.tile([P, 2 * PASS], U8, name="w4_%d" % b, align_bytes=64)
             nc.vector.tensor_copy(
-                out=words[:].rearrange("p (t m e) -> p m t e", t=PACK, e=2),
-                in_=w4_raw[:, 2 * PASS * b : 2 * PASS * (b + 1)].rearrange(
-                    "p (m t e) -> p m t e", t=PACK, e=2
-                ),
+                out=w4[:, 2 * PASS * b : 2 * PASS * (b + 1)].rearrange("p (t m e) -> p m t e", t=PACK, e=2),
+                in_=w4_raw[:, 2 * PASS * b : 2 * PASS * (b + 1)].rearrange("p (m t e) -> p m t e", t=PACK, e=2),
             )
-            w4.append(words)
-        load_page(0)
-
-        w4s = []
-
-        def order_w4_scales(b, t0, t1):
-            scales = keep.tile([P, P * (t1 - t0)], U8, name="w4s_%d_%d" % (b, t0), align_bytes=64)
-            nc.vector.tensor_copy(
-                out=scales[:].rearrange("p (t m) -> p m t", t=t1 - t0),
-                in_=w4s_raw[:, PASS * b : PASS * (b + 1)].rearrange("p (m t) -> p m t", t=PACK)[:, :, t0:t1],
-            )
-            for t in range(t0, t1):
-                w4s.append(scales[:, P * (t - t0) : P * (t - t0 + 1)])
-
-        halves = [slice(BANK * half, BANK * (half + 1)) for half in range(HALVES)]
-        v = []
-        vs = []
-        for half in range(HALVES):
-            scales = keep.tile([P, BANK], U8, name="vs_%d" % half, align_bytes=64)
-            nc.vector.tensor_copy(scales[:], tabs[:].indirect(entries(list1, halves[half])))
-            vs.append(scales)
         load_weights(0)
 
-        def gather_vacancies(half):
-            words = slot([P, BANK], U32, "v", "v_second" if half else "v_first")
+        w1_codes = keep.tile([P, H], U32, name="w1_codes", align_bytes=64)
+        w1_scales = keep.tile([P, H], U8, name="w1_scales", align_bytes=64)
+
+        def prepare_w1(b, engine):
+            rounded = slot([P, PACK * PASS], BF16, "w1_rounded", "wg1" if b == 0 else "codes0_0")
+            round_on(
+                engine,
+                rounded[:].rearrange("p (t m j) -> p m j t", t=PACK, j=PACK),
+                w1_raw[b][:].rearrange("p j (m t) -> p m j t", t=PACK),
+            )
+            cols = slice(PASS * b, PASS * (b + 1))
+            nc.vector.quantize_mx(
+                out=w1_codes[:, cols].bitcast(FP8X4), scales=w1_scales[:, cols], in_=rounded[:]
+            )
+
+        prepare_w1(0, "scalar")
+        load_page(0)
+        load_weights(1)
+        vs = keep.tile([P, S], U8, name="vs", align_bytes=64)
+        nc.vector.tensor_copy(vs[:], tabs[:].indirect(list1[:]))
+        w4s = slot([P, H], U8, "w4s", "w4s")
+        for b in range(PASSES):
+            nc.vector.tensor_copy(
+                out=w4s[:, PASS * b : PASS * (b + 1)].rearrange("p (t m) -> p m t", t=PACK),
+                in_=w4s_raw[:, PASS * b : PASS * (b + 1)].rearrange("p (m t) -> p m t", t=PACK),
+            )
+        load_w1(1)
+
+        v = []
+        for half in range(HALVES):
+            words = keep.tile([P, BANK], U32, name="v%d" % half, align_bytes=64)
             nc.vector.tensor_copy(words[:], tab[:].indirect(entries(list1, halves[half])))
             v.append(words)
+        load_page(1)
 
-        w1_rounded = []
-        w1q = []
+        woven0_tags = ["W0a", "W0b"]
+        made = {}
+        last_tiles = {}
 
-        def round_w1(b):
-            rounded = slot([P, PACK * PASS], BF16, "w1_rounded", "wg1" if b == 0 else "w1_rounded_late")
-            nc.scalar.copy(
-                out=rounded[:].rearrange("p (t m j) -> p m j t", t=PACK, j=PACK),
-                in_=w1_raw[b][:].rearrange("p j (m t) -> p m j t", t=PACK),
+        def products(k, cols, bank_b, bank_a):
+            rows = slice(P * k, P * (k + 1))
+            half, start = divmod(cols.start, BANK)
+            width = cols.stop - cols.start
+            words = v[half][:, start : start + width].bitcast(FP8X4)
+            acc_b = bank(bank_b, "acc_b")[:, 0:width]
+            acc_a = bank(bank_a, "acc_a")[:, 0:width]
+            nc.tensor.matmul_mx(
+                out=acc_b,
+                lhsT=w4[:, 2 * rows.start : 2 * rows.stop].bitcast(FP4X4), lhsT_scale=w4s[:, rows],
+                rhs=words, rhs_scale=vs[:, cols], start=True, stop=True,
             )
-            w1_rounded.append(rounded)
+            nc.tensor.matmul_mx(
+                out=acc_a,
+                lhsT=w1_codes[:, rows].bitcast(FP8X4), lhsT_scale=w1_scales[:, rows],
+                rhs=words, rhs_scale=vs[:, cols], start=True, stop=True,
+            )
+            return acc_b, acc_a
 
-        def quantise_w1_first():
-            for t in range(PACK):
-                codes = slot([P, P], U32, "w1_codes", W1_SLOTS[t][0])
-                scales = slot([P, P], U8, "w1_scales", W1_SLOTS[t][1])
-                nc.vector.quantize_mx(
-                    out=codes[:].bitcast(FP8X4), scales=scales[:],
-                    in_=w1_rounded[0][:, PASS * t : PASS * (t + 1)],
-                )
-                w1q.append((codes[:], scales[:]))
+        def size(root, acc_b):
+            nc.scalar.activation(out=root, in_=acc_b, func=ACT.Abs)
 
-        def quantise_w1_second():
-            codes = slot([P, PASS], U32, "w1_codes", "w1_codes_late")
-            scales = keep.tile([P, PASS], U8, name="w1_scales_late", align_bytes=64)
-            nc.vector.quantize_mx(out=codes[:].bitcast(FP8X4), scales=scales[:], in_=w1_rounded[1][:])
-            for t in range(PACK):
-                w1q.append((codes[:, P * t : P * (t + 1)], scales[:, P * t : P * (t + 1)]))
+        def invert(root):
+            nc.scalar.activation(out=root, in_=root, func=ACT.Abs_reciprocal_sqrt, bias=one[:])
 
-        first_results = {}
+        def damp(gain, root):
+            nc.scalar.activation(out=gain, in_=root, func=ACT.Square)
+
+        def put(k, edit, cols):
+            nc.vector.tensor_copy(pages[k][:].indirect(entries(list3, cols)), edit[:, cols])
+
+        def first_plane():
+            gain = slot([P, S], F32, "gain", GAIN_SLOTS[0])
+            edit = slot([P, S], F32, "edit", EDIT_SLOTS[0])
+            root_tags = ["root0", "wg2", "wg3"]
+            for i, cols in enumerate(FIRST_PARTS):
+                acc_b, acc_a = products(0, cols, 2 * i, 2 * i + 1)
+                root = slot([P, cols.stop - cols.start], F32, "root", root_tags[i])[:]
+                size(root, acc_b)
+                invert(root)
+                damp(gain[:, cols], root)
+                engine = nc.vector if i == 0 else nc.gpsimd
+                engine.tensor_tensor(out=gain[:, cols], in0=gain[:, cols], in1=wg[0][:, cols], op=MULT)
+                nc.vector.tensor_tensor(out=edit[:, cols], in0=acc_a, in1=gain[:, cols], op=MULT)
+                put(0, edit, cols)
 
         def first_stage(k):
-            b, t = divmod(k, PACK)
-            base = 4 * (k % 2)
-            acc_b = [bank(base + half, "acc_b") for half in range(HALVES)]
-            acc_a = [bank(base + HALVES + half, "acc_a") for half in range(HALVES)]
-            for half in range(HALVES):
-                nc.tensor.matmul_mx(
-                    out=acc_b[half][:],
-                    lhsT=w4[b][:, 2 * P * t : 2 * P * (t + 1)].bitcast(FP4X4), lhsT_scale=w4s[k],
-                    rhs=v[half][:].bitcast(FP8X4), rhs_scale=vs[half][:],
-                    start=True, stop=True,
-                )
-                nc.tensor.matmul_mx(
-                    out=acc_a[half][:],
-                    lhsT=w1q[k][0].bitcast(FP8X4), lhsT_scale=w1q[k][1],
-                    rhs=v[half][:].bitcast(FP8X4), rhs_scale=vs[half][:],
-                    start=True, stop=True,
-                )
-            damp = []
-            for half in range(HALVES):
-                tag = DAMP_SLOTS.get((k, half), "damp%d" % (HALVES * (k % 2) + half))
-                damp.append(slot([P, BANK], F32, "damp", tag))
-            if k == 0:
-                for half in range(HALVES):
-                    size = slot([P, BANK], F32, "size", "root0")
-                    root = slot([P, BANK], F32, "root", "root1")
-                    for cols in FIRST_PARTS[half]:
-                        nc.scalar.activation(out=size[:, cols], in_=acc_b[half][:, cols], func=ACT.Abs)
-                    for cols in FIRST_PARTS[half]:
-                        nc.scalar.activation(
-                            out=root[:, cols], in_=size[:, cols], func=ACT.Abs_reciprocal_sqrt, bias=one[:]
-                        )
-                    for cols in FIRST_PARTS[half]:
-                        nc.scalar.activation(out=damp[half][:, cols], in_=root[:, cols], func=ACT.Square)
-            else:
-                roots = [slot([P, BANK], F32, "root", "root%d" % half) for half in range(HALVES)]
-                sizes = list(roots)
-                if k == ROUND_W1_AFTER:
-                    sizes[1] = slot([P, BANK], F32, "size", "w1_rounded_late")
-                for half in range(HALVES):
-                    nc.scalar.activation(out=sizes[half][:], in_=acc_b[half][:], func=ACT.Abs)
-                for half in range(HALVES):
-                    nc.scalar.activation(
-                        out=roots[half][:], in_=sizes[half][:], func=ACT.Abs_reciprocal_sqrt, bias=one[:]
-                    )
-                for half in range(HALVES):
-                    nc.scalar.activation(out=damp[half][:], in_=roots[half][:], func=ACT.Square)
-            first_results[k] = (acc_a, damp)
-
-        def edit_first_plane():
-            acc_a, damp = first_results[0]
-            for half in range(HALVES):
-                h = slot([P, BANK], F32, "h_half", "h1")
-                for cols in FIRST_PARTS[half]:
-                    listed = slice(BANK * half + cols.start, BANK * half + cols.stop)
-                    nc.vector.tensor_tensor(
-                        out=h[:, cols], in0=acc_a[half][:, cols], in1=damp[half][:, cols], op=MULT
-                    )
-                    nc.vector.tensor_tensor(
-                        pages[0][:].indirect(entries(list3, listed)), h[:, cols], wg[0][:, listed], MULT
-                    )
-
-        features = {}
-
-        def make_h(k):
-            acc_a, damp = first_results[k]
-            h = slot([P, S], F32, "h", "h%d" % (k % 2))
-            for half in range(HALVES):
-                nc.vector.tensor_tensor(
-                    out=h[:, halves[half]], in0=acc_a[half][:], in1=damp[half][:], op=MULT
-                )
-            features[k] = h
+            t = k % PACK
+            banks = (6, 0, 7, 1) if k % 2 else (2, 3, 4, 5)
+            accs = [products(k, halves[half], banks[2 * half], banks[2 * half + 1]) for half in range(HALVES)]
+            root_tags = ["root0", "root1"]
+            if k == LAST - 1:
+                root_tags = woven0_tags
+            if k == LAST:
+                root_tags = ["B", "root1"]
+            roots = [slot([P, BANK], F32, "root", root_tags[half])[:] for half in range(HALVES)]
+            gain = slot([P, S], F32, "gain", GAIN_SLOTS[k])
+            plain = slot([P, S], F32, "plain", PLAIN_SLOTS[k])
+            edit = slot([P, S], F32, "edit", EDIT_SLOTS[k])
+            size(roots[0], accs[0][0])
+            size(roots[1], accs[1][0])
+            invert(roots[0])
+            nc.scalar.copy(out=plain[:, halves[0]], in_=accs[0][1])
+            damp(gain[:, halves[0]], roots[0])
+            invert(roots[1])
+            nc.scalar.copy(out=plain[:, halves[1]], in_=accs[1][1])
+            damp(gain[:, halves[1]], roots[1])
+            parts = [slice(0, S)]
+            if k < SPLIT_SCATTERS:
+                parts = halves
+            if k == LAST:
+                parts = halves[::-1]
+            for h in parts:
+                weighted = slot([P, h.stop - h.start], F32, "weighted", "weighted")
+                nc.gpsimd.tensor_tensor(out=weighted[:], in0=gain[:, h], in1=wg[t][:, h], op=MULT)
+                nc.gpsimd.tensor_tensor(out=edit[:, h], in0=plain[:, h], in1=weighted[:], op=MULT)
+            made[k] = edit
+            last_tiles[k] = gain
 
         def scatter(k):
-            nc.vector.tensor_tensor(pages[k][:].indirect(list3[:]), features[k][:], wg[k % PACK][:], MULT)
+            for cols in halves if k < SPLIT_SCATTERS else [slice(0, S)]:
+                put(k, made[k], cols)
 
-        pairs = {}
-        woven = {}
-        page_codes = {}
-        page_q = {}
+        side0 = []
 
-        def tail_engine(c):
-            return "vector" if c % 2 == 0 else "scalar"
+        def gather_plane_pass0(k):
+            for w in range(2):
+                if k == 0:
+                    side0.append(slot([P, PACK, WIDE], F32, "side0", "AB"[w]))
+                nc.sync.dma_start(out=side0[w][:, k, :], in_=pages[k][:, WIDE * w : WIDE * (w + 1)])
 
-        def round_plane(k, c, engine):
-            b, t = divmod(k, PACK)
-            if t == 0:
-                pairs[(b, c)] = work.tile(
-                    [P, PACK * BANK], BF16, name="pairs", tag="pairs", bufs=CHUNKS, align_bytes=64
+        codes0 = []
+        scales0 = keep.tile([P, T2], U8, name="scales0", align_bytes=64)
+
+        woven = []
+
+        def weave_pass0():
+            for w in range(2):
+                tile_w = slot([P, PACK * WIDE], BF16, "woven0", woven0_tags[w])
+                nc.scalar.copy(
+                    out=tile_w[:].rearrange("p (c i t) -> p c t i", i=LINE, t=PACK),
+                    in_=side0[w][:].rearrange("p t (c i) -> p c t i", i=LINE),
                 )
-            dst = pairs[(b, c)][:].rearrange("p (u c e) -> p u c e", u=2, e=2)
-            src = pages[k][:, BANK * c : BANK * (c + 1)]
-            if k == LAST - 1 and tail_engine(c) == "vector":
-                copy_on(engine, dst[:, t // 2, :, :], src.unsqueeze(2).to_broadcast([P, BANK, 2]))
-            else:
-                copy_on(engine, dst[:, t // 2, :, t % 2], src)
+                woven.append(tile_w)
 
-        def weave(b, c, engine):
-            dense = work.tile([P, PACK * BANK], BF16, name="woven", tag="woven", bufs=CHUNKS, align_bytes=64)
-            copy_on(
-                engine,
-                dense[:].bitcast(F32).rearrange("p (c u) -> p c u", u=2),
-                pairs[(b, c)][:].bitcast(F32).rearrange("p (u c) -> p c u", u=2),
+        def quantise_pass0(w):
+            codes = slot([P, WIDE], U32, "codes0", "codes0_%d" % w)
+            nc.vector.quantize_mx(
+                out=codes[:].bitcast(FP8X4), scales=scales0[:, WIDE * w : WIDE * (w + 1)], in_=woven[w][:]
             )
-            woven[(b, c)] = dense
+            codes0.append(codes)
 
-        def quantise_page(b, c):
-            if c == 0:
-                page_codes[b] = slot([P, T2], U32, "page_codes", "page_codes%d" % b)
-            codes = page_codes[b][:, BANK * c : BANK * (c + 1)]
-            scales = keep.tile([P, BANK], U8, name="page_scales_%d_%d" % (b, c), align_bytes=64)
-            nc.vector.quantize_mx(out=codes.bitcast(FP8X4), scales=scales[:], in_=woven[(b, c)][:])
-            page_q[(b, c)] = (codes, scales)
-
-        tab2_scale_tile = []
-        tab2_passes = []
+        tab2 = []
         v2 = []
-        v2s = []
 
-        def load_worker_scales():
-            tab2s = slot([P, T3], U8, "tab2s", "tab2s")
-            nc.vector.memset(tab2s[:].bitcast(I32), 0)
-            load_scale_rows(nc.sync, tab2s, lambda rows: tab2_scales[:, rows, :], 4 * PASSES)
-            tab2_scale_tile.append(tab2s)
+        def load_workers(b):
+            table = slot([P, T3], U32, "tab2", "tab2_%d" % b)
+            nc.sync.dma_start(
+                out=table[:].bitcast(I32),
+                in_=tab2_words[b].rearrange("p n i -> p (n i)").bitcast(I32),
+            )
+            tab2.append(table)
 
-        def load_worker_words():
-            tab2 = slot([P, PASSES * T3], U32, "tab2", "tab2")
-            for b in range(PASSES):
-                table = tab2[:, T3 * b : T3 * (b + 1)]
-                nc.sync.dma_start(
-                    out=table.bitcast(I32),
-                    in_=tab2_words[b].rearrange("p n i -> p (n i)").bitcast(I32),
-                )
-                tab2_passes.append(table)
+        def gather_workers(b):
+            words = slot([P, S2], U32, "v2", woven0_tags[b])
+            nc.vector.tensor_copy(words[:], tab2[b][:].indirect(list2[:]))
+            v2.append(words)
 
-        def gather_workers():
-            for b in range(PASSES):
-                words = slot([P, S2], U32, "v2", "v2_%d" % b)
-                nc.vector.tensor_copy(words[:], tab2_passes[b].indirect(list2[:]))
-                v2.append(words)
-            scales = slot([P, S2], U8, "v2s", "v2s")
-            nc.vector.tensor_copy(scales[:], tab2_scale_tile[0][:].indirect(list2[:]))
-            v2s.append(scales)
+        first_plane()
+        load_weights(2)
+        load_weights(3)
+        load_page(2)
+        first_stage(1)
+        gather_plane_pass0(0)
+        load_page(3)
+        first_stage(2)
+        prepare_w1(1, "scalar")
+        scatter(1)
+        gather_plane_pass0(1)
+        load_page(4)
+        tab2s = slot([P, T3], U8, "tab2s", "tab2s")
+        nc.gpsimd.memset(tab2s[:].bitcast(I32), 0)
+        load_scale_rows(nc.sync, tab2s, lambda rows: tab2_scales[:, rows, :], 4 * PASSES)
+        first_stage(3)
+        scatter(2)
+        gather_plane_pass0(2)
+        load_page(5)
+        first_stage(4)
+        scatter(3)
+        gather_plane_pass0(3)
+        load_page(6)
+        load_workers(0)
+        first_stage(5)
+        scatter(4)
+        load_workers(1)
+        load_page(7)
+        v2s = slot([P, S2], U8, "v2s", "v2s")
+        nc.vector.tensor_copy(v2s[:], tab2s[:].indirect(list2[:]))
+        first_stage(6)
+        scatter(5)
+        weave_pass0()
+        quantise_pass0(0)
+        gather_workers(0)
+        scatter(6)
+        quantise_pass0(1)
+        gather_workers(1)
+        first_stage(LAST)
+        nc.scalar.activation(out=warm[:, 1:2], in_=last_tiles[LAST][:, 0:1], func=ACT.Sigmoid)
+
+        side1 = slot([P, 2, T2], F32, "side1", "side1")
+        for e in range(2):
+            nc.sync.dma_start(out=side1[:, e, :], in_=pages[PACK + e][:])
+        allowed = []
+        for i in range(2):
+            rows = slot([P, 2, PICK], F32, "allowed", "page%d" % (PACK + i))
+            nc.sync.dma_start(
+                out=rows[:], in_=permit[2 * P * i : 2 * P * (i + 1), :].rearrange("(n p) m -> p n m", p=P)
+            )
+            allowed.append(rows)
+
+        first_two = slot([P, 2 * PACK * BANK], BF16, "woven1", "B")
+        woven1 = [
+            first_two[:, 0 : PACK * BANK],
+            first_two[:, PACK * BANK : 2 * PACK * BANK],
+            slot([P, PACK * BANK], BF16, "woven1", "weighted")[:],
+            slot([P, PACK * BANK], BF16, "woven1", "plain")[:],
+        ]
+        early = ["scalar", "scalar", "gpsimd", "gpsimd"]
+        late = ["vector", "vector", "scalar", "scalar"]
+        views = [w.rearrange("p (c t) -> p c t", t=PACK) for w in woven1]
+        for c in range(CHUNKS):
+            round_on(early[c], views[c][:, :, 0:2], side1[:, :, chunks[c]].rearrange("p e c -> p c e"))
+        for c in range(CHUNKS):
+            round_on(
+                early[c], views[c][:, :, 2:4],
+                pages[LAST - 1][:, chunks[c]].unsqueeze(2).to_broadcast([P, BANK, 2]),
+            )
+        scatter(LAST)
 
         scores = {}
+        codes1 = []
 
         def score_pass(n, c, b):
             if b == 0:
                 scores[(n, c)] = bank(CHUNKS * (n % 2) + c, "score")
+                rhs, rhs_scale = codes0[c // 2][:, halves[c % 2]], scales0[:, chunks[c]]
+            else:
+                rhs, rhs_scale = codes1[c][0][:], codes1[c][1][:]
             cols = slice(P * n, P * (n + 1))
             nc.tensor.matmul_mx(
                 out=scores[(n, c)][:],
-                lhsT=v2[b][:, cols].bitcast(FP8X4), lhsT_scale=v2s[0][4 * b : P, cols],
-                rhs=page_q[(b, c)][0].bitcast(FP8X4), rhs_scale=page_q[(b, c)][1][:],
+                lhsT=v2[b][:, cols].bitcast(FP8X4), lhsT_scale=v2s[4 * b : P, cols],
+                rhs=rhs.bitcast(FP8X4), rhs_scale=rhs_scale,
                 start=(b == 0), stop=(b == PASSES - 1),
             )
-
-        round_w1(0)
-        quantise_w1_first()
-        load_page(1)
-        load_weights(1)
-        order_w4_scales(0, 0, 1)
-        gather_vacancies(0)
-        order_w4_scales(0, 1, PACK)
-        order_w4_scales(1, 0, PACK)
-        gather_vacancies(1)
-        load_w1(1)
-        first_stage(0)
-        load_page(2)
-        load_weights(2)
-        edit_first_plane()
-        first_stage(1)
-        load_weights(3)
-        load_worker_scales()
-        first_stage(2)
-        load_page(3)
-        load_page(4)
-        round_w1(1)
-        allowed = slot([P, ROW_TILES, PICK], F32, "allowed", "big")
-        make_h(1)
-
-        for k in range(1, PLANES):
-            if k < LAST:
-                make_h(k + 1)
-            if k == LATE_LOADS_STEP:
-                quantise_w1_second()
-            scatter(k)
-            if k == GATHER_WORKERS_STEP:
-                gather_workers()
-            if k == LATE_LOADS_STEP:
-                load_page(5)
-                load_page(6)
-                load_worker_words()
-                nc.sync.dma_start(out=allowed[:], in_=permit.rearrange("(n p) m -> p n m", p=P))
-            if k == PAGE7_STEP:
-                load_page(7)
-            if k + 2 <= LAST:
-                first_stage(k + 2)
-            if k + 2 == LAST:
-                nc.scalar.activation(out=warm[:, 1:2], in_=first_results[LAST][1][1][:, 0:1], func=ACT.Sigmoid)
-            for c in range(CHUNKS):
-                round_plane(k - 1, c, "scalar")
-            if k == PACK:
-                for c in range(CHUNKS):
-                    weave(0, c, "scalar")
-            if k == QUANTISE_PASS0_STEP:
-                for c in range(CHUNKS):
-                    quantise_page(0, c)
 
         for n in range(2):
             for c in range(CHUNKS):
                 score_pass(n, c, 0)
-        for c in CHUNK_ORDER:
-            round_plane(LAST, c, tail_engine(c))
-        for c in CHUNK_ORDER:
-            weave(1, c, tail_engine(c))
-        for c in CHUNK_ORDER:
-            quantise_page(1, c)
+        for c in range(CHUNKS):
+            round_on(late[c], views[c][:, :, 3], pages[LAST][:, chunks[c]])
+        for c in range(CHUNKS):
+            codes = slot([P, BANK], U32, "codes1", "wg%d" % c)
+            scales = keep.tile([P, BANK], U8, name="scales1_%d" % c, align_bytes=64)
+            nc.vector.quantize_mx(out=codes[:].bitcast(FP8X4), scales=scales[:], in_=woven1[c])
+            codes1.append((codes, scales))
             for n in range(2):
                 score_pass(n, c, 1)
 
+        x_tags = ["edit_a", "edit_b", "A", "gain"]
+
         def pick_scores(n):
             e = slot([P, T2], F32, "e", "page%d" % n)
-            for c in CHUNK_ORDER:
-                engine = "vector" if (n == 0 and c == CHUNK_ORDER[-1]) else "scalar"
-                copy_on(engine, e[:, BANK * c : BANK * (c + 1)], scores[(n, c)][:])
+            for c in range(CHUNKS):
+                engine = "vector" if (n, c) == (0, 2) else "scalar"
+                round_on(engine, e[:, chunks[c]], scores[(n, c)][:])
             if n + 2 < ROW_TILES:
-                for c in CHUNK_ORDER:
+                for c in range(CHUNKS):
                     for b in range(PASSES):
                         score_pass(n + 2, c, b)
-            x = work.tile([P, PICK], F32, name="x", tag="pairs", bufs=CHUNKS, align_bytes=64)
+            x = slot([P, PICK], F32, "x", x_tags[n])
             parts = LAST_PARTS if n == ROW_TILES - 1 else [slice(0, PICK)]
             for cols in parts:
                 nc.vector.tensor_copy(x[:, cols], e[:].indirect(entries(list4, cols)))
@@ -448,7 +432,7 @@ def tile_list_farm_job_board_kernel(
             engine = nc.gpsimd if n < GPSIMD_ROW_TILES else nc.vector
             for cols in parts:
                 nc.scalar.activation(out=x[:, cols], in_=x[:, cols], func=ACT.Sigmoid)
-                engine.tensor_tensor(out=x[:, cols], in0=x[:, cols], in1=allowed[:, n, cols], op=MULT)
+                engine.tensor_tensor(out=x[:, cols], in0=x[:, cols], in1=allowed[n // 2][:, n % 2, cols], op=MULT)
                 nc.sync.dma_start(out=out[P * n : P * (n + 1), cols], in_=x[:, cols])
 
         picked = []

@@ -31,11 +31,11 @@ WIDE = T2 // 2
 LINE = 4
 QUADRANTS = (0, 2, 1, 3)
 LAST_PARTS = [slice(0, 768), slice(768, 1024)]
-GPSIMD_ROW_TILES = 2
 GAIN_SLOTS = ["page2", "page3", "page4", "page5", "gain", "page7", "gain", "gain"]
 PLAIN_SLOTS = [None, "plain", "tab2s", "plain", "tab2_0", "tab2_1", "side1", "plain"]
-EDIT_SLOTS = ["edit_a", "edit_b", "edit_a", "page6", "v2s", "codes0_0", "codes0_1", "edit_b"]
+EDIT_SLOTS = ["edit_a", "edit_b", "edit_c", "page6", "v2s", "codes0_0", "codes0_1", "edit_b"]
 SPLIT_SCATTERS = 2
+END = 768
 FIRST_PARTS = [slice(0, 256), slice(256, 512), slice(512, 1024)]
 
 
@@ -83,8 +83,8 @@ def tile_list_farm_job_board_kernel(
 
         tabs = slot([P, T], U8, "tabs", "w4s")
         w4s_raw = slot([P, H], U8, "w4s_raw", "w1_late")
-        w4_raw = slot([P, 2 * H], U8, "w4_raw", "wg0")
-        seed = slot([P, 1], F32, "seed", "page1")
+        w4_raw = slot([P, 2 * H], U8, "w4_raw", "page0")
+        seed = slot([P, 1], F32, "seed", "A")
         one = keep.tile([P, 1], F32, name="one")
         warm = keep.tile([P, 2], F32, name="warm")
         nc.vector.memset(tabs[:].bitcast(I32), 0)
@@ -96,7 +96,7 @@ def tile_list_farm_job_board_kernel(
         w1_raw = []
 
         def load_w1(b):
-            raw = slot([P, PACK, PASS], F32, "w1_raw", "page0" if b == 0 else "w1_late")
+            raw = slot([P, PACK, PASS], F32, "w1_raw", "wg0" if b == 0 else "w1_late")
             nc.sync.dma_start(
                 out=raw[:],
                 in_=w1[:, PASS * b : PASS * (b + 1)].rearrange("(p j) c -> p j c", j=PACK),
@@ -128,7 +128,7 @@ def tile_list_farm_job_board_kernel(
         nc.sync.dma_start(out=w4_raw[:].bitcast(I32), in_=w4_words[0].bitcast(I32))
         load_w1(0)
         load_scale_rows(nc.sync, tabs, lambda rows: tab_scales[0, rows, :], 4)
-        tab = slot([P, T], U32, "tab", "page1")
+        tab = slot([P, T], U32, "tab", "A")
         nc.sync.dma_start(
             out=tab[:].bitcast(I32),
             in_=tab_words[0].rearrange("p n i -> p (n i)").bitcast(I32),
@@ -141,7 +141,7 @@ def tile_list_farm_job_board_kernel(
                 out=w4[:, 2 * PASS * b : 2 * PASS * (b + 1)].rearrange("p (t m e) -> p m t e", t=PACK, e=2),
                 in_=w4_raw[:, 2 * PASS * b : 2 * PASS * (b + 1)].rearrange("p (m t e) -> p m t e", t=PACK, e=2),
             )
-        load_weights(0)
+        load_page(0)
 
         w1_codes = keep.tile([P, H], U32, name="w1_codes", align_bytes=64)
         w1_scales = keep.tile([P, H], U8, name="w1_scales", align_bytes=64)
@@ -159,7 +159,7 @@ def tile_list_farm_job_board_kernel(
             )
 
         prepare_w1(0, "scalar")
-        load_page(0)
+        load_weights(0)
         load_weights(1)
         vs = keep.tile([P, S], U8, name="vs", align_bytes=64)
         nc.vector.tensor_copy(vs[:], tabs[:].indirect(list1[:]))
@@ -176,7 +176,6 @@ def tile_list_farm_job_board_kernel(
             words = keep.tile([P, BANK], U32, name="v%d" % half, align_bytes=64)
             nc.vector.tensor_copy(words[:], tab[:].indirect(entries(list1, halves[half])))
             v.append(words)
-        load_page(1)
 
         woven0_tags = ["W0a", "W0b"]
         made = {}
@@ -216,7 +215,7 @@ def tile_list_farm_job_board_kernel(
         def first_plane():
             gain = slot([P, S], F32, "gain", GAIN_SLOTS[0])
             edit = slot([P, S], F32, "edit", EDIT_SLOTS[0])
-            root_tags = ["root0", "wg2", "wg3"]
+            root_tags = ["page1", "wg2", "wg3"]
             for i, cols in enumerate(FIRST_PARTS):
                 acc_b, acc_a = products(0, cols, 2 * i, 2 * i + 1)
                 root = slot([P, cols.stop - cols.start], F32, "root", root_tags[i])[:]
@@ -236,7 +235,7 @@ def tile_list_farm_job_board_kernel(
             if k == LAST - 1:
                 root_tags = woven0_tags
             if k == LAST:
-                root_tags = ["B", "root1"]
+                root_tags = ["root0", "B"]
             roots = [slot([P, BANK], F32, "root", root_tags[half])[:] for half in range(HALVES)]
             gain = slot([P, S], F32, "gain", GAIN_SLOTS[k])
             plain = slot([P, S], F32, "plain", PLAIN_SLOTS[k])
@@ -247,17 +246,25 @@ def tile_list_farm_job_board_kernel(
             nc.scalar.copy(out=plain[:, halves[0]], in_=accs[0][1])
             damp(gain[:, halves[0]], roots[0])
             invert(roots[1])
-            nc.scalar.copy(out=plain[:, halves[1]], in_=accs[1][1])
+            if k == LAST:
+                end_plain = slot([P, S - END], F32, "end_plain", "end_plain")
+                nc.scalar.copy(out=plain[:, BANK:END], in_=accs[1][1][:, 0 : END - BANK])
+                nc.scalar.copy(out=end_plain[:], in_=accs[1][1][:, END - BANK : BANK])
+            else:
+                nc.scalar.copy(out=plain[:, halves[1]], in_=accs[1][1])
             damp(gain[:, halves[1]], roots[1])
             parts = [slice(0, S)]
-            if k < SPLIT_SCATTERS:
+            if k < SPLIT_SCATTERS or k == LAST:
                 parts = halves
-            if k == LAST:
-                parts = halves[::-1]
             for h in parts:
                 weighted = slot([P, h.stop - h.start], F32, "weighted", "weighted")
                 nc.gpsimd.tensor_tensor(out=weighted[:], in0=gain[:, h], in1=wg[t][:, h], op=MULT)
-                nc.gpsimd.tensor_tensor(out=edit[:, h], in0=plain[:, h], in1=weighted[:], op=MULT)
+                if k == LAST and h.stop == S:
+                    last_tiles["end"] = (end_plain, weighted)
+                    h = slice(h.start, END)
+                nc.gpsimd.tensor_tensor(
+                    out=edit[:, h], in0=plain[:, h], in1=weighted[:, 0 : h.stop - h.start], op=MULT
+                )
             made[k] = edit
             last_tiles[k] = gain
 
@@ -306,11 +313,12 @@ def tile_list_farm_job_board_kernel(
             tab2.append(table)
 
         def gather_workers(b):
-            words = slot([P, S2], U32, "v2", woven0_tags[b])
+            words = slot([P, S2], U32, "v2", woven0_tags[1] if b == 0 else "tab2_0")
             nc.vector.tensor_copy(words[:], tab2[b][:].indirect(list2[:]))
             v2.append(words)
 
         first_plane()
+        load_page(1)
         load_weights(2)
         load_weights(3)
         load_page(2)
@@ -344,12 +352,12 @@ def tile_list_farm_job_board_kernel(
         scatter(5)
         weave_pass0()
         quantise_pass0(0)
-        gather_workers(0)
         scatter(6)
         quantise_pass0(1)
+        gather_workers(0)
         gather_workers(1)
         first_stage(LAST)
-        nc.scalar.activation(out=warm[:, 1:2], in_=last_tiles[LAST][:, 0:1], func=ACT.Sigmoid)
+        nc.scalar.activation(out=warm[:, 1:2], in_=last_tiles[LAST][:, S - 1 : S], func=ACT.Sigmoid)
 
         side1 = slot([P, 2, T2], F32, "side1", "side1")
         for e in range(2):
@@ -366,8 +374,8 @@ def tile_list_farm_job_board_kernel(
         woven1 = [
             first_two[:, 0 : PACK * BANK],
             first_two[:, PACK * BANK : 2 * PACK * BANK],
-            slot([P, PACK * BANK], BF16, "woven1", "weighted")[:],
             slot([P, PACK * BANK], BF16, "woven1", "plain")[:],
+            slot([P, PACK * BANK], BF16, "woven1", "gain")[:],
         ]
         early = ["scalar", "scalar", "gpsimd", "gpsimd"]
         late = ["vector", "vector", "scalar", "scalar"]
@@ -376,10 +384,14 @@ def tile_list_farm_job_board_kernel(
             round_on(early[c], views[c][:, :, 0:2], side1[:, :, chunks[c]].rearrange("p e c -> p c e"))
         for c in range(CHUNKS):
             round_on(
-                early[c], views[c][:, :, 2:4],
+                "scalar" if c < CHUNKS - 1 else "gpsimd", views[c][:, :, 2:4],
                 pages[LAST - 1][:, chunks[c]].unsqueeze(2).to_broadcast([P, BANK, 2]),
             )
-        scatter(LAST)
+        put(LAST, made[LAST], slice(0, END))
+        end_plain, end_weighted = last_tiles["end"]
+        end_edit = slot([P, S - END], F32, "end_edit", "page6")
+        nc.gpsimd.tensor_tensor(out=end_edit[:], in0=end_plain[:], in1=end_weighted[:, END - BANK : BANK], op=MULT)
+        nc.vector.tensor_copy(pages[LAST][:].indirect(entries(list3, slice(END, S))), end_edit[:])
 
         scores = {}
         codes1 = []
@@ -412,33 +424,38 @@ def tile_list_farm_job_board_kernel(
                 score_pass(n, c, 1)
 
         x_tags = ["edit_a", "edit_b", "A", "gain"]
+        e_tags = ["page7", "page0", "page1", "page2"]
+        vector_banks = [(0, 2), (2, 3), (3, 3)]
+        picked = []
 
-        def pick_scores(n):
-            e = slot([P, T2], F32, "e", "page%d" % n)
+        def pick_scores(n, parts):
+            e = slot([P, T2], F32, "e", e_tags[n])
             for c in range(CHUNKS):
-                engine = "vector" if (n, c) == (0, 2) else "scalar"
+                engine = "vector" if (n, c) in vector_banks else "scalar"
                 round_on(engine, e[:, chunks[c]], scores[(n, c)][:])
             if n + 2 < ROW_TILES:
                 for c in range(CHUNKS):
                     for b in range(PASSES):
                         score_pass(n + 2, c, b)
             x = slot([P, PICK], F32, "x", x_tags[n])
-            parts = LAST_PARTS if n == ROW_TILES - 1 else [slice(0, PICK)]
             for cols in parts:
                 nc.vector.tensor_copy(x[:, cols], e[:].indirect(entries(list4, cols)))
-            return x, parts
+            picked.append(x)
 
-        def weigh_and_store(n, x, parts):
-            engine = nc.gpsimd if n < GPSIMD_ROW_TILES else nc.vector
-            for cols in parts:
-                nc.scalar.activation(out=x[:, cols], in_=x[:, cols], func=ACT.Sigmoid)
-                engine.tensor_tensor(out=x[:, cols], in0=x[:, cols], in1=allowed[n // 2][:, n % 2, cols], op=MULT)
-                nc.sync.dma_start(out=out[P * n : P * (n + 1), cols], in_=x[:, cols])
+        def weigh_and_store(n, cols, engine):
+            x = picked[n]
+            nc.scalar.activation(out=x[:, cols], in_=x[:, cols], func=ACT.Sigmoid)
+            engine.tensor_tensor(out=x[:, cols], in0=x[:, cols], in1=allowed[n // 2][:, n % 2, cols], op=MULT)
+            nc.sync.dma_start(out=out[P * n : P * (n + 1), cols], in_=x[:, cols])
 
-        picked = []
-        for n in range(ROW_TILES):
-            picked.append(pick_scores(n))
-            if n == ROW_TILES - 2:
-                weigh_and_store(0, picked[0][0], picked[0][1])
-        for n in range(1, ROW_TILES):
-            weigh_and_store(n, picked[n][0], picked[n][1])
+        whole = slice(0, PICK)
+        pick_scores(0, [whole])
+        pick_scores(1, [whole])
+        weigh_and_store(0, whole, nc.gpsimd)
+        pick_scores(2, [whole])
+        weigh_and_store(1, whole, nc.gpsimd)
+        pick_scores(3, LAST_PARTS)
+        weigh_and_store(2, halves[0], nc.gpsimd)
+        weigh_and_store(2, halves[1], nc.vector)
+        for cols in LAST_PARTS:
+            weigh_and_store(3, cols, nc.vector)

@@ -31,11 +31,12 @@ WIDE = T2 // 2
 LINE = 4
 QUADRANTS = (0, 2, 1, 3)
 LAST_PARTS = [slice(0, 768), slice(768, 1024)]
-GAIN_SLOTS = ["page2", "page3", "page4", "page5", "gain", "page7", "gain", "gain"]
-PLAIN_SLOTS = [None, "plain", "tab2s", "plain", "tab2_0", "tab2_1", "side1", "plain"]
-EDIT_SLOTS = ["edit_a", "edit_b", "edit_c", "page6", "v2s", "codes0_0", "codes0_1", "edit_b"]
+GAIN_SLOTS = ["page2", "page3", "page4", "W0b", "gain", "page7", "gain", "gain"]
+PLAIN_SLOTS = [None, "plain", "plain_b", "plain", "tab2_0", "tab2_1", "plain_b", "plain"]
+EDIT_SLOTS = ["edit_a", "edit_b", "page5", "page6", "edit_d", "codes0_0", "codes0_1", "root0"]
 SPLIT_SCATTERS = 2
 END = 768
+PLACED = {"tab": 0, "v2s": 0, "A": S2}
 FIRST_PARTS = [slice(0, 256), slice(256, 512), slice(512, 1024)]
 
 
@@ -47,12 +48,15 @@ def tile_list_farm_job_board_kernel(
     with ExitStack() as ctx:
         keep = ctx.enter_context(tc.tile_pool(name="keep", bufs=1))
         work = ctx.enter_context(tc.tile_pool(name="work", bufs=1))
+        placed = ctx.enter_context(tc.tile_pool(name="placed", bufs=1))
         psum = ctx.enter_context(tc.psum_pool(name="psum", bufs=1))
 
         def bank(i, name):
             return psum.tile([P, BANK], F32, name=name, tag="bank%d" % i)
 
         def slot(shape, dtype, name, tag):
+            if tag in PLACED:
+                return placed.tile(shape, dtype, name=name, tag=tag, align_bytes=64, offset=PLACED[tag])
             return work.tile(shape, dtype, name=name, tag=tag, align_bytes=64)
 
         def entries(offsets, cols):
@@ -82,9 +86,9 @@ def tile_list_farm_job_board_kernel(
         list4 = keep.tile([P, PICK // 16], U16, name="list4")
 
         tabs = slot([P, T], U8, "tabs", "w4s")
-        w4s_raw = slot([P, H], U8, "w4s_raw", "w1_late")
-        w4_raw = slot([P, 2 * H], U8, "w4_raw", "page0")
-        seed = slot([P, 1], F32, "seed", "A")
+        w4s_raw = slot([P, H], U8, "w4s_raw", "wg1")
+        w4_raw = slot([P, 2 * H], U8, "w4_raw", "tab2s")
+        seed = slot([P, 1], F32, "seed", "tab")
         one = keep.tile([P, 1], F32, name="one")
         warm = keep.tile([P, 2], F32, name="warm")
         nc.vector.memset(tabs[:].bitcast(I32), 0)
@@ -96,7 +100,7 @@ def tile_list_farm_job_board_kernel(
         w1_raw = []
 
         def load_w1(b):
-            raw = slot([P, PACK, PASS], F32, "w1_raw", "wg0" if b == 0 else "w1_late")
+            raw = slot([P, PACK, PASS], F32, "w1_raw", "page0" if b == 0 else "A")
             nc.sync.dma_start(
                 out=raw[:],
                 in_=w1[:, PASS * b : PASS * (b + 1)].rearrange("(p j) c -> p j c", j=PACK),
@@ -128,7 +132,7 @@ def tile_list_farm_job_board_kernel(
         nc.sync.dma_start(out=w4_raw[:].bitcast(I32), in_=w4_words[0].bitcast(I32))
         load_w1(0)
         load_scale_rows(nc.sync, tabs, lambda rows: tab_scales[0, rows, :], 4)
-        tab = slot([P, T], U32, "tab", "A")
+        tab = slot([P, T], U32, "tab", "tab")
         nc.sync.dma_start(
             out=tab[:].bitcast(I32),
             in_=tab_words[0].rearrange("p n i -> p (n i)").bitcast(I32),
@@ -138,16 +142,17 @@ def tile_list_farm_job_board_kernel(
         w4 = keep.tile([P, 2 * H], U8, name="w4", align_bytes=64)
         for b in range(PASSES):
             nc.vector.tensor_copy(
-                out=w4[:, 2 * PASS * b : 2 * PASS * (b + 1)].rearrange("p (t m e) -> p m t e", t=PACK, e=2),
-                in_=w4_raw[:, 2 * PASS * b : 2 * PASS * (b + 1)].rearrange("p (m t e) -> p m t e", t=PACK, e=2),
+                out=w4[:].bitcast(U16)[:, PASS * b : PASS * (b + 1)].rearrange("p (t m) -> p m t", t=PACK),
+                in_=w4_raw[:].bitcast(U16)[:, PASS * b : PASS * (b + 1)].rearrange("p (m t) -> p m t", t=PACK),
             )
-        load_page(0)
+        tab2s = slot([P, T3], U8, "tab2s", "tab2s")
+        nc.vector.memset(tab2s[:].bitcast(I32), 0)
 
         w1_codes = keep.tile([P, H], U32, name="w1_codes", align_bytes=64)
         w1_scales = keep.tile([P, H], U8, name="w1_scales", align_bytes=64)
 
         def prepare_w1(b, engine):
-            rounded = slot([P, PACK * PASS], BF16, "w1_rounded", "wg1" if b == 0 else "codes0_0")
+            rounded = slot([P, PACK * PASS], BF16, "w1_rounded", "wg0" if b == 0 else "B")
             round_on(
                 engine,
                 rounded[:].rearrange("p (t m j) -> p m j t", t=PACK, j=PACK),
@@ -159,8 +164,9 @@ def tile_list_farm_job_board_kernel(
             )
 
         prepare_w1(0, "scalar")
+        load_page(0)
+        load_scale_rows(nc.scalar, tab2s, lambda rows: tab2_scales[:, rows, :], 4 * PASSES)
         load_weights(0)
-        load_weights(1)
         vs = keep.tile([P, S], U8, name="vs", align_bytes=64)
         nc.vector.tensor_copy(vs[:], tabs[:].indirect(list1[:]))
         w4s = slot([P, H], U8, "w4s", "w4s")
@@ -169,13 +175,16 @@ def tile_list_farm_job_board_kernel(
                 out=w4s[:, PASS * b : PASS * (b + 1)].rearrange("p (t m) -> p m t", t=PACK),
                 in_=w4s_raw[:, PASS * b : PASS * (b + 1)].rearrange("p (m t) -> p m t", t=PACK),
             )
-        load_w1(1)
+        load_weights(1)
 
         v = []
         for half in range(HALVES):
             words = keep.tile([P, BANK], U32, name="v%d" % half, align_bytes=64)
             nc.vector.tensor_copy(words[:], tab[:].indirect(entries(list1, halves[half])))
             v.append(words)
+        load_w1(1)
+        v2s = slot([P, S2], U8, "v2s", "v2s")
+        nc.vector.tensor_copy(v2s[:], tab2s[:].indirect(list2[:]))
 
         woven0_tags = ["W0a", "W0b"]
         made = {}
@@ -239,7 +248,7 @@ def tile_list_farm_job_board_kernel(
             roots = [slot([P, BANK], F32, "root", root_tags[half])[:] for half in range(HALVES)]
             gain = slot([P, S], F32, "gain", GAIN_SLOTS[k])
             plain = slot([P, S], F32, "plain", PLAIN_SLOTS[k])
-            edit = slot([P, S], F32, "edit", EDIT_SLOTS[k])
+            edit = slot([P, S if k < LAST else END], F32, "edit", EDIT_SLOTS[k])
             size(roots[0], accs[0][0])
             size(roots[1], accs[1][0])
             invert(roots[0])
@@ -247,14 +256,14 @@ def tile_list_farm_job_board_kernel(
             damp(gain[:, halves[0]], roots[0])
             invert(roots[1])
             if k == LAST:
-                end_plain = slot([P, S - END], F32, "end_plain", "end_plain")
+                end_plain = slot([P, S - END], F32, "end_plain", "root1")
                 nc.scalar.copy(out=plain[:, BANK:END], in_=accs[1][1][:, 0 : END - BANK])
                 nc.scalar.copy(out=end_plain[:], in_=accs[1][1][:, END - BANK : BANK])
             else:
                 nc.scalar.copy(out=plain[:, halves[1]], in_=accs[1][1])
             damp(gain[:, halves[1]], roots[1])
             parts = [slice(0, S)]
-            if k < SPLIT_SCATTERS or k == LAST:
+            if k < PACK or k == LAST:
                 parts = halves
             for h in parts:
                 weighted = slot([P, h.stop - h.start], F32, "weighted", "weighted")
@@ -323,16 +332,13 @@ def tile_list_farm_job_board_kernel(
         load_weights(3)
         load_page(2)
         first_stage(1)
-        gather_plane_pass0(0)
         load_page(3)
         first_stage(2)
         prepare_w1(1, "scalar")
+        gather_plane_pass0(0)
         scatter(1)
         gather_plane_pass0(1)
         load_page(4)
-        tab2s = slot([P, T3], U8, "tab2s", "tab2s")
-        nc.gpsimd.memset(tab2s[:].bitcast(I32), 0)
-        load_scale_rows(nc.sync, tab2s, lambda rows: tab2_scales[:, rows, :], 4 * PASSES)
         first_stage(3)
         scatter(2)
         gather_plane_pass0(2)
@@ -346,10 +352,11 @@ def tile_list_farm_job_board_kernel(
         scatter(4)
         load_workers(1)
         load_page(7)
-        v2s = slot([P, S2], U8, "v2s", "v2s")
-        nc.vector.tensor_copy(v2s[:], tab2s[:].indirect(list2[:]))
+        side1 = slot([P, 2, T2], F32, "side1", "side1")
+        nc.sync.dma_start(out=side1[:, 0, :], in_=pages[PACK][:])
         first_stage(6)
         scatter(5)
+        nc.sync.dma_start(out=side1[:, 1, :], in_=pages[PACK + 1][:])
         weave_pass0()
         quantise_pass0(0)
         scatter(6)
@@ -359,9 +366,6 @@ def tile_list_farm_job_board_kernel(
         first_stage(LAST)
         nc.scalar.activation(out=warm[:, 1:2], in_=last_tiles[LAST][:, S - 1 : S], func=ACT.Sigmoid)
 
-        side1 = slot([P, 2, T2], F32, "side1", "side1")
-        for e in range(2):
-            nc.sync.dma_start(out=side1[:, e, :], in_=pages[PACK + e][:])
         allowed = []
         for i in range(2):
             rows = slot([P, 2, PICK], F32, "allowed", "page%d" % (PACK + i))
@@ -384,7 +388,7 @@ def tile_list_farm_job_board_kernel(
             round_on(early[c], views[c][:, :, 0:2], side1[:, :, chunks[c]].rearrange("p e c -> p c e"))
         for c in range(CHUNKS):
             round_on(
-                "scalar" if c < CHUNKS - 1 else "gpsimd", views[c][:, :, 2:4],
+                "scalar", views[c][:, :, 2:4],
                 pages[LAST - 1][:, chunks[c]].unsqueeze(2).to_broadcast([P, BANK, 2]),
             )
         put(LAST, made[LAST], slice(0, END))
@@ -423,12 +427,14 @@ def tile_list_farm_job_board_kernel(
             for n in range(2):
                 score_pass(n, c, 1)
 
-        x_tags = ["edit_a", "edit_b", "A", "gain"]
         e_tags = ["page7", "page0", "page1", "page2"]
         vector_banks = [(0, 2), (2, 3), (3, 3)]
-        picked = []
+        whole = slice(0, PICK)
+        pick_parts = [[whole], [whole], halves, LAST_PARTS]
+        pick_tags = [["edit_a"], ["edit_b"], ["A", "end_pick"], ["gain", "end_pick"]]
+        picked = {}
 
-        def pick_scores(n, parts):
+        def fetch_scores(n):
             e = slot([P, T2], F32, "e", e_tags[n])
             for c in range(CHUNKS):
                 engine = "vector" if (n, c) in vector_banks else "scalar"
@@ -437,25 +443,43 @@ def tile_list_farm_job_board_kernel(
                 for c in range(CHUNKS):
                     for b in range(PASSES):
                         score_pass(n + 2, c, b)
-            x = slot([P, PICK], F32, "x", x_tags[n])
-            for cols in parts:
-                nc.vector.tensor_copy(x[:, cols], e[:].indirect(entries(list4, cols)))
-            picked.append(x)
+            return e
 
-        def weigh_and_store(n, cols, engine):
-            x = picked[n]
-            nc.scalar.activation(out=x[:, cols], in_=x[:, cols], func=ACT.Sigmoid)
-            engine.tensor_tensor(out=x[:, cols], in0=x[:, cols], in1=allowed[n // 2][:, n % 2, cols], op=MULT)
-            nc.sync.dma_start(out=out[P * n : P * (n + 1), cols], in_=x[:, cols])
+        def pick(n, i, e):
+            cols = pick_parts[n][i]
+            x = slot([P, cols.stop - cols.start], F32, "x", pick_tags[n][i])
+            nc.vector.tensor_copy(x[:], e[:].indirect(entries(list4, cols)))
+            picked[(n, i)] = x
 
-        whole = slice(0, PICK)
-        pick_scores(0, [whole])
-        pick_scores(1, [whole])
-        weigh_and_store(0, whole, nc.gpsimd)
-        pick_scores(2, [whole])
-        weigh_and_store(1, whole, nc.gpsimd)
-        pick_scores(3, LAST_PARTS)
-        weigh_and_store(2, halves[0], nc.gpsimd)
-        weigh_and_store(2, halves[1], nc.vector)
-        for cols in LAST_PARTS:
-            weigh_and_store(3, cols, nc.vector)
+        def squash(n, i, tag=None):
+            x = picked[(n, i)]
+            y = x if tag is None else slot(list(x.shape), F32, "y", tag)
+            nc.scalar.activation(out=y[:], in_=x[:], func=ACT.Sigmoid)
+            picked[(n, i)] = y
+
+        def weigh_and_store(n, i, engine):
+            cols = pick_parts[n][i]
+            y = picked[(n, i)]
+            engine.tensor_tensor(out=y[:], in0=y[:], in1=allowed[n // 2][:, n % 2, cols], op=MULT)
+            nc.sync.dma_start(out=out[P * n : P * (n + 1), cols], in_=y[:])
+
+        pick(0, 0, fetch_scores(0))
+        pick(1, 0, fetch_scores(1))
+        squash(0, 0)
+        weigh_and_store(0, 0, nc.gpsimd)
+        e = fetch_scores(2)
+        pick(2, 0, e)
+        pick(2, 1, e)
+        squash(1, 0)
+        weigh_and_store(1, 0, nc.gpsimd)
+        e = fetch_scores(3)
+        pick(3, 0, e)
+        squash(2, 0)
+        squash(2, 1, "weighted")
+        weigh_and_store(2, 0, nc.gpsimd)
+        pick(3, 1, e)
+        squash(3, 0)
+        weigh_and_store(2, 1, nc.vector)
+        squash(3, 1)
+        weigh_and_store(3, 0, nc.vector)
+        weigh_and_store(3, 1, nc.vector)

@@ -357,13 +357,13 @@ def tile_list_farm_job_board_kernel(
         first_stage(6)
         scatter(5)
         nc.sync.dma_start(out=side1[:, 1, :], in_=pages[PACK + 1][:])
+        first_stage(LAST)
         weave_pass0()
         quantise_pass0(0)
         scatter(6)
         quantise_pass0(1)
         gather_workers(0)
         gather_workers(1)
-        first_stage(LAST)
         nc.scalar.activation(out=warm[:, 1:2], in_=last_tiles[LAST][:, S - 1 : S], func=ACT.Sigmoid)
 
         allowed = []
@@ -374,18 +374,12 @@ def tile_list_farm_job_board_kernel(
             )
             allowed.append(rows)
 
-        first_two = slot([P, 2 * PACK * BANK], BF16, "woven1", "B")
-        woven1 = [
-            first_two[:, 0 : PACK * BANK],
-            first_two[:, PACK * BANK : 2 * PACK * BANK],
-            slot([P, PACK * BANK], BF16, "woven1", "plain")[:],
-            slot([P, PACK * BANK], BF16, "woven1", "gain")[:],
-        ]
-        early = ["scalar", "scalar", "gpsimd", "gpsimd"]
+        woven_all = slot([P, PACK * T2], BF16, "woven1", "B")
+        woven1 = [woven_all[:, PACK * BANK * c : PACK * BANK * (c + 1)] for c in range(CHUNKS)]
         late = ["vector", "vector", "scalar", "scalar"]
         views = [w.rearrange("p (c t) -> p c t", t=PACK) for w in woven1]
         for c in range(CHUNKS):
-            round_on(early[c], views[c][:, :, 0:2], side1[:, :, chunks[c]].rearrange("p e c -> p c e"))
+            round_on("scalar", views[c][:, :, 0:2], side1[:, :, chunks[c]].rearrange("p e c -> p c e"))
         for c in range(CHUNKS):
             round_on(
                 "scalar", views[c][:, :, 2:4],

@@ -262,12 +262,13 @@ def tile_list_farm_job_board_kernel(
             else:
                 nc.scalar.copy(out=plain[:, halves[1]], in_=accs[1][1])
             damp(gain[:, halves[1]], roots[1])
-            parts = [slice(0, S)]
-            if k < PACK or k == LAST:
-                parts = halves
-            for h in parts:
-                weighted = slot([P, h.stop - h.start], F32, "weighted", "weighted")
+            products_of = []
+            for half, h in enumerate(halves):
+                weighted = slot([P, BANK], F32, "weighted", "weighted%d" % half)
                 nc.gpsimd.tensor_tensor(out=weighted[:], in0=gain[:, h], in1=wg[t][:, h], op=MULT)
+                products_of.append(weighted)
+            for half, h in enumerate(halves):
+                weighted = products_of[half]
                 if k == LAST and h.stop == S:
                     last_tiles["end"] = (end_plain, weighted)
                     h = slice(h.start, END)
@@ -469,7 +470,7 @@ def tile_list_farm_job_board_kernel(
         e = fetch_scores(3)
         pick(3, 0, e)
         squash(2, 0)
-        squash(2, 1, "weighted")
+        squash(2, 1, "weighted0")
         weigh_and_store(2, 0, nc.gpsimd)
         pick(3, 1, e)
         squash(3, 0)

@@ -30,14 +30,33 @@ LAST = PLANES - 1
 WIDE = T2 // 2
 LINE = 4
 QUADRANTS = (0, 2, 1, 3)
-LAST_PARTS = [slice(0, 768), slice(768, 1024)]
-GAIN_SLOTS = ["page2", "page3", "page4", "W0b", "gain", "page7", "gain", "gain"]
-PLAIN_SLOTS = [None, "plain", "plain_b", "plain", "tab2_0", "tab2_1", "plain_b", "plain"]
-EDIT_SLOTS = ["edit_a", "edit_b", "page5", "page6", "edit_d", "codes0_0", "codes0_1", "root0"]
-SPLIT_SCATTERS = 2
 END = 768
-PLACED = {"tab": 0, "v2s": 0, "A": S2}
-FIRST_PARTS = [slice(0, 256), slice(256, 512), slice(512, 1024)]
+SPLIT_SCATTERS = 2
+
+PAGE_AT = [14, 29, 6, 49, 57, 65, 41, 73]
+WG_AT = [None, 25, 37, 2]
+WG0_AT = [0, 23]
+W1_RAW_AT = [2, 41]
+W1_ROUNDED_AT = [55, 79]
+GAIN_AT = [65, 79, 155, 159, 155, 159, 115, 123]
+EDIT_AT = [69, 163, 167, 171, 175, 163, 167, 179]
+WEIGHTED_AT = [187, 189]
+SIDE0_AT = [83, 99]
+WOVEN0_AT = [115, 123]
+CODES0_AT = [14, 18]
+SIDE1_AT = [131, 137, 143, 149]
+WOVEN1_AT = [83, 87, 91, 95]
+CODES1_AT = [99, 101, 103, 105]
+SCALES1_AT = [107, 107.5, 108, 108.5]
+TAB2_AT = [29, 6]
+WORKERS_AT = [[179, 180], [95, 96]]
+PERMIT_AT = [65, 57]
+SCORES_AT = [115, 123, 49, 41]
+PICKED_AT = [[163], [167], [171], [175, 178]]
+AT = {
+    "w4_raw": 1, "tabs": 21.5, "w4s": 22, "tab": 29, "tab2s": 81, "end_edit": 148.5,
+    "v2s": 181, "end_plain": 182, "w4s_raw": 184, "scales0": 185,
+}
 
 
 def tile_list_farm_job_board_kernel(
@@ -47,17 +66,15 @@ def tile_list_farm_job_board_kernel(
     nc = tc.nc
     with ExitStack() as ctx:
         keep = ctx.enter_context(tc.tile_pool(name="keep", bufs=1))
-        work = ctx.enter_context(tc.tile_pool(name="work", bufs=1))
         placed = ctx.enter_context(tc.tile_pool(name="placed", bufs=1))
         psum = ctx.enter_context(tc.psum_pool(name="psum", bufs=1))
 
         def bank(i, name):
             return psum.tile([P, BANK], F32, name=name, tag="bank%d" % i)
 
-        def slot(shape, dtype, name, tag):
-            if tag in PLACED:
-                return placed.tile(shape, dtype, name=name, tag=tag, align_bytes=64, offset=PLACED[tag])
-            return work.tile(shape, dtype, name=name, tag=tag, align_bytes=64)
+        def place(shape, dtype, name, kib=None):
+            start = AT[name] if kib is None else kib
+            return placed.tile(shape, dtype, name=name, tag=name, align_bytes=64, offset=int(1024 * start))
 
         def entries(offsets, cols):
             return offsets[:, cols.start // 16 : cols.stop // 16]
@@ -84,313 +101,303 @@ def tile_list_farm_job_board_kernel(
         list2 = keep.tile([P, S2 // 16], U16, name="list2")
         list3 = keep.tile([P, S // 16], U16, name="list3")
         list4 = keep.tile([P, PICK // 16], U16, name="list4")
-
-        tabs = slot([P, T], U8, "tabs", "w4s")
-        w4s_raw = slot([P, H], U8, "w4s_raw", "wg1")
-        w4_raw = slot([P, 2 * H], U8, "w4_raw", "tab2s")
-        seed = slot([P, 1], F32, "seed", "tab")
         one = keep.tile([P, 1], F32, name="one")
         warm = keep.tile([P, 2], F32, name="warm")
-        nc.vector.memset(tabs[:].bitcast(I32), 0)
-        nc.vector.memset(seed[:], 1.0)
-        nc.vector.tensor_copy(out=one[:], in_=seed[:])
+
+        w4s_raw = place([P, H], U8, "w4s_raw")
+        tabs = place([P, T], U8, "tabs")
+        w4_raw = place([P, 2 * H], U8, "w4_raw")
+        tab = place([P, T], U32, "tab")
+        nc.vector.memset(one[:], 1.0)
         nc.vector.memset(w4s_raw[:].bitcast(I32), 0)
+        nc.vector.memset(tabs[:].bitcast(I32), 0)
         nc.scalar.activation(out=warm[:, 0:1], in_=one[:], func=ACT.Abs_reciprocal_sqrt)
+
+        nc.sync.dma_start(list1[:], offs)
+        nc.sync.dma_start(out=w4_raw[:].bitcast(I32), in_=w4_words[0].bitcast(I32))
+        nc.sync.dma_start(list3[:], offs3)
+        nc.sync.dma_start(
+            out=tab[:].bitcast(I32),
+            in_=tab_words[0].rearrange("p n i -> p (n i)").bitcast(I32),
+        )
+        nc.sync.dma_start(list2[:], offs2)
+        nc.sync.dma_start(list4[:], offs4)
+        load_scale_rows(nc.gpsimd, w4s_raw, lambda rows: w4_scales[0, rows, :], 4)
+        load_scale_rows(nc.scalar, tabs, lambda rows: tab_scales[0, rows, :], 4)
+
+        w4 = keep.tile([P, 2 * H], U8, name="w4", align_bytes=64)
+        nc.vector.tensor_copy(
+            out=w4[:].bitcast(U16).rearrange("p (b t m) -> p b m t", b=PASSES, t=PACK),
+            in_=w4_raw[:].bitcast(U16).rearrange("p (b m t) -> p b m t", b=PASSES, t=PACK),
+        )
 
         w1_raw = []
 
         def load_w1(b):
-            raw = slot([P, PACK, PASS], F32, "w1_raw", "page0" if b == 0 else "A")
+            raw = place([P, PACK, PASS], F32, "w1_raw%d" % b, W1_RAW_AT[b])
             nc.sync.dma_start(
                 out=raw[:],
                 in_=w1[:, PASS * b : PASS * (b + 1)].rearrange("(p j) c -> p j c", j=PACK),
             )
             w1_raw.append(raw)
 
-        pages = []
+        pages = {}
 
         def load_page(k):
             b, t = divmod(k, PACK)
-            page = slot([P, T2], F32, "page", "page%d" % k)
+            page = place([P, T2], F32, "page%d" % k, PAGE_AT[k])
             rows = page0[PASS * b : PASS * (b + 1), :].rearrange("(p t) c -> t p c", t=PACK)
             nc.sync.dma_start(out=page[:], in_=rows[t])
-            pages.append(page)
+            pages[k] = page
 
         wg_rows = wgs.rearrange("(q t) j -> t q j", t=PACK)
-        wg = []
+        wg = {}
 
-        def load_weights(t):
-            rows = slot([P, S], F32, "wg", "wg%d" % t)
+        def load_weights(t, cols, kib):
+            rows = place([P, cols.stop - cols.start], F32, "wg%d_%d" % (t, cols.start), kib)
             for q in QUADRANTS:
-                nc.sync.dma_start(out=rows[32 * q : 32 * (q + 1), :], in_=wg_rows[t])
-            wg.append(rows)
+                nc.sync.dma_start(out=rows[32 * q : 32 * (q + 1), :], in_=wg_rows[t][:, cols])
+            for half, h in enumerate(halves):
+                if cols.start <= h.start and h.stop <= cols.stop:
+                    wg[(t, half)] = rows[:, h.start - cols.start : h.stop - cols.start]
 
-        nc.sync.dma_start(list1[:], offs)
-        nc.sync.dma_start(list3[:], offs3)
-        nc.sync.dma_start(list2[:], offs2)
-        nc.sync.dma_start(list4[:], offs4)
-        nc.sync.dma_start(out=w4_raw[:].bitcast(I32), in_=w4_words[0].bitcast(I32))
+        whole_list = slice(0, S)
         load_w1(0)
-        load_scale_rows(nc.sync, tabs, lambda rows: tab_scales[0, rows, :], 4)
-        tab = slot([P, T], U32, "tab", "tab")
-        nc.sync.dma_start(
-            out=tab[:].bitcast(I32),
-            in_=tab_words[0].rearrange("p n i -> p (n i)").bitcast(I32),
-        )
-        load_scale_rows(nc.scalar, w4s_raw, lambda rows: w4_scales[0, rows, :], 4)
+        load_weights(0, halves[0], WG0_AT[0])
 
-        w4 = keep.tile([P, 2 * H], U8, name="w4", align_bytes=64)
-        for b in range(PASSES):
-            nc.vector.tensor_copy(
-                out=w4[:].bitcast(U16)[:, PASS * b : PASS * (b + 1)].rearrange("p (t m) -> p m t", t=PACK),
-                in_=w4_raw[:].bitcast(U16)[:, PASS * b : PASS * (b + 1)].rearrange("p (m t) -> p m t", t=PACK),
-            )
-        tab2s = slot([P, T3], U8, "tab2s", "tab2s")
-        nc.vector.memset(tab2s[:].bitcast(I32), 0)
-
-        w1_codes = keep.tile([P, H], U32, name="w1_codes", align_bytes=64)
-        w1_scales = keep.tile([P, H], U8, name="w1_scales", align_bytes=64)
-
-        def prepare_w1(b, engine):
-            rounded = slot([P, PACK * PASS], BF16, "w1_rounded", "wg0" if b == 0 else "B")
-            round_on(
-                engine,
-                rounded[:].rearrange("p (t m j) -> p m j t", t=PACK, j=PACK),
-                w1_raw[b][:].rearrange("p j (m t) -> p m j t", t=PACK),
-            )
-            cols = slice(PASS * b, PASS * (b + 1))
-            nc.vector.quantize_mx(
-                out=w1_codes[:, cols].bitcast(FP8X4), scales=w1_scales[:, cols], in_=rounded[:]
-            )
-
-        prepare_w1(0, "scalar")
-        load_page(0)
-        load_scale_rows(nc.scalar, tab2s, lambda rows: tab2_scales[:, rows, :], 4 * PASSES)
-        load_weights(0)
         vs = keep.tile([P, S], U8, name="vs", align_bytes=64)
         nc.vector.tensor_copy(vs[:], tabs[:].indirect(list1[:]))
-        w4s = slot([P, H], U8, "w4s", "w4s")
-        for b in range(PASSES):
-            nc.vector.tensor_copy(
-                out=w4s[:, PASS * b : PASS * (b + 1)].rearrange("p (t m) -> p m t", t=PACK),
-                in_=w4s_raw[:, PASS * b : PASS * (b + 1)].rearrange("p (m t) -> p m t", t=PACK),
-            )
-        load_weights(1)
-
+        load_page(0)
+        load_weights(0, halves[1], WG0_AT[1])
+        load_weights(1, whole_list, WG_AT[1])
+        w4s = place([P, H], U8, "w4s")
+        nc.vector.tensor_copy(
+            out=w4s[:].rearrange("p (b t m) -> p b m t", b=PASSES, t=PACK),
+            in_=w4s_raw[:].rearrange("p (b m t) -> p b m t", b=PASSES, t=PACK),
+        )
         v = []
         for half in range(HALVES):
             words = keep.tile([P, BANK], U32, name="v%d" % half, align_bytes=64)
             nc.vector.tensor_copy(words[:], tab[:].indirect(entries(list1, halves[half])))
             v.append(words)
+        load_page(1)
+        load_weights(2, whole_list, WG_AT[2])
         load_w1(1)
-        v2s = slot([P, S2], U8, "v2s", "v2s")
-        nc.vector.tensor_copy(v2s[:], tab2s[:].indirect(list2[:]))
 
-        woven0_tags = ["W0a", "W0b"]
-        made = {}
-        last_tiles = {}
+        w1_codes = keep.tile([P, H], U32, name="w1_codes", align_bytes=64)
+        w1_scales = keep.tile([P, H], U8, name="w1_scales", align_bytes=64)
+        w1_rounded = []
 
-        def products(k, cols, bank_b, bank_a):
+        def round_w1(b, engine):
+            rounded = place([P, PACK * PASS], BF16, "w1_rounded%d" % b, W1_ROUNDED_AT[b])
+            round_on(
+                engine,
+                rounded[:].rearrange("p (t m j) -> p m j t", t=PACK, j=PACK),
+                w1_raw[b][:].rearrange("p j (m t) -> p m j t", t=PACK),
+            )
+            w1_rounded.append(rounded)
+
+        def quantise_w1(first, last):
+            b = first // PACK
+            cols = slice(P * first, P * (last + 1))
+            nc.vector.quantize_mx(
+                out=w1_codes[:, cols].bitcast(FP8X4), scales=w1_scales[:, cols],
+                in_=w1_rounded[b][:, PASS * (first - PACK * b) : PASS * (last + 1 - PACK * b)],
+            )
+
+        def products(k, half):
             rows = slice(P * k, P * (k + 1))
-            half, start = divmod(cols.start, BANK)
-            width = cols.stop - cols.start
-            words = v[half][:, start : start + width].bitcast(FP8X4)
-            acc_b = bank(bank_b, "acc_b")[:, 0:width]
-            acc_a = bank(bank_a, "acc_a")[:, 0:width]
+            words = v[half][:].bitcast(FP8X4)
+            first_bank = PACK * (k % 2) + 2 * half
+            acc_b = bank(first_bank, "acc_b")
+            acc_a = bank(first_bank + 1, "acc_a")
             nc.tensor.matmul_mx(
-                out=acc_b,
+                out=acc_b[:],
                 lhsT=w4[:, 2 * rows.start : 2 * rows.stop].bitcast(FP4X4), lhsT_scale=w4s[:, rows],
-                rhs=words, rhs_scale=vs[:, cols], start=True, stop=True,
+                rhs=words, rhs_scale=vs[:, halves[half]], start=True, stop=True,
             )
             nc.tensor.matmul_mx(
-                out=acc_a,
+                out=acc_a[:],
                 lhsT=w1_codes[:, rows].bitcast(FP8X4), lhsT_scale=w1_scales[:, rows],
-                rhs=words, rhs_scale=vs[:, cols], start=True, stop=True,
+                rhs=words, rhs_scale=vs[:, halves[half]], start=True, stop=True,
             )
             return acc_b, acc_a
 
-        def size(root, acc_b):
-            nc.scalar.activation(out=root, in_=acc_b, func=ACT.Abs)
+        def size(gain, acc_b):
+            nc.scalar.activation(out=gain, in_=acc_b, func=ACT.Abs)
 
-        def invert(root):
-            nc.scalar.activation(out=root, in_=root, func=ACT.Abs_reciprocal_sqrt, bias=one[:])
+        def invert(gain):
+            nc.scalar.activation(out=gain, in_=gain, func=ACT.Abs_reciprocal_sqrt, bias=one[:])
 
-        def damp(gain, root):
-            nc.scalar.activation(out=gain, in_=root, func=ACT.Square)
+        def square(gain):
+            nc.scalar.activation(out=gain, in_=gain, func=ACT.Square)
 
-        def put(k, edit, cols):
-            nc.vector.tensor_copy(pages[k][:].indirect(entries(list3, cols)), edit[:, cols])
+        def times(engine, dst, x, y):
+            engine.tensor_tensor(out=dst, in0=x, in1=y, op=MULT)
+
+        edits = {}
+        end = {}
+
+        def put(k, values, cols):
+            nc.vector.tensor_copy(pages[k][:].indirect(entries(list3, cols)), values)
 
         def first_plane():
-            gain = slot([P, S], F32, "gain", GAIN_SLOTS[0])
-            edit = slot([P, S], F32, "edit", EDIT_SLOTS[0])
-            root_tags = ["page1", "wg2", "wg3"]
-            for i, cols in enumerate(FIRST_PARTS):
-                acc_b, acc_a = products(0, cols, 2 * i, 2 * i + 1)
-                root = slot([P, cols.stop - cols.start], F32, "root", root_tags[i])[:]
-                size(root, acc_b)
-                invert(root)
-                damp(gain[:, cols], root)
-                engine = nc.vector if i == 0 else nc.gpsimd
-                engine.tensor_tensor(out=gain[:, cols], in0=gain[:, cols], in1=wg[0][:, cols], op=MULT)
-                nc.vector.tensor_tensor(out=edit[:, cols], in0=acc_a, in1=gain[:, cols], op=MULT)
-                put(0, edit, cols)
+            gain = place([P, S], F32, "gain0", GAIN_AT[0])
+            edit = place([P, S], F32, "edit0", EDIT_AT[0])
+            h0, h1 = halves
+            accs = [products(0, half) for half in range(HALVES)]
+            size(gain[:, h0], accs[0][0][:])
+            size(gain[:, h1], accs[1][0][:])
+            invert(gain[:, h0])
+            invert(gain[:, h1])
+            square(gain[:, h0])
+            square(gain[:, h1])
+            nc.scalar.copy(out=edit[:, h1], in_=accs[1][1][:])
+            times(nc.vector, gain[:, h0], gain[:, h0], wg[(0, 0)])
+            quantise_w1(1, 1)
+            quantise_w1(2, 3)
+            times(nc.vector, edit[:, h0], accs[0][1][:], gain[:, h0])
+            weighted = place([P, BANK], F32, "weighted0_1", WEIGHTED_AT[0])
+            times(nc.gpsimd, weighted[:], gain[:, h1], wg[(0, 1)])
+            times(nc.gpsimd, edit[:, h1], edit[:, h1], weighted[:])
+            edits[0] = edit
 
         def first_stage(k):
             t = k % PACK
-            banks = (6, 0, 7, 1) if k % 2 else (2, 3, 4, 5)
-            accs = [products(k, halves[half], banks[2 * half], banks[2 * half + 1]) for half in range(HALVES)]
-            root_tags = ["root0", "root1"]
-            if k == LAST - 1:
-                root_tags = woven0_tags
+            h0, h1 = halves
+            accs = [products(k, half) for half in range(HALVES)]
+            gain = place([P, S], F32, "gain%d" % k, GAIN_AT[k])
+            edit = place([P, S if k < LAST else END], F32, "edit%d" % k, EDIT_AT[k])
+            size(gain[:, h0], accs[0][0][:])
+            size(gain[:, h1], accs[1][0][:])
+            invert(gain[:, h0])
+            nc.scalar.copy(out=edit[:, h0], in_=accs[0][1][:])
+            square(gain[:, h0])
+            invert(gain[:, h1])
+            main = h1 if k < LAST else slice(BANK, END)
+            width = main.stop - main.start
+            nc.scalar.copy(out=edit[:, main], in_=accs[1][1][:, 0:width])
             if k == LAST:
-                root_tags = ["root0", "B"]
-            roots = [slot([P, BANK], F32, "root", root_tags[half])[:] for half in range(HALVES)]
-            gain = slot([P, S], F32, "gain", GAIN_SLOTS[k])
-            plain = slot([P, S], F32, "plain", PLAIN_SLOTS[k])
-            edit = slot([P, S if k < LAST else END], F32, "edit", EDIT_SLOTS[k])
-            size(roots[0], accs[0][0])
-            size(roots[1], accs[1][0])
-            invert(roots[0])
-            nc.scalar.copy(out=plain[:, halves[0]], in_=accs[0][1])
-            damp(gain[:, halves[0]], roots[0])
-            invert(roots[1])
-            if k == LAST:
-                end_plain = slot([P, S - END], F32, "end_plain", "root1")
-                nc.scalar.copy(out=plain[:, BANK:END], in_=accs[1][1][:, 0 : END - BANK])
-                nc.scalar.copy(out=end_plain[:], in_=accs[1][1][:, END - BANK : BANK])
-            else:
-                nc.scalar.copy(out=plain[:, halves[1]], in_=accs[1][1])
-            damp(gain[:, halves[1]], roots[1])
-            products_of = []
-            for half, h in enumerate(halves):
-                weighted = slot([P, BANK], F32, "weighted", "weighted%d" % half)
-                nc.gpsimd.tensor_tensor(out=weighted[:], in0=gain[:, h], in1=wg[t][:, h], op=MULT)
-                products_of.append(weighted)
-            for half, h in enumerate(halves):
-                weighted = products_of[half]
-                if k == LAST and h.stop == S:
-                    last_tiles["end"] = (end_plain, weighted)
-                    h = slice(h.start, END)
-                nc.gpsimd.tensor_tensor(
-                    out=edit[:, h], in0=plain[:, h], in1=weighted[:, 0 : h.stop - h.start], op=MULT
-                )
-            made[k] = edit
-            last_tiles[k] = gain
-
-        def scatter(k):
-            for cols in halves if k < SPLIT_SCATTERS else [slice(0, S)]:
-                put(k, made[k], cols)
+                end["plain"] = place([P, S - END], F32, "end_plain")
+                nc.scalar.copy(out=end["plain"][:], in_=accs[1][1][:, width:BANK])
+            square(gain[:, h1])
+            weighted = [place([P, BANK], F32, "weighted%d_%d" % (k, half), WEIGHTED_AT[half]) for half in range(HALVES)]
+            times(nc.gpsimd, weighted[0][:], gain[:, h0], wg[(t, 0)])
+            times(nc.gpsimd, weighted[1][:], gain[:, h1], wg[(t, 1)])
+            times(nc.gpsimd, edit[:, h0], edit[:, h0], weighted[0][:])
+            times(nc.gpsimd, edit[:, main], edit[:, main], weighted[1][:, 0:width])
+            end["gain"] = weighted[1][:, width:BANK]
+            edits[k] = edit
 
         side0 = []
+        side1 = []
 
-        def gather_plane_pass0(k):
-            for w in range(2):
-                if k == 0:
-                    side0.append(slot([P, PACK, WIDE], F32, "side0", "AB"[w]))
-                nc.sync.dma_start(out=side0[w][:, k, :], in_=pages[k][:, WIDE * w : WIDE * (w + 1)])
-
-        codes0 = []
-        scales0 = keep.tile([P, T2], U8, name="scales0", align_bytes=64)
-
-        woven = []
-
-        def weave_pass0():
-            for w in range(2):
-                tile_w = slot([P, PACK * WIDE], BF16, "woven0", woven0_tags[w])
-                nc.scalar.copy(
-                    out=tile_w[:].rearrange("p (c i t) -> p c t i", i=LINE, t=PACK),
-                    in_=side0[w][:].rearrange("p t (c i) -> p c t i", i=LINE),
-                )
-                woven.append(tile_w)
-
-        def quantise_pass0(w):
-            codes = slot([P, WIDE], U32, "codes0", "codes0_%d" % w)
-            nc.vector.quantize_mx(
-                out=codes[:].bitcast(FP8X4), scales=scales0[:, WIDE * w : WIDE * (w + 1)], in_=woven[w][:]
-            )
-            codes0.append(codes)
+        def scatter(k):
+            for cols in halves if k < SPLIT_SCATTERS else [whole_list]:
+                put(k, edits[k][:, cols], cols)
+            if k < PACK:
+                for w in range(2):
+                    if k == 0:
+                        side0.append(place([P, PACK, WIDE], F32, "side0_%d" % w, SIDE0_AT[w]))
+                    nc.sync.dma_start(out=side0[w][:, k, :], in_=pages[k][:, WIDE * w : WIDE * (w + 1)])
+            else:
+                for c in range(CHUNKS):
+                    if k == PACK:
+                        side1.append(place([P, PACK - 1, BANK], F32, "side1_%d" % c, SIDE1_AT[c]))
+                    nc.sync.dma_start(out=side1[c][:, k - PACK, :], in_=pages[k][:, chunks[c]])
 
         tab2 = []
-        v2 = []
 
         def load_workers(b):
-            table = slot([P, T3], U32, "tab2", "tab2_%d" % b)
+            table = place([P, T3], U32, "tab2_%d" % b, TAB2_AT[b])
             nc.sync.dma_start(
                 out=table[:].bitcast(I32),
                 in_=tab2_words[b].rearrange("p n i -> p (n i)").bitcast(I32),
             )
             tab2.append(table)
 
-        def gather_workers(b):
-            words = slot([P, S2], U32, "v2", woven0_tags[1] if b == 0 else "tab2_0")
-            nc.vector.tensor_copy(words[:], tab2[b][:].indirect(list2[:]))
-            v2.append(words)
-
-        first_plane()
-        load_page(1)
-        load_weights(2)
-        load_weights(3)
-        load_page(2)
-        first_stage(1)
-        load_page(3)
-        first_stage(2)
-        prepare_w1(1, "scalar")
-        gather_plane_pass0(0)
-        scatter(1)
-        gather_plane_pass0(1)
-        load_page(4)
-        first_stage(3)
-        scatter(2)
-        gather_plane_pass0(2)
-        load_page(5)
-        first_stage(4)
-        scatter(3)
-        gather_plane_pass0(3)
-        load_page(6)
-        load_workers(0)
-        first_stage(5)
-        scatter(4)
-        load_workers(1)
-        load_page(7)
-        side1 = slot([P, 2, T2], F32, "side1", "side1")
-        nc.sync.dma_start(out=side1[:, 0, :], in_=pages[PACK][:])
-        first_stage(6)
-        scatter(5)
-        nc.sync.dma_start(out=side1[:, 1, :], in_=pages[PACK + 1][:])
-        first_stage(LAST)
-        weave_pass0()
-        quantise_pass0(0)
-        scatter(6)
-        quantise_pass0(1)
-        gather_workers(0)
-        gather_workers(1)
-        nc.scalar.activation(out=warm[:, 1:2], in_=last_tiles[LAST][:, S - 1 : S], func=ACT.Sigmoid)
-
         allowed = []
-        for i in range(2):
-            rows = slot([P, 2, PICK], F32, "allowed", "page%d" % (PACK + i))
+
+        def load_permit(i):
+            rows = place([P, 2, PICK], F32, "allowed%d" % i, PERMIT_AT[i])
             nc.sync.dma_start(
                 out=rows[:], in_=permit[2 * P * i : 2 * P * (i + 1), :].rearrange("(n p) m -> p n m", p=P)
             )
             allowed.append(rows)
 
-        woven_all = slot([P, PACK * T2], BF16, "woven1", "B")
-        woven1 = [woven_all[:, PACK * BANK * c : PACK * BANK * (c + 1)] for c in range(CHUNKS)]
-        late = ["vector", "vector", "scalar", "scalar"]
-        views = [w.rearrange("p (c t) -> p c t", t=PACK) for w in woven1]
-        for c in range(CHUNKS):
-            round_on("scalar", views[c][:, :, 0:2], side1[:, :, chunks[c]].rearrange("p e c -> p c e"))
-        for c in range(CHUNKS):
+        round_w1(0, "vector")
+        quantise_w1(0, 0)
+        load_page(2)
+        load_weights(3, whole_list, WG_AT[3])
+        first_plane()
+        load_page(3)
+        load_page(4)
+        first_stage(1)
+        scatter(0)
+        load_page(5)
+        first_stage(2)
+        round_w1(1, "scalar")
+        scatter(1)
+        quantise_w1(PACK, LAST)
+        load_page(6)
+        load_page(7)
+        tab2s = place([P, T3], U8, "tab2s")
+        nc.vector.memset(tab2s[:].bitcast(I32), 0)
+        load_scale_rows(nc.sync, tab2s, lambda rows: tab2_scales[:, rows, :], 4 * PASSES)
+        load_workers(0)
+        for k in range(3, PLANES):
+            first_stage(k)
+            scatter(k - 1)
+            if k == 3:
+                load_workers(1)
+        nc.scalar.activation(out=warm[:, 1:2], in_=end["plain"][:, 0:1], func=ACT.Sigmoid)
+        load_permit(0)
+        load_permit(1)
+
+        scales0 = place([P, T2], U8, "scales0")
+        codes0 = []
+        woven0 = []
+        for w, engine in enumerate(["scalar", "scalar"]):
+            woven = place([P, PACK * WIDE], BF16, "woven0_%d" % w, WOVEN0_AT[w])
             round_on(
-                "scalar", views[c][:, :, 2:4],
-                pages[LAST - 1][:, chunks[c]].unsqueeze(2).to_broadcast([P, BANK, 2]),
+                engine,
+                woven[:].rearrange("p (c i t) -> p c t i", i=LINE, t=PACK),
+                side0[w][:].rearrange("p t (c i) -> p c t i", i=LINE),
             )
-        put(LAST, made[LAST], slice(0, END))
-        end_plain, end_weighted = last_tiles["end"]
-        end_edit = slot([P, S - END], F32, "end_edit", "page6")
-        nc.gpsimd.tensor_tensor(out=end_edit[:], in0=end_plain[:], in1=end_weighted[:, END - BANK : BANK], op=MULT)
-        nc.vector.tensor_copy(pages[LAST][:].indirect(entries(list3, slice(END, S))), end_edit[:])
+            woven0.append(woven)
+        put(LAST, edits[LAST][:], slice(0, END))
+        for w in range(2):
+            codes = place([P, WIDE], U32, "codes0_%d" % w, CODES0_AT[w])
+            nc.vector.quantize_mx(
+                out=codes[:].bitcast(FP8X4), scales=scales0[:, WIDE * w : WIDE * (w + 1)], in_=woven0[w][:]
+            )
+            codes0.append(codes)
+
+        v2s = place([P, S2], U8, "v2s")
+        nc.vector.tensor_copy(v2s[:], tab2s[:].indirect(list2[:]))
+        v2 = {}
+
+        def gather_workers(pair):
+            cols = slice(2 * P * pair, 2 * P * (pair + 1))
+            for b in range(PASSES):
+                words = place([P, 2 * P], U32, "v2_%d_%d" % (pair, b), WORKERS_AT[pair][b])
+                nc.vector.tensor_copy(words[:], tab2[b][:].indirect(entries(list2, cols)))
+                v2[(pair, b)] = words
+
+        gather_workers(0)
+
+        woven1 = []
+        for c, engine in enumerate(["scalar", "scalar", "scalar", "gpsimd"]):
+            woven = place([P, PACK * BANK], BF16, "woven1_%d" % c, WOVEN1_AT[c])
+            round_on(
+                engine,
+                woven[:].rearrange("p (c i t) -> p c t i", i=LINE, t=PACK)[:, :, 0 : PACK - 1, :],
+                side1[c][:].rearrange("p t (c i) -> p c t i", i=LINE),
+            )
+            woven1.append(woven)
+        end_edit = place([P, S - END], F32, "end_edit")
+        times(nc.gpsimd, end_edit[:], end["plain"][:], end["gain"])
+        put(LAST, end_edit[:], slice(END, S))
 
         scores = {}
         codes1 = []
@@ -401,10 +408,11 @@ def tile_list_farm_job_board_kernel(
                 rhs, rhs_scale = codes0[c // 2][:, halves[c % 2]], scales0[:, chunks[c]]
             else:
                 rhs, rhs_scale = codes1[c][0][:], codes1[c][1][:]
-            cols = slice(P * n, P * (n + 1))
+            pair, within = divmod(n, 2)
             nc.tensor.matmul_mx(
                 out=scores[(n, c)][:],
-                lhsT=v2[b][:, cols].bitcast(FP8X4), lhsT_scale=v2s[4 * b : P, cols],
+                lhsT=v2[(pair, b)][:, P * within : P * (within + 1)].bitcast(FP8X4),
+                lhsT_scale=v2s[4 * b : P, P * n : P * (n + 1)],
                 rhs=rhs.bitcast(FP8X4), rhs_scale=rhs_scale,
                 start=(b == 0), stop=(b == PASSES - 1),
             )
@@ -412,25 +420,29 @@ def tile_list_farm_job_board_kernel(
         for n in range(2):
             for c in range(CHUNKS):
                 score_pass(n, c, 0)
+        for c, engine in enumerate(["vector", "vector", "scalar", "scalar"]):
+            round_on(
+                engine,
+                woven1[c][:].rearrange("p (c t) -> p c t", t=PACK)[:, :, PACK - 1],
+                pages[LAST][:, chunks[c]],
+            )
         for c in range(CHUNKS):
-            round_on(late[c], views[c][:, :, 3], pages[LAST][:, chunks[c]])
-        for c in range(CHUNKS):
-            codes = slot([P, BANK], U32, "codes1", "wg%d" % c)
-            scales = keep.tile([P, BANK], U8, name="scales1_%d" % c, align_bytes=64)
-            nc.vector.quantize_mx(out=codes[:].bitcast(FP8X4), scales=scales[:], in_=woven1[c])
+            codes = place([P, BANK], U32, "codes1_%d" % c, CODES1_AT[c])
+            scales = place([P, BANK], U8, "scales1_%d" % c, SCALES1_AT[c])
+            nc.vector.quantize_mx(out=codes[:].bitcast(FP8X4), scales=scales[:], in_=woven1[c][:])
             codes1.append((codes, scales))
-            for n in range(2):
-                score_pass(n, c, 1)
+            score_pass(0, c, 1)
+        for c in range(CHUNKS):
+            score_pass(1, c, 1)
+        gather_workers(1)
 
-        e_tags = ["page7", "page0", "page1", "page2"]
-        vector_banks = [(0, 2), (2, 3), (3, 3)]
+        vector_banks = [(2, 3), (3, 3)]
         whole = slice(0, PICK)
-        pick_parts = [[whole], [whole], halves, LAST_PARTS]
-        pick_tags = [["edit_a"], ["edit_b"], ["A", "end_pick"], ["gain", "end_pick"]]
+        pick_parts = [[whole], [whole], [whole], [slice(0, END), slice(END, PICK)]]
         picked = {}
 
         def fetch_scores(n):
-            e = slot([P, T2], F32, "e", e_tags[n])
+            e = place([P, T2], F32, "e%d" % n, SCORES_AT[n])
             for c in range(CHUNKS):
                 engine = "vector" if (n, c) in vector_banks else "scalar"
                 round_on(engine, e[:, chunks[c]], scores[(n, c)][:])
@@ -442,39 +454,32 @@ def tile_list_farm_job_board_kernel(
 
         def pick(n, i, e):
             cols = pick_parts[n][i]
-            x = slot([P, cols.stop - cols.start], F32, "x", pick_tags[n][i])
+            x = place([P, cols.stop - cols.start], F32, "x%d_%d" % (n, i), PICKED_AT[n][i])
             nc.vector.tensor_copy(x[:], e[:].indirect(entries(list4, cols)))
             picked[(n, i)] = x
 
-        def squash(n, i, tag=None):
+        def squash(n, i):
             x = picked[(n, i)]
-            y = x if tag is None else slot(list(x.shape), F32, "y", tag)
-            nc.scalar.activation(out=y[:], in_=x[:], func=ACT.Sigmoid)
-            picked[(n, i)] = y
+            nc.scalar.activation(out=x[:], in_=x[:], func=ACT.Sigmoid)
 
         def weigh_and_store(n, i, engine):
             cols = pick_parts[n][i]
             y = picked[(n, i)]
-            engine.tensor_tensor(out=y[:], in0=y[:], in1=allowed[n // 2][:, n % 2, cols], op=MULT)
+            times(engine, y[:], y[:], allowed[n // 2][:, n % 2, cols])
             nc.sync.dma_start(out=out[P * n : P * (n + 1), cols], in_=y[:])
 
         pick(0, 0, fetch_scores(0))
         pick(1, 0, fetch_scores(1))
         squash(0, 0)
         weigh_and_store(0, 0, nc.gpsimd)
-        e = fetch_scores(2)
-        pick(2, 0, e)
-        pick(2, 1, e)
+        pick(2, 0, fetch_scores(2))
         squash(1, 0)
         weigh_and_store(1, 0, nc.gpsimd)
         e = fetch_scores(3)
         pick(3, 0, e)
-        squash(2, 0)
-        squash(2, 1, "weighted0")
-        weigh_and_store(2, 0, nc.gpsimd)
         pick(3, 1, e)
-        squash(3, 0)
-        weigh_and_store(2, 1, nc.vector)
-        squash(3, 1)
-        weigh_and_store(3, 0, nc.vector)
-        weigh_and_store(3, 1, nc.vector)
+        squash(2, 0)
+        weigh_and_store(2, 0, nc.gpsimd)
+        for i in range(2):
+            squash(3, i)
+            weigh_and_store(3, i, nc.vector)

@@ -40,11 +40,11 @@ W1_RAW_AT = [2, 41]
 W1_ROUNDED_AT = [55, 79]
 GAIN_AT = [65, 79, 155, 159, 155, 159, 115, 123]
 EDIT_AT = [69, 163, 167, 171, 175, 163, 167, 179]
-WEIGHTED_AT = [187, 189]
+WEIGHTED_AT = [187, 191]
 SIDE0_AT = [83, 99]
 WOVEN0_AT = [115, 123]
 CODES0_AT = [14, 18]
-SIDE1_AT = [131, 137, 143, 149]
+SIDE1_AT = [149, 131, 137, 143]
 WOVEN1_AT = [83, 87, 91, 95]
 CODES1_AT = [99, 101, 103, 105]
 SCALES1_AT = [107, 107.5, 108, 108.5]
@@ -52,10 +52,10 @@ TAB2_AT = [29, 6]
 WORKERS_AT = [[179, 180], [95, 96]]
 PERMIT_AT = [65, 57]
 SCORES_AT = [115, 123, 49, 41]
-PICKED_AT = [[163], [167], [171], [175, 178]]
+PICKED_AT = [[163], [167], [171, 173], [175, 178]]
 AT = {
     "w4_raw": 1, "tabs": 21.5, "w4s": 22, "tab": 29, "tab2s": 81, "end_edit": 148.5,
-    "v2s": 181, "end_plain": 182, "w4s_raw": 184, "scales0": 185,
+    "v2s": 181, "end_plain": 182, "end_root": 183, "w4s_raw": 184, "scales0": 185,
 }
 
 
@@ -235,6 +235,9 @@ def tile_list_farm_job_board_kernel(
         def times(engine, dst, x, y):
             engine.tensor_tensor(out=dst, in0=x, in1=y, op=MULT)
 
+        weighted = place([P, S], F32, "weighted", WEIGHTED_AT[0])
+        second = place([P, BANK], F32, "second", WEIGHTED_AT[1])
+        late = {}
         edits = {}
         end = {}
 
@@ -246,20 +249,16 @@ def tile_list_farm_job_board_kernel(
             edit = place([P, S], F32, "edit0", EDIT_AT[0])
             h0, h1 = halves
             accs = [products(0, half) for half in range(HALVES)]
-            size(gain[:, h0], accs[0][0][:])
-            size(gain[:, h1], accs[1][0][:])
-            invert(gain[:, h0])
-            invert(gain[:, h1])
-            square(gain[:, h0])
-            square(gain[:, h1])
-            nc.scalar.copy(out=edit[:, h1], in_=accs[1][1][:])
+            for half, h in enumerate(halves):
+                size(gain[:, h], accs[half][0][:])
+                invert(gain[:, h])
+                square(gain[:, h])
             times(nc.vector, gain[:, h0], gain[:, h0], wg[(0, 0)])
             quantise_w1(1, 1)
             quantise_w1(2, 3)
             times(nc.vector, edit[:, h0], accs[0][1][:], gain[:, h0])
-            weighted = place([P, BANK], F32, "weighted0_1", WEIGHTED_AT[0])
-            times(nc.gpsimd, weighted[:], gain[:, h1], wg[(0, 1)])
-            times(nc.gpsimd, edit[:, h1], edit[:, h1], weighted[:])
+            times(nc.gpsimd, weighted[:, h1], gain[:, h1], wg[(0, 1)])
+            late[0] = (accs[1][1], weighted[:, h1])
             edits[0] = edit
 
         def first_stage(k):
@@ -273,28 +272,45 @@ def tile_list_farm_job_board_kernel(
             invert(gain[:, h0])
             nc.scalar.copy(out=edit[:, h0], in_=accs[0][1][:])
             square(gain[:, h0])
-            invert(gain[:, h1])
             main = h1 if k < LAST else slice(BANK, END)
             width = main.stop - main.start
-            nc.scalar.copy(out=edit[:, main], in_=accs[1][1][:, 0:width])
+            invert(gain[:, main])
+            if k == LAST:
+                end["root"] = place([P, S - END], F32, "end_root")
+                nc.scalar.activation(
+                    out=end["root"][:], in_=gain[:, END:S], func=ACT.Abs_reciprocal_sqrt, bias=one[:]
+                )
+            if k >= SPLIT_SCATTERS:
+                nc.scalar.copy(out=edit[:, main], in_=accs[1][1][:, 0:width])
             if k == LAST:
                 end["plain"] = place([P, S - END], F32, "end_plain")
                 nc.scalar.copy(out=end["plain"][:], in_=accs[1][1][:, width:BANK])
-            square(gain[:, h1])
-            weighted = [place([P, BANK], F32, "weighted%d_%d" % (k, half), WEIGHTED_AT[half]) for half in range(HALVES)]
-            times(nc.gpsimd, weighted[0][:], gain[:, h0], wg[(t, 0)])
-            times(nc.gpsimd, weighted[1][:], gain[:, h1], wg[(t, 1)])
-            times(nc.gpsimd, edit[:, h0], edit[:, h0], weighted[0][:])
-            times(nc.gpsimd, edit[:, main], edit[:, main], weighted[1][:, 0:width])
-            end["gain"] = weighted[1][:, width:BANK]
+            square(gain[:, main])
+            if k < SPLIT_SCATTERS:
+                times(nc.gpsimd, weighted[:, h0], gain[:, h0], wg[(t, 0)])
+                times(nc.gpsimd, edit[:, h0], edit[:, h0], weighted[:, h0])
+                times(nc.gpsimd, second[:], gain[:, h1], wg[(t, 1)])
+                late[k] = (accs[1][1], second[:])
+            else:
+                for half, h in enumerate((h0, main)):
+                    times(nc.gpsimd, weighted[:, h], gain[:, h], wg[(t, half)][:, 0 : h.stop - h.start])
+                for h in (h0, main):
+                    times(nc.gpsimd, edit[:, h], edit[:, h], weighted[:, h])
+                if k == LAST:
+                    times(nc.gpsimd, end["plain"][:], end["plain"][:], wg[(t, 1)][:, width:BANK])
             edits[k] = edit
 
         side0 = []
         side1 = []
 
         def scatter(k):
-            for cols in halves if k < SPLIT_SCATTERS else [whole_list]:
-                put(k, edits[k][:, cols], cols)
+            if k < SPLIT_SCATTERS:
+                h0, h1 = halves
+                put(k, edits[k][:, h0], h0)
+                times(nc.vector, edits[k][:, h1], late[k][0][:], late[k][1])
+                put(k, edits[k][:, h1], h1)
+            else:
+                put(k, edits[k][:], whole_list)
             if k < PACK:
                 for w in range(2):
                     if k == 0:
@@ -350,7 +366,7 @@ def tile_list_farm_job_board_kernel(
             scatter(k - 1)
             if k == 3:
                 load_workers(1)
-        nc.scalar.activation(out=warm[:, 1:2], in_=end["plain"][:, 0:1], func=ACT.Sigmoid)
+        nc.scalar.activation(out=warm[:, 1:2], in_=end["root"][:, 0:1], func=ACT.Sigmoid)
         load_permit(0)
         load_permit(1)
 
@@ -387,17 +403,22 @@ def tile_list_farm_job_board_kernel(
         gather_workers(0)
 
         woven1 = []
-        for c, engine in enumerate(["scalar", "scalar", "scalar", "gpsimd"]):
+        for c in range(CHUNKS):
             woven = place([P, PACK * BANK], BF16, "woven1_%d" % c, WOVEN1_AT[c])
-            round_on(
-                engine,
-                woven[:].rearrange("p (c i t) -> p c t i", i=LINE, t=PACK)[:, :, 0 : PACK - 1, :],
-                side1[c][:].rearrange("p t (c i) -> p c t i", i=LINE),
-            )
+            dst = woven[:].rearrange("p (c i t) -> p c t i", i=LINE, t=PACK)[:, :, 0 : PACK - 1, :]
+            src = side1[c][:].rearrange("p t (c i) -> p c t i", i=LINE)
+            if c == 0:
+                middle = BANK // LINE // 2
+                round_on("gpsimd", dst[:, 0:middle], src[:, 0:middle])
+                round_on("scalar", dst[:, middle : 2 * middle], src[:, middle : 2 * middle])
+            else:
+                round_on("scalar", dst, src)
             woven1.append(woven)
-        end_edit = place([P, S - END], F32, "end_edit")
-        times(nc.gpsimd, end_edit[:], end["plain"][:], end["gain"])
-        put(LAST, end_edit[:], slice(END, S))
+        end_gain = place([P, S - END], F32, "end_edit")
+        nc.scalar.activation(out=end_gain[:], in_=end["root"][:], func=ACT.Square)
+        times(
+            nc.vector, pages[LAST][:].indirect(entries(list3, slice(END, S))), end["plain"][:], end_gain[:]
+        )
 
         scores = {}
         codes1 = []
@@ -438,7 +459,7 @@ def tile_list_farm_job_board_kernel(
 
         vector_banks = [(2, 3), (3, 3)]
         whole = slice(0, PICK)
-        pick_parts = [[whole], [whole], [whole], [slice(0, END), slice(END, PICK)]]
+        pick_parts = [[whole], [whole], halves, [slice(0, END), slice(END, PICK)]]
         picked = {}
 
         def fetch_scores(n):
@@ -472,7 +493,9 @@ def tile_list_farm_job_board_kernel(
         pick(1, 0, fetch_scores(1))
         squash(0, 0)
         weigh_and_store(0, 0, nc.gpsimd)
-        pick(2, 0, fetch_scores(2))
+        e = fetch_scores(2)
+        pick(2, 0, e)
+        pick(2, 1, e)
         squash(1, 0)
         weigh_and_store(1, 0, nc.gpsimd)
         e = fetch_scores(3)
@@ -480,6 +503,8 @@ def tile_list_farm_job_board_kernel(
         pick(3, 1, e)
         squash(2, 0)
         weigh_and_store(2, 0, nc.gpsimd)
+        squash(2, 1)
+        weigh_and_store(2, 1, nc.vector)
         for i in range(2):
             squash(3, i)
             weigh_and_store(3, i, nc.vector)

@@ -33,29 +33,32 @@ QUADRANTS = (0, 2, 1, 3)
 END = 768
 SPLIT_SCATTERS = 2
 
-PAGE_AT = [14, 29, 6, 49, 57, 65, 41, 73]
-WG_AT = [None, 25, 37, 2]
-WG0_AT = [0, 23]
-W1_RAW_AT = [2, 41]
-W1_ROUNDED_AT = [55, 79]
-GAIN_AT = [65, 79, 155, 159, 155, 159, 115, 123]
-EDIT_AT = [69, 163, 167, 171, 175, 163, 167, 179]
-WEIGHTED_AT = [187, 191]
-SIDE0_AT = [83, 99]
-WOVEN0_AT = [115, 123]
-CODES0_AT = [14, 18]
-SIDE1_AT = [149, 131, 137, 143]
-WOVEN1_AT = [83, 87, 91, 95]
-CODES1_AT = [99, 101, 103, 105]
-SCALES1_AT = [107, 107.5, 108, 108.5]
-TAB2_AT = [29, 6]
-WORKERS_AT = [[179, 180], [95, 96]]
-PERMIT_AT = [65, 57]
-SCORES_AT = [115, 123, 49, 41]
-PICKED_AT = [[163], [167], [171, 173], [175, 178]]
+PAGE_AT = [0, 23, 43, 51.5, 59.5, 67.5, 15, 75.5]
+WG_AT = [None, 33, 37, 11]
+WG0_AT = [9, 31]
+W1_RAW_AT = [11, 15]
+W1_ROUNDED_AT = [57.5, 81.5]
+GAIN_AT = [202.5, 67.5, 81.5, 157.5, 161.5, 207.5, 117.5, 125.5]
+EDIT_AT = [71.5, 165.5, 169.5, 173.5, 177.5, 211.5, 195.5, 181.5]
+W1_CODES_AT = [199.5, 169.5]
+W1_SCALES_AT = [201.5, 171.5]
+B_BANKS = [(0, 2), (4, 6), (0, 2), (4, 6), (0, 2), (1, 3), (5, 7), (0, 2)]
+A_BANKS = [(1, 3), (5, 7), (1, 3), (5, 7), (1, 3), (5, 7), (0, 2), (4, 6)]
+SIDE0_AT = [85.5, 101.5]
+WOVEN0_AT = [117.5, 125.5]
+CODES0_AT = [0, 4]
+SIDE1_AT = [145.5, 151.5, 133.5, 139.5]
+WOVEN1_AT = [85.5, 89.5, 220, 224]
+CODES1_AT = [101.5, 103.5, 105.5, 107.5]
+SCALES1_AT = [109.5, 110, 110.5, 111]
+TAB2_AT = [23, 43]
+WORKERS_AT = [[181.5, 182.5], [224, 225]]
+PERMIT_AT = [15, 133.5]
+SCORES_AT = [117.5, 125.5, 51.5, 59.5]
+PICKED_AT = [[165.5], [169.5], [173.5, 175.5], [177.5, 180.5]]
 AT = {
-    "w4_raw": 1, "tabs": 21.5, "w4s": 22, "tab": 29, "tab2s": 81, "end_edit": 148.5,
-    "v2s": 181, "end_plain": 182, "end_root": 183, "w4s_raw": 184, "scales0": 185,
+    "w4_raw": 7, "tabs": 216, "w4": 216, "tab": 28, "vs_rows": 10.5, "tab2s": 41, "end_edit": 151,
+    "v2s": 183.5, "end_plain": 184.5, "end_root": 223.5, "w4s_raw": 186.5, "scales0": 187.5, "second": 189.5,
 }
 
 
@@ -107,28 +110,24 @@ def tile_list_farm_job_board_kernel(
         w4s_raw = place([P, H], U8, "w4s_raw")
         tabs = place([P, T], U8, "tabs")
         w4_raw = place([P, 2 * H], U8, "w4_raw")
-        tab = place([P, T], U32, "tab")
-        nc.vector.memset(one[:], 1.0)
+        vs = keep.tile([P, S], U8, name="vs", align_bytes=64)
+        nc.gpsimd.memset(tabs[:, 0 : T // 2].bitcast(I32), 0)
+        nc.vector.memset(tabs[:, T // 2 : T].bitcast(I32), 0)
         nc.vector.memset(w4s_raw[:].bitcast(I32), 0)
-        nc.vector.memset(tabs[:].bitcast(I32), 0)
+        nc.vector.memset(one[:], 1.0)
+        tab = place([P, T], U32, "tab")
         nc.scalar.activation(out=warm[:, 0:1], in_=one[:], func=ACT.Abs_reciprocal_sqrt)
 
         nc.sync.dma_start(list1[:], offs)
         nc.sync.dma_start(out=w4_raw[:].bitcast(I32), in_=w4_words[0].bitcast(I32))
         nc.sync.dma_start(list3[:], offs3)
+        nc.sync.dma_start(list2[:], offs2)
+        nc.sync.dma_start(list4[:], offs4)
+        nc.sync.dma_start(out=tabs[0:16, :].bitcast(I32), in_=tab_scales[0].bitcast(I32))
+        nc.sync.dma_start(out=w4s_raw[0:16, :].bitcast(I32), in_=w4_scales[0].bitcast(I32))
         nc.sync.dma_start(
             out=tab[:].bitcast(I32),
             in_=tab_words[0].rearrange("p n i -> p (n i)").bitcast(I32),
-        )
-        nc.sync.dma_start(list2[:], offs2)
-        nc.sync.dma_start(list4[:], offs4)
-        load_scale_rows(nc.gpsimd, w4s_raw, lambda rows: w4_scales[0, rows, :], 4)
-        load_scale_rows(nc.scalar, tabs, lambda rows: tab_scales[0, rows, :], 4)
-
-        w4 = keep.tile([P, 2 * H], U8, name="w4", align_bytes=64)
-        nc.vector.tensor_copy(
-            out=w4[:].bitcast(U16).rearrange("p (b t m) -> p b m t", b=PASSES, t=PACK),
-            in_=w4_raw[:].bitcast(U16).rearrange("p (b m t) -> p b m t", b=PASSES, t=PACK),
         )
 
         w1_raw = []
@@ -162,30 +161,44 @@ def tile_list_farm_job_board_kernel(
                     wg[(t, half)] = rows[:, h.start - cols.start : h.stop - cols.start]
 
         whole_list = slice(0, S)
-        load_w1(0)
-        load_weights(0, halves[0], WG0_AT[0])
+        vs_rows = place([P, S], U8, "vs_rows")
+        nc.vector.tensor_copy(vs_rows[:], tabs[:].indirect(list1[:]))
 
-        vs = keep.tile([P, S], U8, name="vs", align_bytes=64)
-        nc.vector.tensor_copy(vs[:], tabs[:].indirect(list1[:]))
-        load_page(0)
-        load_weights(0, halves[1], WG0_AT[1])
-        load_weights(1, whole_list, WG_AT[1])
-        w4s = place([P, H], U8, "w4s")
+        def spread_scale_rows(scales):
+            for q in QUADRANTS[1:]:
+                nc.sync.dma_start(
+                    out=scales[32 * q : 32 * q + 4, :].bitcast(I32), in_=scales[4 * q : 4 * q + 4, :].bitcast(I32)
+                )
+
+        w4s = keep.tile([P, H], U8, name="w4s", align_bytes=64)
         nc.vector.tensor_copy(
             out=w4s[:].rearrange("p (b t m) -> p b m t", b=PASSES, t=PACK),
             in_=w4s_raw[:].rearrange("p (b m t) -> p b m t", b=PASSES, t=PACK),
         )
+        spread_scale_rows(w4s)
+        nc.vector.tensor_copy(out=vs[:].bitcast(I32), in_=vs_rows[:].bitcast(I32))
+        spread_scale_rows(vs)
+        load_w1(0)
+        load_weights(0, halves[0], WG0_AT[0])
+        w4 = place([P, 2 * H], U8, "w4")
+        nc.vector.tensor_copy(
+            out=w4[:].bitcast(U16).rearrange("p (b t m) -> p b m t", b=PASSES, t=PACK),
+            in_=w4_raw[:].bitcast(U16).rearrange("p (b m t) -> p b m t", b=PASSES, t=PACK),
+        )
+        load_page(0)
         v = []
         for half in range(HALVES):
             words = keep.tile([P, BANK], U32, name="v%d" % half, align_bytes=64)
             nc.vector.tensor_copy(words[:], tab[:].indirect(entries(list1, halves[half])))
             v.append(words)
+        load_weights(0, halves[1], WG0_AT[1])
+        load_weights(1, whole_list, WG_AT[1])
         load_page(1)
         load_weights(2, whole_list, WG_AT[2])
-        load_w1(1)
+        load_page(2)
 
-        w1_codes = keep.tile([P, H], U32, name="w1_codes", align_bytes=64)
-        w1_scales = keep.tile([P, H], U8, name="w1_scales", align_bytes=64)
+        w1_codes = []
+        w1_scales = []
         w1_rounded = []
 
         def round_w1(b, engine):
@@ -199,18 +212,22 @@ def tile_list_farm_job_board_kernel(
 
         def quantise_w1(first, last):
             b = first // PACK
-            cols = slice(P * first, P * (last + 1))
+            if first % PACK == 0:
+                w1_codes.append(place([P, PASS], U32, "w1_codes%d" % b, W1_CODES_AT[b]))
+                w1_scales.append(place([P, PASS], U8, "w1_scales%d" % b, W1_SCALES_AT[b]))
+            cols = slice(P * (first - PACK * b), P * (last + 1 - PACK * b))
             nc.vector.quantize_mx(
-                out=w1_codes[:, cols].bitcast(FP8X4), scales=w1_scales[:, cols],
+                out=w1_codes[b][:, cols].bitcast(FP8X4), scales=w1_scales[b][:, cols],
                 in_=w1_rounded[b][:, PASS * (first - PACK * b) : PASS * (last + 1 - PACK * b)],
             )
 
         def products(k, half):
             rows = slice(P * k, P * (k + 1))
+            b, t = divmod(k, PACK)
+            cols = slice(P * t, P * (t + 1))
             words = v[half][:].bitcast(FP8X4)
-            first_bank = PACK * (k % 2) + 2 * half
-            acc_b = bank(first_bank, "acc_b")
-            acc_a = bank(first_bank + 1, "acc_a")
+            acc_b = bank(B_BANKS[k][half], "acc_b")
+            acc_a = bank(A_BANKS[k][half], "acc_a")
             nc.tensor.matmul_mx(
                 out=acc_b[:],
                 lhsT=w4[:, 2 * rows.start : 2 * rows.stop].bitcast(FP4X4), lhsT_scale=w4s[:, rows],
@@ -218,7 +235,7 @@ def tile_list_farm_job_board_kernel(
             )
             nc.tensor.matmul_mx(
                 out=acc_a[:],
-                lhsT=w1_codes[:, rows].bitcast(FP8X4), lhsT_scale=w1_scales[:, rows],
+                lhsT=w1_codes[b][:, cols].bitcast(FP8X4), lhsT_scale=w1_scales[b][:, cols],
                 rhs=words, rhs_scale=vs[:, halves[half]], start=True, stop=True,
             )
             return acc_b, acc_a
@@ -235,9 +252,10 @@ def tile_list_farm_job_board_kernel(
         def times(engine, dst, x, y):
             engine.tensor_tensor(out=dst, in0=x, in1=y, op=MULT)
 
-        weighted = place([P, S], F32, "weighted", WEIGHTED_AT[0])
-        second = place([P, BANK], F32, "second", WEIGHTED_AT[1])
-        late = {}
+        row = place([P, S + S // 4], F32, "row", GAIN_AT[0])
+        weighted = row[:, S // 4 : S + S // 4]
+        second = place([P, BANK], F32, "second")
+        late = []
         edits = {}
         end = {}
 
@@ -245,20 +263,26 @@ def tile_list_farm_job_board_kernel(
             nc.vector.tensor_copy(pages[k][:].indirect(entries(list3, cols)), values)
 
         def first_plane():
-            gain = place([P, S], F32, "gain0", GAIN_AT[0])
+            gain = row[:, 0:S]
             edit = place([P, S], F32, "edit0", EDIT_AT[0])
             h0, h1 = halves
             accs = [products(0, half) for half in range(HALVES)]
-            for half, h in enumerate(halves):
-                size(gain[:, h], accs[half][0][:])
-                invert(gain[:, h])
-                square(gain[:, h])
+            quarters = [slice(0, BANK // 2), slice(BANK // 2, BANK)]
+            for q in quarters:
+                size(gain[:, q], accs[0][0][:, q])
+            for q in quarters:
+                invert(gain[:, q])
+            for q in quarters:
+                square(gain[:, q])
+            size(gain[:, h1], accs[1][0][:])
+            invert(gain[:, h1])
+            square(gain[:, h1])
             times(nc.vector, gain[:, h0], gain[:, h0], wg[(0, 0)])
             quantise_w1(1, 1)
             quantise_w1(2, 3)
             times(nc.vector, edit[:, h0], accs[0][1][:], gain[:, h0])
-            times(nc.gpsimd, weighted[:, h1], gain[:, h1], wg[(0, 1)])
-            late[0] = (accs[1][1], weighted[:, h1])
+            times(nc.gpsimd, second[:], gain[:, h1], wg[(0, 1)])
+            late.append(accs[1][1])
             edits[0] = edit
 
         def first_stage(k):
@@ -280,24 +304,18 @@ def tile_list_farm_job_board_kernel(
                 nc.scalar.activation(
                     out=end["root"][:], in_=gain[:, END:S], func=ACT.Abs_reciprocal_sqrt, bias=one[:]
                 )
-            if k >= SPLIT_SCATTERS:
-                nc.scalar.copy(out=edit[:, main], in_=accs[1][1][:, 0:width])
+            nc.scalar.copy(out=edit[:, main], in_=accs[1][1][:, 0:width])
             if k == LAST:
                 end["plain"] = place([P, S - END], F32, "end_plain")
                 nc.scalar.copy(out=end["plain"][:], in_=accs[1][1][:, width:BANK])
             square(gain[:, main])
-            if k < SPLIT_SCATTERS:
-                times(nc.gpsimd, weighted[:, h0], gain[:, h0], wg[(t, 0)])
-                times(nc.gpsimd, edit[:, h0], edit[:, h0], weighted[:, h0])
-                times(nc.gpsimd, second[:], gain[:, h1], wg[(t, 1)])
-                late[k] = (accs[1][1], second[:])
-            else:
-                for half, h in enumerate((h0, main)):
-                    times(nc.gpsimd, weighted[:, h], gain[:, h], wg[(t, half)][:, 0 : h.stop - h.start])
-                for h in (h0, main):
-                    times(nc.gpsimd, edit[:, h], edit[:, h], weighted[:, h])
-                if k == LAST:
-                    times(nc.gpsimd, end["plain"][:], end["plain"][:], wg[(t, 1)][:, width:BANK])
+            parts = [(h, wg[(t, half)][:, 0 : h.stop - h.start]) for half, h in enumerate((h0, main))]
+            for h, w in parts:
+                times(nc.gpsimd, weighted[:, h], gain[:, h], edit[:, h] if k < PACK else w)
+            for h, w in parts:
+                times(nc.gpsimd, edit[:, h], weighted[:, h], w if k < PACK else edit[:, h])
+            if k == LAST:
+                times(nc.gpsimd, end["plain"][:], end["plain"][:], wg[(t, 1)][:, width:BANK])
             edits[k] = edit
 
         side0 = []
@@ -307,7 +325,8 @@ def tile_list_farm_job_board_kernel(
             if k < SPLIT_SCATTERS:
                 h0, h1 = halves
                 put(k, edits[k][:, h0], h0)
-                times(nc.vector, edits[k][:, h1], late[k][0][:], late[k][1])
+                if k == 0:
+                    times(nc.vector, edits[k][:, h1], late[0][:], second[:])
                 put(k, edits[k][:, h1], h1)
             else:
                 put(k, edits[k][:], whole_list)
@@ -343,32 +362,31 @@ def tile_list_farm_job_board_kernel(
 
         round_w1(0, "vector")
         quantise_w1(0, 0)
-        load_page(2)
+        load_w1(1)
         load_weights(3, whole_list, WG_AT[3])
         first_plane()
+        tab2s = place([P, T3], U8, "tab2s")
+        nc.vector.memset(tab2s[:].bitcast(I32), 0)
+        load_scale_rows(nc.sync, tab2s, lambda rows: tab2_scales[:, rows, :], 4 * PASSES)
         load_page(3)
         load_page(4)
         first_stage(1)
         scatter(0)
         load_page(5)
         first_stage(2)
-        round_w1(1, "scalar")
         scatter(1)
+        first_stage(3)
+        round_w1(1, "scalar")
+        scatter(2)
         quantise_w1(PACK, LAST)
         load_page(6)
         load_page(7)
-        tab2s = place([P, T3], U8, "tab2s")
-        nc.vector.memset(tab2s[:].bitcast(I32), 0)
-        load_scale_rows(nc.sync, tab2s, lambda rows: tab2_scales[:, rows, :], 4 * PASSES)
         load_workers(0)
-        for k in range(3, PLANES):
+        load_workers(1)
+        for k in range(PACK, PLANES):
             first_stage(k)
             scatter(k - 1)
-            if k == 3:
-                load_workers(1)
-        nc.scalar.activation(out=warm[:, 1:2], in_=end["root"][:, 0:1], func=ACT.Sigmoid)
         load_permit(0)
-        load_permit(1)
 
         scales0 = place([P, T2], U8, "scales0")
         codes0 = []
@@ -381,6 +399,7 @@ def tile_list_farm_job_board_kernel(
                 side0[w][:].rearrange("p t (c i) -> p c t i", i=LINE),
             )
             woven0.append(woven)
+        nc.scalar.activation(out=warm[:, 1:2], in_=woven0[1][:, 0:1], func=ACT.Sigmoid)
         put(LAST, edits[LAST][:], slice(0, END))
         for w in range(2):
             codes = place([P, WIDE], U32, "codes0_%d" % w, CODES0_AT[w])
@@ -414,11 +433,13 @@ def tile_list_farm_job_board_kernel(
             else:
                 round_on("scalar", dst, src)
             woven1.append(woven)
-        end_gain = place([P, S - END], F32, "end_edit")
-        nc.scalar.activation(out=end_gain[:], in_=end["root"][:], func=ACT.Square)
+            if c == 1:
+                end_gain = place([P, S - END], F32, "end_edit")
+                nc.scalar.activation(out=end_gain[:], in_=end["root"][:], func=ACT.Square)
         times(
             nc.vector, pages[LAST][:].indirect(entries(list3, slice(END, S))), end["plain"][:], end_gain[:]
         )
+        load_permit(1)
 
         scores = {}
         codes1 = []

from contextlib import ExitStack

import concourse.mybir as mybir

K, T, S, H, T2, T3, S2, PICK = 512, 4096, 1024, 1024, 2048, 2048, 512, 1024
FLOPS = 2 * (2 * K * H * S + H * S2 * T2)

F32 = mybir.dt.float32
BF16 = mybir.dt.bfloat16
I32 = mybir.dt.int32
U32 = mybir.dt.uint32
U8 = mybir.dt.uint8
U16 = mybir.dt.uint16
FP8X4 = mybir.dt.float8_e4m3fn_x4
FP4X4 = mybir.dt.float4_e2m1fn_x4
ACT = mybir.ActivationFunctionType
MULT = mybir.AluOpType.mult
ADD = mybir.AluOpType.add

P = 128
BANK = 512
PACK = 4
PASS = P * PACK
PASSES = H // PASS
PLANES = PACK * PASSES
HALVES = S // BANK
CHUNKS = T2 // BANK
ROW_TILES = S2 // P
LAST = PLANES - 1
WIDE = T2 // 2
LINE = 4
QUADRANTS = (0, 2, 1, 3)
END = 768
SPLIT_SCATTERS = 2

PAGE_AT = [0, 23, 43, 51.5, 59.5, 67.5, 15, 75.5]
WG_AT = [None, 33, 37, 11]
WG0_AT = [9, 31]
W1_RAW_AT = [11, 15]
W1_ROUNDED_AT = [57.5, 81.5]
GAIN_AT = [202.5, 67.5, 81.5, 157.5, 161.5, 207.5, 117.5, 125.5]
EDIT_AT = [71.5, 165.5, 169.5, 173.5, 177.5, 211.5, 195.5, 181.5]
W1_CODES_AT = [199.5, 169.5]
W1_SCALES_AT = [201.5, 171.5]
B_BANKS = [(0, 2), (4, 6), (0, 2), (4, 6), (0, 2), (1, 3), (5, 7), (0, 2)]
A_BANKS = [(1, 3), (5, 7), (1, 3), (5, 7), (1, 3), (5, 7), (0, 2), (4, 6)]
SIDE0_AT = [85.5, 101.5]
WOVEN0_AT = [117.5, 125.5]
CODES0_AT = [0, 4]
SIDE1_AT = [145.5, 151.5, 133.5, 139.5]
WOVEN1_AT = [85.5, 89.5, 220, 224]
CODES1_AT = [101.5, 103.5, 105.5, 107.5]
SCALES1_AT = [109.5, 110, 110.5, 111]
TAB2_AT = [23, 43]
WORKERS_AT = [[181.5, 182.5], [224, 225]]
PERMIT_AT = [15, 133.5]
SCORES_AT = [117.5, 125.5, 51.5, 59.5]
PICKED_AT = [[165.5], [169.5], [173.5, 175.5], [177.5, 180.5]]
AT = {
    "w4_raw": 7, "tabs": 216, "w4": 216, "tab": 28, "vs_rows": 10.5, "tab2s": 41, "end_edit": 151,
    "v2s": 183.5, "end_plain": 184.5, "end_root": 223.5, "w4s_raw": 186.5, "scales0": 187.5, "second": 189.5,
}


def tile_list_farm_job_board_kernel(
    tc, tab_words, tab_scales, tab2_words, tab2_scales, offs, offs2, offs3, offs4,
    w1, w4_words, w4_scales, page0, wgs, permit, out,
):
    nc = tc.nc
    with ExitStack() as ctx:
        keep = ctx.enter_context(tc.tile_pool(name="keep", bufs=1))
        placed = ctx.enter_context(tc.tile_pool(name="placed", bufs=1))
        psum = ctx.enter_context(tc.psum_pool(name="psum", bufs=1))

        def bank(i, name):
            return psum.tile([P, BANK], F32, name=name, tag="bank%d" % i)

        def place(shape, dtype, name, kib=None):
            start = AT[name] if kib is None else kib
            return placed.tile(shape, dtype, name=name, tag=name, align_bytes=64, offset=int(1024 * start))

        def entries(offsets, cols):
            return offsets[:, cols.start // 16 : cols.stop // 16]

        def load_scale_rows(queue, scales, quadrant_rows, count):
            for q in QUADRANTS:
                queue.dma_start(
                    out=scales[32 * q : 32 * q + count, :].bitcast(I32),
                    in_=quadrant_rows(slice(4 * q, 4 * q + 4)).bitcast(I32),
                )

        def round_on(engine, dst, src):
            if engine == "vector":
                nc.vector.tensor_copy(out=dst, in_=src)
            elif engine == "scalar":
                nc.scalar.copy(out=dst, in_=src)
            else:
                nc.gpsimd.tensor_scalar(out=dst, in0=src, scalar1=1.0, scalar2=0.0, op0=MULT, op1=ADD)

        halves = [slice(BANK * half, BANK * (half + 1)) for half in range(HALVES)]
        chunks = [slice(BANK * c, BANK * (c + 1)) for c in range(CHUNKS)]

        list1 = keep.tile([P, S // 16], U16, name="list1")
        list2 = keep.tile([P, S2 // 16], U16, name="list2")
        list3 = keep.tile([P, S // 16], U16, name="list3")
        list4 = keep.tile([P, PICK // 16], U16, name="list4")
        one = keep.tile([P, 1], F32, name="one")
        warm = keep.tile([P, 2], F32, name="warm")

        w4s_raw = place([P, H], U8, "w4s_raw")
        tabs = place([P, T], U8, "tabs")
        w4_raw = place([P, 2 * H], U8, "w4_raw")
        vs = keep.tile([P, S], U8, name="vs", align_bytes=64)
        nc.gpsimd.memset(tabs[:, 0 : T // 2].bitcast(I32), 0)
        nc.vector.memset(tabs[:, T // 2 : T].bitcast(I32), 0)
        nc.vector.memset(w4s_raw[:].bitcast(I32), 0)
        nc.vector.memset(one[:], 1.0)
        tab = place([P, T], U32, "tab")
        nc.scalar.activation(out=warm[:, 0:1], in_=one[:], func=ACT.Abs_reciprocal_sqrt)

        nc.sync.dma_start(list1[:], offs)
        nc.sync.dma_start(out=w4_raw[:].bitcast(I32), in_=w4_words[0].bitcast(I32))
        nc.sync.dma_start(list3[:], offs3)
        nc.sync.dma_start(list2[:], offs2)
        nc.sync.dma_start(list4[:], offs4)
        nc.sync.dma_start(out=tabs[0:16, :].bitcast(I32), in_=tab_scales[0].bitcast(I32))
        nc.sync.dma_start(out=w4s_raw[0:16, :].bitcast(I32), in_=w4_scales[0].bitcast(I32))
        nc.sync.dma_start(
            out=tab[:].bitcast(I32),
            in_=tab_words[0].rearrange("p n i -> p (n i)").bitcast(I32),
        )

        w1_raw = []

        def load_w1(b):
            raw = place([P, PACK, PASS], F32, "w1_raw%d" % b, W1_RAW_AT[b])
            nc.sync.dma_start(
                out=raw[:],
                in_=w1[:, PASS * b : PASS * (b + 1)].rearrange("(p j) c -> p j c", j=PACK),
            )
            w1_raw.append(raw)

        pages = {}

        def load_page(k):
            b, t = divmod(k, PACK)
            page = place([P, T2], F32, "page%d" % k, PAGE_AT[k])
            rows = page0[PASS * b : PASS * (b + 1), :].rearrange("(p t) c -> t p c", t=PACK)
            nc.sync.dma_start(out=page[:], in_=rows[t])
            pages[k] = page

        wg_rows = wgs.rearrange("(q t) j -> t q j", t=PACK)
        wg = {}

        def load_weights(t, cols, kib):
            rows = place([P, cols.stop - cols.start], F32, "wg%d_%d" % (t, cols.start), kib)
            for q in QUADRANTS:
                nc.sync.dma_start(out=rows[32 * q : 32 * (q + 1), :], in_=wg_rows[t][:, cols])
            for half, h in enumerate(halves):
                if cols.start <= h.start and h.stop <= cols.stop:
                    wg[(t, half)] = rows[:, h.start - cols.start : h.stop - cols.start]

        whole_list = slice(0, S)
        vs_rows = place([P, S], U8, "vs_rows")
        nc.vector.tensor_copy(vs_rows[:], tabs[:].indirect(list1[:]))

        def spread_scale_rows(scales):
            for q in QUADRANTS[1:]:
                nc.sync.dma_start(
                    out=scales[32 * q : 32 * q + 4, :].bitcast(I32), in_=scales[4 * q : 4 * q + 4, :].bitcast(I32)
                )

        w4s = keep.tile([P, H], U8, name="w4s", align_bytes=64)
        nc.vector.tensor_copy(
            out=w4s[:].rearrange("p (b t m) -> p b m t", b=PASSES, t=PACK),
            in_=w4s_raw[:].rearrange("p (b m t) -> p b m t", b=PASSES, t=PACK),
        )
        spread_scale_rows(w4s)
        nc.vector.tensor_copy(out=vs[:].bitcast(I32), in_=vs_rows[:].bitcast(I32))
        spread_scale_rows(vs)
        load_w1(0)
        load_weights(0, halves[0], WG0_AT[0])
        w4 = place([P, 2 * H], U8, "w4")
        nc.vector.tensor_copy(
            out=w4[:].bitcast(U16).rearrange("p (b t m) -> p b m t", b=PASSES, t=PACK),
            in_=w4_raw[:].bitcast(U16).rearrange("p (b m t) -> p b m t", b=PASSES, t=PACK),
        )
        load_page(0)
        v = []
        for half in range(HALVES):
            words = keep.tile([P, BANK], U32, name="v%d" % half, align_bytes=64)
            nc.vector.tensor_copy(words[:], tab[:].indirect(entries(list1, halves[half])))
            v.append(words)
        load_weights(0, halves[1], WG0_AT[1])
        load_weights(1, whole_list, WG_AT[1])
        load_page(1)
        load_weights(2, whole_list, WG_AT[2])
        load_page(2)

        w1_codes = []
        w1_scales = []
        w1_rounded = []

        def round_w1(b, engine):
            rounded = place([P, PACK * PASS], BF16, "w1_rounded%d" % b, W1_ROUNDED_AT[b])
            round_on(
                engine,
                rounded[:].rearrange("p (t m j) -> p m j t", t=PACK, j=PACK),
                w1_raw[b][:].rearrange("p j (m t) -> p m j t", t=PACK),
            )
            w1_rounded.append(rounded)

        def quantise_w1(first, last):
            b = first // PACK
            if first % PACK == 0:
                w1_codes.append(place([P, PASS], U32, "w1_codes%d" % b, W1_CODES_AT[b]))
                w1_scales.append(place([P, PASS], U8, "w1_scales%d" % b, W1_SCALES_AT[b]))
            cols = slice(P * (first - PACK * b), P * (last + 1 - PACK * b))
            nc.vector.quantize_mx(
                out=w1_codes[b][:, cols].bitcast(FP8X4), scales=w1_scales[b][:, cols],
                in_=w1_rounded[b][:, PASS * (first - PACK * b) : PASS * (last + 1 - PACK * b)],
            )

        def products(k, half):
            rows = slice(P * k, P * (k + 1))
            b, t = divmod(k, PACK)
            cols = slice(P * t, P * (t + 1))
            words = v[half][:].bitcast(FP8X4)
            acc_b = bank(B_BANKS[k][half], "acc_b")
            acc_a = bank(A_BANKS[k][half], "acc_a")
            nc.tensor.matmul_mx(
                out=acc_b[:],
                lhsT=w4[:, 2 * rows.start : 2 * rows.stop].bitcast(FP4X4), lhsT_scale=w4s[:, rows],
                rhs=words, rhs_scale=vs[:, halves[half]], start=True, stop=True,
            )
            nc.tensor.matmul_mx(
                out=acc_a[:],
                lhsT=w1_codes[b][:, cols].bitcast(FP8X4), lhsT_scale=w1_scales[b][:, cols],
                rhs=words, rhs_scale=vs[:, halves[half]], start=True, stop=True,
            )
            return acc_b, acc_a

        def size(gain, acc_b):
            nc.scalar.activation(out=gain, in_=acc_b, func=ACT.Abs)

        def invert(gain):
            nc.scalar.activation(out=gain, in_=gain, func=ACT.Abs_reciprocal_sqrt, bias=one[:])

        def square(gain):
            nc.scalar.activation(out=gain, in_=gain, func=ACT.Square)

        def times(engine, dst, x, y):
            engine.tensor_tensor(out=dst, in0=x, in1=y, op=MULT)

        row = place([P, S + S // 4], F32, "row", GAIN_AT[0])
        weighted = row[:, S // 4 : S + S // 4]
        second = place([P, BANK], F32, "second")
        late = []
        edits = {}
        end = {}

        def put(k, values, cols):
            nc.vector.tensor_copy(pages[k][:].indirect(entries(list3, cols)), values)

        def first_plane():
            gain = row[:, 0:S]
            edit = place([P, S], F32, "edit0", EDIT_AT[0])
            h0, h1 = halves
            accs = [products(0, half) for half in range(HALVES)]
            quarters = [slice(0, BANK // 2), slice(BANK // 2, BANK)]
            for q in quarters:
                size(gain[:, q], accs[0][0][:, q])
            for q in quarters:
                invert(gain[:, q])
            for q in quarters:
                square(gain[:, q])
            size(gain[:, h1], accs[1][0][:])
            invert(gain[:, h1])
            square(gain[:, h1])
            times(nc.vector, gain[:, h0], gain[:, h0], wg[(0, 0)])
            quantise_w1(1, 1)
            quantise_w1(2, 3)
            times(nc.vector, edit[:, h0], accs[0][1][:], gain[:, h0])
            times(nc.gpsimd, second[:], gain[:, h1], wg[(0, 1)])
            late.append(accs[1][1])
            edits[0] = edit

        def first_stage(k):
            t = k % PACK
            h0, h1 = halves
            accs = [products(k, half) for half in range(HALVES)]
            gain = place([P, S], F32, "gain%d" % k, GAIN_AT[k])
            edit = place([P, S if k < LAST else END], F32, "edit%d" % k, EDIT_AT[k])
            size(gain[:, h0], accs[0][0][:])
            size(gain[:, h1], accs[1][0][:])
            invert(gain[:, h0])
            nc.scalar.copy(out=edit[:, h0], in_=accs[0][1][:])
            square(gain[:, h0])
            main = h1 if k < LAST else slice(BANK, END)
            width = main.stop - main.start
            invert(gain[:, main])
            if k == LAST:
                end["root"] = place([P, S - END], F32, "end_root")
                nc.scalar.activation(
                    out=end["root"][:], in_=gain[:, END:S], func=ACT.Abs_reciprocal_sqrt, bias=one[:]
                )
            nc.scalar.copy(out=edit[:, main], in_=accs[1][1][:, 0:width])
            if k == LAST:
                end["plain"] = place([P, S - END], F32, "end_plain")
                nc.scalar.copy(out=end["plain"][:], in_=accs[1][1][:, width:BANK])
            square(gain[:, main])
            parts = [(h, wg[(t, half)][:, 0 : h.stop - h.start]) for half, h in enumerate((h0, main))]
            for h, w in parts:
                times(nc.gpsimd, weighted[:, h], gain[:, h], edit[:, h] if k < PACK else w)
            for h, w in parts:
                times(nc.gpsimd, edit[:, h], weighted[:, h], w if k < PACK else edit[:, h])
            if k == LAST:
                times(nc.gpsimd, end["plain"][:], end["plain"][:], wg[(t, 1)][:, width:BANK])
            edits[k] = edit

        side0 = []
        side1 = []

        def scatter(k):
            if k < SPLIT_SCATTERS:
                h0, h1 = halves
                put(k, edits[k][:, h0], h0)
                if k == 0:
                    times(nc.vector, edits[k][:, h1], late[0][:], second[:])
                put(k, edits[k][:, h1], h1)
            else:
                put(k, edits[k][:], whole_list)
            if k < PACK:
                for w in range(2):
                    if k == 0:
                        side0.append(place([P, PACK, WIDE], F32, "side0_%d" % w, SIDE0_AT[w]))
                    nc.sync.dma_start(out=side0[w][:, k, :], in_=pages[k][:, WIDE * w : WIDE * (w + 1)])
            else:
                for c in range(CHUNKS):
                    if k == PACK:
                        side1.append(place([P, PACK - 1, BANK], F32, "side1_%d" % c, SIDE1_AT[c]))
                    nc.sync.dma_start(out=side1[c][:, k - PACK, :], in_=pages[k][:, chunks[c]])

        tab2 = []

        def load_workers(b):
            table = place([P, T3], U32, "tab2_%d" % b, TAB2_AT[b])
            nc.sync.dma_start(
                out=table[:].bitcast(I32),
                in_=tab2_words[b].rearrange("p n i -> p (n i)").bitcast(I32),
            )
            tab2.append(table)

        allowed = []

        def load_permit(i):
            rows = place([P, 2, PICK], F32, "allowed%d" % i, PERMIT_AT[i])
            nc.sync.dma_start(
                out=rows[:], in_=permit[2 * P * i : 2 * P * (i + 1), :].rearrange("(n p) m -> p n m", p=P)
            )
            allowed.append(rows)

        round_w1(0, "vector")
        quantise_w1(0, 0)
        load_w1(1)
        load_weights(3, whole_list, WG_AT[3])
        first_plane()
        tab2s = place([P, T3], U8, "tab2s")
        nc.vector.memset(tab2s[:].bitcast(I32), 0)
        load_scale_rows(nc.sync, tab2s, lambda rows: tab2_scales[:, rows, :], 4 * PASSES)
        load_page(3)
        load_page(4)
        first_stage(1)
        scatter(0)
        load_page(5)
        first_stage(2)
        scatter(1)
        first_stage(3)
        round_w1(1, "scalar")
        scatter(2)
        quantise_w1(PACK, LAST)
        load_page(6)
        load_page(7)
        load_workers(0)
        load_workers(1)
        for k in range(PACK, PLANES):
            first_stage(k)
            scatter(k - 1)
        load_permit(0)

        scales0 = place([P, T2], U8, "scales0")
        codes0 = []
        woven0 = []
        for w, engine in enumerate(["scalar", "scalar"]):
            woven = place([P, PACK * WIDE], BF16, "woven0_%d" % w, WOVEN0_AT[w])
            round_on(
                engine,
                woven[:].rearrange("p (c i t) -> p c t i", i=LINE, t=PACK),
                side0[w][:].rearrange("p t (c i) -> p c t i", i=LINE),
            )
            woven0.append(woven)
        nc.scalar.activation(out=warm[:, 1:2], in_=woven0[1][:, 0:1], func=ACT.Sigmoid)
        put(LAST, edits[LAST][:], slice(0, END))
        for w in range(2):
            codes = place([P, WIDE], U32, "codes0_%d" % w, CODES0_AT[w])
            nc.vector.quantize_mx(
                out=codes[:].bitcast(FP8X4), scales=scales0[:, WIDE * w : WIDE * (w + 1)], in_=woven0[w][:]
            )
            codes0.append(codes)

        v2s = place([P, S2], U8, "v2s")
        nc.vector.tensor_copy(v2s[:], tab2s[:].indirect(list2[:]))
        v2 = {}

        def gather_workers(pair):
            cols = slice(2 * P * pair, 2 * P * (pair + 1))
            for b in range(PASSES):
                words = place([P, 2 * P], U32, "v2_%d_%d" % (pair, b), WORKERS_AT[pair][b])
                nc.vector.tensor_copy(words[:], tab2[b][:].indirect(entries(list2, cols)))
                v2[(pair, b)] = words

        gather_workers(0)

        woven1 = []
        for c in range(CHUNKS):
            woven = place([P, PACK * BANK], BF16, "woven1_%d" % c, WOVEN1_AT[c])
            dst = woven[:].rearrange("p (c i t) -> p c t i", i=LINE, t=PACK)[:, :, 0 : PACK - 1, :]
            src = side1[c][:].rearrange("p t (c i) -> p c t i", i=LINE)
            if c == 0:
                middle = BANK // LINE // 2
                round_on("gpsimd", dst[:, 0:middle], src[:, 0:middle])
                round_on("scalar", dst[:, middle : 2 * middle], src[:, middle : 2 * middle])
            else:
                round_on("scalar", dst, src)
            woven1.append(woven)
            if c == 1:
                end_gain = place([P, S - END], F32, "end_edit")
                nc.scalar.activation(out=end_gain[:], in_=end["root"][:], func=ACT.Square)
        times(
            nc.vector, pages[LAST][:].indirect(entries(list3, slice(END, S))), end["plain"][:], end_gain[:]
        )
        load_permit(1)

        scores = {}
        codes1 = []

        def score_pass(n, c, b):
            if b == 0:
                scores[(n, c)] = bank(CHUNKS * (n % 2) + c, "score")
                rhs, rhs_scale = codes0[c // 2][:, halves[c % 2]], scales0[:, chunks[c]]
            else:
                rhs, rhs_scale = codes1[c][0][:], codes1[c][1][:]
            pair, within = divmod(n, 2)
            nc.tensor.matmul_mx(
                out=scores[(n, c)][:],
                lhsT=v2[(pair, b)][:, P * within : P * (within + 1)].bitcast(FP8X4),
                lhsT_scale=v2s[4 * b : P, P * n : P * (n + 1)],
                rhs=rhs.bitcast(FP8X4), rhs_scale=rhs_scale,
                start=(b == 0), stop=(b == PASSES - 1),
            )

        for n in range(2):
            for c in range(CHUNKS):
                score_pass(n, c, 0)
        for c, engine in enumerate(["vector", "vector", "scalar", "scalar"]):
            round_on(
                engine,
                woven1[c][:].rearrange("p (c t) -> p c t", t=PACK)[:, :, PACK - 1],
                pages[LAST][:, chunks[c]],
            )
        for c in range(CHUNKS):
            codes = place([P, BANK], U32, "codes1_%d" % c, CODES1_AT[c])
            scales = place([P, BANK], U8, "scales1_%d" % c, SCALES1_AT[c])
            nc.vector.quantize_mx(out=codes[:].bitcast(FP8X4), scales=scales[:], in_=woven1[c][:])
            codes1.append((codes, scales))
            score_pass(0, c, 1)
        for c in range(CHUNKS):
            score_pass(1, c, 1)
        gather_workers(1)

        vector_banks = [(2, 3), (3, 3)]
        whole = slice(0, PICK)
        pick_parts = [[whole], [whole], halves, [slice(0, END), slice(END, PICK)]]
        picked = {}

        def fetch_scores(n):
            e = place([P, T2], F32, "e%d" % n, SCORES_AT[n])
            for c in range(CHUNKS):
                engine = "vector" if (n, c) in vector_banks else "scalar"
                round_on(engine, e[:, chunks[c]], scores[(n, c)][:])
            if n + 2 < ROW_TILES:
                for c in range(CHUNKS):
                    for b in range(PASSES):
                        score_pass(n + 2, c, b)
            return e

        def pick(n, i, e):
            cols = pick_parts[n][i]
            x = place([P, cols.stop - cols.start], F32, "x%d_%d" % (n, i), PICKED_AT[n][i])
            nc.vector.tensor_copy(x[:], e[:].indirect(entries(list4, cols)))
            picked[(n, i)] = x

        def squash(n, i):
            x = picked[(n, i)]
            nc.scalar.activation(out=x[:], in_=x[:], func=ACT.Sigmoid)

        def weigh_and_store(n, i, engine):
            cols = pick_parts[n][i]
            y = picked[(n, i)]
            times(engine, y[:], y[:], allowed[n // 2][:, n % 2, cols])
            nc.sync.dma_start(out=out[P * n : P * (n + 1), cols], in_=y[:])

        pick(0, 0, fetch_scores(0))
        pick(1, 0, fetch_scores(1))
        squash(0, 0)
        weigh_and_store(0, 0, nc.gpsimd)
        e = fetch_scores(2)
        pick(2, 0, e)
        pick(2, 1, e)
        squash(1, 0)
        weigh_and_store(1, 0, nc.gpsimd)
        e = fetch_scores(3)
        pick(3, 0, e)
        pick(3, 1, e)
        squash(2, 0)
        weigh_and_store(2, 0, nc.gpsimd)
        squash(2, 1)
        weigh_and_store(2, 1, nc.vector)
        for i in range(2):
            squash(3, i)
            weigh_and_store(3, i, nc.vector)
